import numpy as np
import ml_dtypes


def mxq(x, axis, fmt="e4m3"):
    dtype, down = {"e4m3": (ml_dtypes.float8_e4m3fn, 7), "e5m2": (ml_dtypes.float8_e5m2, 14)}[fmt]
    v = np.moveaxis(np.asarray(x, np.float32).astype(ml_dtypes.bfloat16).astype(np.float64), axis, -1)
    blocks = v.reshape(v.shape[:-1] + (-1, 32))
    amax = np.abs(blocks).max(-1, keepdims=True)
    byte = np.maximum(np.where(amax > 0, np.frexp(amax)[1] - 1 + 127, 0) - down, 1)
    scale = np.exp2(byte - 127.0)
    codes = (blocks / scale).astype(np.float32).astype(dtype).astype(np.float64)
    return np.moveaxis((codes * scale).reshape(v.shape), -1, axis)


WIDE = False


def mx_kscale(k):
    if not WIDE:
        return np.ones(k)
    levels = np.array([10, -10, 5, -5, 0])
    if k % 512:
        return np.exp2(np.random.permutation(np.resize(levels, k // 32))).repeat(32)
    a = np.empty((k // 512, 16))
    for p in range(k // 512):
        a[p, :8] = np.random.permutation(np.resize(levels, 8))
        for g in range(8):
            far = levels[np.abs(levels - a[p, g]) >= 10]
            a[p, g + 8] = far[np.random.randint(len(far))]
    return np.exp2(a.ravel()).repeat(32)


def f64(x):
    return np.asarray(x).astype(np.float64)


def striped(idx):
    return np.tile(idx.reshape(-1, 16).T, (8, 1)).astype(np.uint16)


def unstriped(offs):
    return offs[:16].T.reshape(-1).astype(np.int64)


E2M1 = np.array([0.0, 0.5, 1.0, 1.5, 2.0, 3.0, 4.0, 6.0, -0.0, -0.5, -1.0, -1.5, -2.0, -3.0, -4.0, -6.0])


def pack_weight(w, fmt):
    k, n = w.shape
    w = f64(np.asarray(w, np.float32).astype(ml_dtypes.bfloat16)).reshape(k // 32, 32, n)
    amax = np.abs(w).max(1)
    if fmt == "e4m3":
        byte = np.frexp(amax)[1] - 1 + 127 - 7
    else:
        mant, ex = np.frexp(amax / 6.0)
        byte = np.where(mant > 0.5, ex, ex - 1) + 127
    byte = np.clip(np.where(amax > 0, byte, 1), 1, 254)
    scaled = (w * np.exp2(127.0 - byte)[:, None, :]).reshape(k, n).astype(np.float32)
    by_word = np.ascontiguousarray(scaled.reshape(k // 512, 128, 4, n).transpose(0, 1, 3, 2))
    if fmt == "e4m3":
        words = by_word.astype(ml_dtypes.float8_e4m3fn).view(np.uint8)
    else:
        c = by_word.astype(ml_dtypes.float4_e2m1fn).view(np.uint8) & 0xF
        words = (c[..., 0::2] | (c[..., 1::2] << 4)).reshape(k // 512, 128, 2 * n)
    return np.ascontiguousarray(words), np.ascontiguousarray(byte.astype(np.uint8).reshape(k // 512, 16, n))


def unpack_weight(words, scales, fmt):
    g, _, n = scales.shape
    words = np.ascontiguousarray(words).reshape(g, 128, n, -1)
    if fmt == "e4m3":
        vals = words.view(ml_dtypes.float8_e4m3fn).astype(np.float64)
    else:
        nib = np.empty((g, 128, n, 4), np.uint8)
        nib[..., 0::2] = words & 0xF
        nib[..., 1::2] = words >> 4
        vals = E2M1[nib]
    vals = vals * np.repeat(np.exp2(scales.astype(np.float64) - 127.0), 8, axis=1)[..., None]
    return vals.transpose(0, 1, 3, 2).reshape(g * 512, n)


def gelu(v):
    return 0.5 * v * (1.0 + np.tanh(np.sqrt(2.0 / np.pi) * (v + 0.044715 * v**3)))


K, H, N, T, S = 1024, 512, 256, 2048, 1024

def setup_inputs():
    n = np.random.standard_normal
    s = mx_kscale(K)[:, None]
    u = mx_kscale(H)[:, None]
    tab_words, tab_scales = pack_weight(n((K, T)) * s, "e4m3")
    wb_words, wb_scales = pack_weight(n((K, H)) / s / np.sqrt(K), "e2m1")
    wd_words, wd_scales = pack_weight(n((K, H)) / s / np.sqrt(K), "e2m1")
    return {
        "tab_words": tab_words, "tab_scales": tab_scales,
        "offs": striped(np.random.permutation(T)[:S]),
        "wa": (n((K, H)) / s * u.T / np.sqrt(K)).astype(np.float32),
        "wb_words": wb_words, "wb_scales": wb_scales,
        "wc": (n((K, H)) / s * u.T / np.sqrt(K)).astype(np.float32),
        "wd_words": wd_words, "wd_scales": wd_scales,
        "gT": (1.0 / (1.0 + np.exp(-n((H, T))))).astype(np.float32),
        "w2": (n((H, N)) / u / np.sqrt(H)).astype(np.float32),
        "b2": (0.3 * n(N)).astype(np.float32),
    }

def reference(tab_words, tab_scales, offs, wa, wb_words, wb_scales, wc, wd_words, wd_scales, gT, w2, b2):
    v = unpack_weight(tab_words, tab_scales, "e4m3")[:, unstriped(offs)]
    g = f64(gT)[:, unstriped(offs)]
    A = mxq(f64(wa), 0, "e4m3").T @ v
    B = unpack_weight(wb_words, wb_scales, "e2m1").T @ v
    C = mxq(f64(wc), 0, "e4m3").T @ v
    D = unpack_weight(wd_words, wd_scales, "e2m1").T @ v
    h = (A * B - C * D) * g
    y = mxq(f64(w2), 0, "e4m3").T @ mxq(h, 0, "e4m3")
    return y + f64(b2)[:, None]

@@ -1,0 +1,235 @@
+from contextlib import ExitStack
+
+import concourse.mybir as mybir
+from concourse.masks import make_identity
+
+K, H, N, T, S = 1024, 512, 256, 2048, 1024
+FLOPS = 2 * (4 * K * H * S + H * N * S)
+
+F32 = mybir.dt.float32
+BF16 = mybir.dt.bfloat16
+I32 = mybir.dt.int32
+U32 = mybir.dt.uint32
+U16 = mybir.dt.uint16
+U8 = mybir.dt.uint8
+FP8X4 = mybir.dt.float8_e4m3fn_x4
+FP4X4 = mybir.dt.float4_e2m1fn_x4
+MULT = mybir.AluOpType.mult
+ADD = mybir.AluOpType.add
+COPY = mybir.ActivationFunctionType.Copy
+IDENTITY = mybir.ActivationFunctionType.Identity
+
+P = 128
+PACK = 4
+PASSES = K // (P * PACK)
+TILES = S // P
+CHUNKS = [(0, 256), (256, 512), (512, 768), (768, 896), (896, 1024)]
+
+
+def tile_list_complex_triple_messages_kernel(
+    tc, tab_words, tab_scales, offs, wa, wb_words, wb_scales, wc, wd_words, wd_scales, gT, w2, b2, out
+):
+    nc = tc.nc
+    with ExitStack() as ctx:
+        keep = ctx.enter_context(tc.tile_pool(name="keep", bufs=1))
+        ring = ctx.enter_context(tc.tile_pool(name="ring", bufs=2))
+        psum = ctx.enter_context(tc.psum_pool(name="psum", bufs=1))
+
+        offsets = keep.tile([P, S // 16], U16, name="offsets")
+        nc.sync.dma_start(offsets[:], offs)
+
+        bias = keep.tile([P, N // P], F32, name="bias")
+        with nc.allow_non_contiguous_dma(reason="one bias value a partition"):
+            nc.sync.dma_start(bias[:], b2.rearrange("(c p) -> p c", p=P))
+        tab_w = [keep.tile([P, T], I32, name=f"tab_w{a}") for a in range(PASSES)]
+        tab_src = [tab_words[a].rearrange("p t i -> p (t i)").bitcast(I32) for a in range(PASSES)]
+        for c in range(0, T, 512):
+            nc.sync.dma_start(tab_w[0][:, c : c + 512], tab_src[0][:, c : c + 512])
+        fp4_w = []
+        for name, src in (("wb_w", wb_words), ("wd_w", wd_words)):
+            fw = keep.tile([P, PASSES, H // 2], I32, name=name, align_bytes=64)
+            nc.sync.dma_start(fw[:], src.rearrange("a p n -> p a n").bitcast(I32))
+            fp4_w.append(fw)
+        tab_sc = keep.tile([P, PASSES, T // 4], I32, name="tab_sc", align_bytes=64)
+        nc.gpsimd.memset(tab_sc[:], 0)
+        for q in range(4):
+            nc.sync.dma_start(
+                tab_sc[32 * q : 32 * q + 4, :, :],
+                tab_scales[:, 4 * q : 4 * q + 4, :].rearrange("a r t -> r a t").bitcast(I32),
+            )
+        nc.sync.dma_start(tab_w[1][:], tab_src[1])
+        fp4_sc = keep.tile([P, 2, PASSES, H // 4], I32, name="fp4_sc", align_bytes=64)
+
+        def load_fp4_scales(w, src):
+            for q in range(4):
+                nc.sync.dma_start(
+                    fp4_sc[32 * q : 32 * q + 4, w, :, :],
+                    src[:, 4 * q : 4 * q + 4, :].rearrange("a r c -> r a c").bitcast(I32),
+                )
+
+        raw = {}
+
+        def load_raw(name, src, a):
+            r = keep.tile([P, PACK, H], F32, name=f"raw_{name}{a}")
+            nc.sync.dma_start(r[:], src[a * 512 : (a + 1) * 512, :].rearrange("(p j) c -> p j c", j=PACK))
+            raw[name, a] = r
+
+        load_fp4_scales(0, wb_scales)
+        load_raw("wa", wa, 0)
+        load_fp4_scales(1, wd_scales)
+        load_raw("wa", wa, 1)
+        load_raw("wc", wc, 0)
+        load_raw("wc", wc, 1)
+        raw_w2 = keep.tile([P, PACK, N], F32, name="raw_w2")
+        nc.sync.dma_start(raw_w2[:], w2.rearrange("(p j) n -> p j n", j=PACK))
+        gates = []
+        for t in range(PACK):
+            g = keep.tile([P, T], F32, name=f"gate{t}")
+            nc.sync.dma_start(g[:], gT.rearrange("(p t) c -> t p c", t=PACK)[t])
+            gates.append(g)
+        ident = keep.tile([P, P], F32, name="ident")
+        make_identity(nc, ident[:])
+
+        v_w = keep.tile([P, PASSES, S], U32, name="v_w", align_bytes=64)
+        v_sc = keep.tile([P, PASSES, S], U8, name="v_sc", align_bytes=64)
+
+        def gather_scales(a, lo, hi):
+            nc.vector.tensor_copy(
+                v_sc[:, a, lo:hi], tab_sc[:, a, :].bitcast(U8).indirect(offsets[:, lo // 16 : hi // 16])
+            )
+
+        def gather_words(a, lo, hi):
+            nc.vector.tensor_copy(
+                v_w[:, a, lo:hi], tab_w[a][:].bitcast(U32).indirect(offsets[:, lo // 16 : hi // 16])
+            )
+
+        gather_words(0, 0, 512)
+        gather_scales(0, 0, 512)
+        gather_scales(1, 0, 512)
+        gather_words(1, 0, 256)
+        gather_words(1, 256, 512)
+        gather_words(0, 512, 1024)
+        gather_scales(0, 512, 1024)
+        gather_scales(1, 512, 1024)
+        gather_words(1, 512, 768)
+        gather_words(1, 768, 1024)
+
+        def product(j, moving):
+            acc = psum.tile([P, H], F32, name="acc", bufs=5)
+            cols = slice(j * P, (j + 1) * P)
+            for a in range(PASSES):
+                codes, scales = moving(a)
+                nc.tensor.matmul_mx(
+                    acc[:],
+                    lhsT=v_w[:, a, cols].bitcast(FP8X4),
+                    lhsT_scale=v_sc[:, a, cols],
+                    rhs=codes,
+                    rhs_scale=scales,
+                    start=(a == 0),
+                    stop=(a == PASSES - 1),
+                )
+            return acc[:].rearrange("p (m t) -> p t m", t=PACK)
+
+        def fp4_operand(w):
+            return lambda a: (fp4_w[w][:, a, :].bitcast(FP4X4), fp4_sc[:, w, a, :].bitcast(U8))
+
+        b_sb = keep.tile([P, TILES, PACK, P], F32, name="b_sb")
+        d_sb = keep.tile([P, TILES, PACK, P], F32, name="d_sb")
+        ab_sb = keep.tile([P, TILES, PACK, P], F32, name="ab_sb")
+
+        def view_b(j):
+            nc.scalar.copy(b_sb[:, j], product(j, fp4_operand(0)))
+
+        def view_d(j):
+            nc.scalar.activation(d_sb[:, j], product(j, fp4_operand(1)), COPY, scale=-1.0)
+
+        for j in range(TILES):
+            view_b(j)
+            if j < TILES // 2:
+                view_d(j)
+
+        def cast_vector(dst, src):
+            nc.vector.tensor_copy(dst, src)
+
+        def cast_gpsimd(dst, src):
+            nc.gpsimd.tensor_scalar(dst, src, 1.0, 0.0, MULT, ADD)
+
+        def cast_scalar(dst, src):
+            nc.scalar.copy(dst, src)
+
+        def quantise(name, src, width, casts):
+            grouped = keep.tile([P, width, PACK], BF16, name=f"grp_{name}", align_bytes=64)
+            codes = keep.tile([P, width], U32, name=f"codes_{name}", align_bytes=64)
+            scales = keep.tile([P, width], U8, name=f"scales_{name}", align_bytes=64)
+            step = width // len(casts)
+            for c, cast in zip(range(0, width, step), casts):
+                cast(grouped[:, c : c + step, :], src[:, :, c : c + step].rearrange("p j c -> p c j"))
+            nc.vector.quantize_mx(codes[:].bitcast(FP8X4), scales[:], grouped[:].rearrange("p c j -> p (c j)"))
+            return codes, scales
+
+        wa_q = [
+            quantise("wa0", raw["wa", 0], H, [cast_gpsimd] * 4),
+            quantise("wa1", raw["wa", 1], H, [cast_scalar, cast_scalar, cast_gpsimd, cast_gpsimd]),
+        ]
+        for j in range(TILES):
+            a_ps = product(j, lambda a: (wa_q[a][0][:].bitcast(FP8X4), wa_q[a][1][:]))
+            nc.vector.tensor_tensor(ab_sb[:, j], a_ps, b_sb[:, j], MULT)
+        wc_q = [quantise(f"wc{a}", raw["wc", a], H, [cast_gpsimd] * 4) for a in range(PASSES)]
+        for j in range(TILES // 2, TILES):
+            view_d(j)
+        w2_codes, w2_scales = quantise("w2", raw_w2, N, [cast_gpsimd] * 2)
+
+        def imaginary(j):
+            c_ps = product(j, lambda a: (wc_q[a][0][:].bitcast(FP8X4), wc_q[a][1][:]))
+            cd = ring.tile([P, PACK, P], F32, name="cd", bufs=4)
+            nc.vector.tensor_tensor(cd[:], c_ps, d_sb[:, j], MULT)
+            return cd
+
+        def turn(lo, hi, cds):
+            diff = ring.tile([P, PACK, hi - lo], F32, name="diff", bufs=4)
+            for j in range(lo // P, hi // P):
+                bank = psum.tile([P, PACK, P], F32, name="turned", bufs=2)
+                for t in range(PACK):
+                    nc.tensor.matmul(bank[:, t, :], ab_sb[:, j, t, :], ident[:], start=True, stop=False, is_transpose=True)
+                    nc.tensor.matmul(bank[:, t, :], cds[j][:, t, :], ident[:], start=False, stop=True, is_transpose=True)
+                nc.scalar.copy(diff[:, :, j * P - lo : (j + 1) * P - lo], bank[:])
+            return diff
+
+        def finish(lo, hi, diff, cast):
+            width = hi - lo
+            h = ring.tile([P, PACK, width], F32, name="h", bufs=4)
+            for t in range(PACK):
+                nc.vector.tensor_tensor(
+                    h[:, t, :], gates[t][:].indirect(offsets[:, lo // 16 : hi // 16]), diff[:, t, :], MULT
+                )
+            grouped = ring.tile([P, width, PACK], BF16, name="h_grp", align_bytes=64)
+            cast(grouped[:], h[:].rearrange("p t c -> p c t"))
+            codes = ring.tile([P, width], U32, name="h_codes", align_bytes=64)
+            scales = ring.tile([P, width], U8, name="h_scales", align_bytes=64)
+            nc.vector.quantize_mx(codes[:].bitcast(FP8X4), scales[:], grouped[:].rearrange("p c t -> p (c t)"))
+            y = psum.tile([P, N // P, width], F32, name="y", bufs=1)
+            res = ring.tile([P, N // P, width], F32, name="res")
+            for n in range(N // P):
+                cols = slice(n * P, (n + 1) * P)
+                nc.tensor.matmul_mx(
+                    y[:, n, :],
+                    lhsT=w2_codes[:, cols].bitcast(FP8X4),
+                    lhsT_scale=w2_scales[:, cols],
+                    rhs=codes[:].bitcast(FP8X4),
+                    rhs_scale=scales[:],
+                    start=True,
+                    stop=True,
+                )
+            for n in range(N // P):
+                nc.scalar.activation(res[:, n, :], y[:, n, :], IDENTITY, bias=bias[:, n : n + 1])
+            nc.sync.dma_start(out[:, lo:hi].rearrange("(n p) j -> p n j", p=P), res[:])
+
+        cds = {}
+        diffs = []
+        for i, (lo, hi) in enumerate(CHUNKS):
+            for j in range(lo // P, hi // P):
+                cds[j] = imaginary(j)
+            diffs.append(turn(lo, hi, cds))
+            if i >= 1:
+                finish(*CHUNKS[i - 1], diffs[i - 1], cast_scalar)
+        finish(*CHUNKS[-1], diffs[-1], cast_vector)

@@ -15,15 +15,17 @@ U8 = mybir.dt.uint8
 FP8X4 = mybir.dt.float8_e4m3fn_x4
 FP4X4 = mybir.dt.float4_e2m1fn_x4
 MULT = mybir.AluOpType.mult
-ADD = mybir.AluOpType.add
 COPY = mybir.ActivationFunctionType.Copy
 IDENTITY = mybir.ActivationFunctionType.Identity
 
 P = 128
 PACK = 4
-PASSES = K // (P * PACK)
+PASSES = 2
 TILES = S // P
-CHUNKS = [(0, 256), (256, 512), (512, 768), (768, 896), (896, 1024)]
+CHUNKS = [[0,256],[256,512],[512,768],[768,896],[896,1024]]
+STYLE = "ssuvv"
+LATE_D = [3,4,5,6,7]
+REVERSED = "ABC"
 
 
 def tile_list_complex_triple_messages_kernel(
@@ -36,179 +38,176 @@ def tile_list_complex_triple_messages_kernel(
         psum = ctx.enter_context(tc.psum_pool(name="psum", bufs=1))
 
         offsets = keep.tile([P, S // 16], U16, name="offsets")
-        nc.sync.dma_start(offsets[:], offs)
-
-        bias = keep.tile([P, N // P], F32, name="bias")
-        with nc.allow_non_contiguous_dma(reason="one bias value a partition"):
-            nc.sync.dma_start(bias[:], b2.rearrange("(c p) -> p c", p=P))
         tab_w = [keep.tile([P, T], I32, name=f"tab_w{a}") for a in range(PASSES)]
         tab_src = [tab_words[a].rearrange("p t i -> p (t i)").bitcast(I32) for a in range(PASSES)]
-        for c in range(0, T, 512):
-            nc.sync.dma_start(tab_w[0][:, c : c + 512], tab_src[0][:, c : c + 512])
-        fp4_w = []
-        for name, src in (("wb_w", wb_words), ("wd_w", wd_words)):
-            fw = keep.tile([P, PASSES, H // 2], I32, name=name, align_bytes=64)
-            nc.sync.dma_start(fw[:], src.rearrange("a p n -> p a n").bitcast(I32))
-            fp4_w.append(fw)
-        tab_sc = keep.tile([P, PASSES, T // 4], I32, name="tab_sc", align_bytes=64)
-        nc.gpsimd.memset(tab_sc[:], 0)
-        for q in range(4):
-            nc.sync.dma_start(
-                tab_sc[32 * q : 32 * q + 4, :, :],
-                tab_scales[:, 4 * q : 4 * q + 4, :].rearrange("a r t -> r a t").bitcast(I32),
-            )
-        nc.sync.dma_start(tab_w[1][:], tab_src[1])
+        tab_sc = keep.tile([P, 2, T // 4], I32, name="tab_sc", align_bytes=64)
         fp4_sc = keep.tile([P, 2, PASSES, H // 4], I32, name="fp4_sc", align_bytes=64)
+        fp4_w = [keep.tile([P, PASSES, H // 2], I32, name=f"fp4_w{w}", align_bytes=64) for w in range(2)]
+        bias = keep.tile([P, N // P], F32, name="bias")
+        gates = [keep.tile([P, T], F32, name=f"gate{t}") for t in range(PACK)]
+        gate_src = gT.rearrange("(p t) c -> t p c", t=PACK)
+        ident = keep.tile([P, P], F32, name="ident")
+        v_w = keep.tile([P, PASSES, S], U32, name="v_w", align_bytes=64)
+        v_sc = [keep.tile([P, S], U8, name=f"v_sc{a}", align_bytes=64) for a in range(PASSES)]
+        b_sb = keep.tile([P, TILES, PACK, P], F32, name="b_sb")
+        d_sb = keep.tile([P, TILES, PACK, P], F32, name="d_sb")
+        ab_sb = keep.tile([P, TILES, PACK, P], F32, name="ab_sb")
+        raw = {}
+        quantised = {}
+        state = {}
+        nc.gpsimd.memset(tab_sc[:], 0)
 
-        def load_fp4_scales(w, src):
+        def load_tab_scales(queue):
             for q in range(4):
-                nc.sync.dma_start(
+                queue.dma_start(
+                    tab_sc[32 * q : 32 * q + 4, :, :],
+                    tab_scales[:, 4 * q : 4 * q + 4, :].rearrange("a r t -> r a t").bitcast(I32),
+                )
+
+        def load_fp4_scales(queue, w, src):
+            for q in range(4):
+                queue.dma_start(
                     fp4_sc[32 * q : 32 * q + 4, w, :, :],
                     src[:, 4 * q : 4 * q + 4, :].rearrange("a r c -> r a c").bitcast(I32),
                 )
 
-        raw = {}
+        def load_fp4_words(queue, w, src):
+            queue.dma_start(fp4_w[w][:], src.rearrange("a p n -> p a n").bitcast(I32))
 
-        def load_raw(name, src, a):
-            r = keep.tile([P, PACK, H], F32, name=f"raw_{name}{a}")
-            nc.sync.dma_start(r[:], src[a * 512 : (a + 1) * 512, :].rearrange("(p j) c -> p j c", j=PACK))
-            raw[name, a] = r
+        def load_raw(queue, name, src, width):
+            raw[name] = keep.tile([P, PACK, width], F32, name=f"raw_{name}")
+            queue.dma_start(raw[name][:], src.rearrange("(p j) c -> p j c", j=PACK))
 
-        load_fp4_scales(0, wb_scales)
-        load_raw("wa", wa, 0)
-        load_fp4_scales(1, wd_scales)
-        load_raw("wa", wa, 1)
-        load_raw("wc", wc, 0)
-        load_raw("wc", wc, 1)
-        raw_w2 = keep.tile([P, PACK, N], F32, name="raw_w2")
-        nc.sync.dma_start(raw_w2[:], w2.rearrange("(p j) n -> p j n", j=PACK))
-        gates = []
-        for t in range(PACK):
-            g = keep.tile([P, T], F32, name=f"gate{t}")
-            nc.sync.dma_start(g[:], gT.rearrange("(p t) c -> t p c", t=PACK)[t])
-            gates.append(g)
-        ident = keep.tile([P, P], F32, name="ident")
-        make_identity(nc, ident[:])
-
-        v_w = keep.tile([P, PASSES, S], U32, name="v_w", align_bytes=64)
-        v_sc = keep.tile([P, PASSES, S], U8, name="v_sc", align_bytes=64)
+        def load_bias(queue):
+            with nc.allow_non_contiguous_dma(reason="one bias value a partition"):
+                queue.dma_start(bias[:], b2.rearrange("(c p) -> p c", p=P))
 
         def gather_scales(a, lo, hi):
-            nc.vector.tensor_copy(
-                v_sc[:, a, lo:hi], tab_sc[:, a, :].bitcast(U8).indirect(offsets[:, lo // 16 : hi // 16])
-            )
+            nc.vector.tensor_copy(v_sc[a][:, lo:hi], tab_sc[:, a, :].bitcast(U8).indirect(offsets[:, lo // 16 : hi // 16]))
+
+        def move_scales(queue, lo, hi):
+            queue.dma_start(v_sc[1][0:112, lo:hi].bitcast(I32), v_sc[0][4:116, lo:hi].bitcast(I32))
 
         def gather_words(a, lo, hi):
-            nc.vector.tensor_copy(
-                v_w[:, a, lo:hi], tab_w[a][:].bitcast(U32).indirect(offsets[:, lo // 16 : hi // 16])
-            )
+            nc.vector.tensor_copy(v_w[:, a, lo:hi], tab_w[a][:].bitcast(U32).indirect(offsets[:, lo // 16 : hi // 16]))
 
-        gather_words(0, 0, 512)
-        gather_scales(0, 0, 512)
-        gather_scales(1, 0, 512)
-        gather_words(1, 0, 256)
-        gather_words(1, 256, 512)
-        gather_words(0, 512, 1024)
-        gather_scales(0, 512, 1024)
-        gather_scales(1, 512, 1024)
-        gather_words(1, 512, 768)
-        gather_words(1, 768, 1024)
-
-        def product(j, moving):
-            acc = psum.tile([P, H], F32, name="acc", bufs=5)
+        def product(name, j):
+            acc = psum.tile([P, H], F32, name="acc", bufs=6)
             cols = slice(j * P, (j + 1) * P)
-            for a in range(PASSES):
-                codes, scales = moving(a)
+            order = (1, 0) if name in REVERSED else (0, 1)
+            for a in order:
+                plane = v_sc[a][:, cols]
+                if name in "BD":
+                    w = "BD".index(name)
+                    codes, scales = fp4_w[w][:, a, :].bitcast(FP4X4), fp4_sc[:, w, a, :].bitcast(U8)
+                else:
+                    codes, scales = quantised[("wa" if name == "A" else "wc") + str(a)]
+                    codes, scales = codes[:].bitcast(FP8X4), scales[:]
                 nc.tensor.matmul_mx(
                     acc[:],
                     lhsT=v_w[:, a, cols].bitcast(FP8X4),
-                    lhsT_scale=v_sc[:, a, cols],
+                    lhsT_scale=plane,
                     rhs=codes,
                     rhs_scale=scales,
-                    start=(a == 0),
-                    stop=(a == PASSES - 1),
+                    start=(a == order[0]),
+                    stop=(a == order[1]),
                 )
             return acc[:].rearrange("p (m t) -> p t m", t=PACK)
 
-        def fp4_operand(w):
-            return lambda a: (fp4_w[w][:, a, :].bitcast(FP4X4), fp4_sc[:, w, a, :].bitcast(U8))
-
-        b_sb = keep.tile([P, TILES, PACK, P], F32, name="b_sb")
-        d_sb = keep.tile([P, TILES, PACK, P], F32, name="d_sb")
-        ab_sb = keep.tile([P, TILES, PACK, P], F32, name="ab_sb")
-
         def view_b(j):
-            nc.scalar.copy(b_sb[:, j], product(j, fp4_operand(0)))
+            nc.scalar.copy(b_sb[:, j], product("B", j))
 
         def view_d(j):
-            nc.scalar.activation(d_sb[:, j], product(j, fp4_operand(1)), COPY, scale=-1.0)
+            nc.scalar.activation(d_sb[:, j], product("D", j), COPY, scale=-1.0)
 
-        for j in range(TILES):
-            view_b(j)
-            if j < TILES // 2:
-                view_d(j)
+        def real_part(j):
+            nc.vector.tensor_tensor(ab_sb[:, j], product("A", j), b_sb[:, j], MULT)
 
-        def cast_vector(dst, src):
-            nc.vector.tensor_copy(dst, src)
+        def cast(engine, dst, src):
+            src = src.rearrange("p t c -> p c t")
+            if engine == "v":
+                nc.vector.tensor_copy(dst, src)
+            else:
+                nc.scalar.copy(dst, src)
 
-        def cast_gpsimd(dst, src):
-            nc.gpsimd.tensor_scalar(dst, src, 1.0, 0.0, MULT, ADD)
-
-        def cast_scalar(dst, src):
-            nc.scalar.copy(dst, src)
-
-        def quantise(name, src, width, casts):
+        def quantise(name, width, engines):
             grouped = keep.tile([P, width, PACK], BF16, name=f"grp_{name}", align_bytes=64)
             codes = keep.tile([P, width], U32, name=f"codes_{name}", align_bytes=64)
             scales = keep.tile([P, width], U8, name=f"scales_{name}", align_bytes=64)
-            step = width // len(casts)
-            for c, cast in zip(range(0, width, step), casts):
-                cast(grouped[:, c : c + step, :], src[:, :, c : c + step].rearrange("p j c -> p c j"))
+            step = width // len(engines)
+            for c, engine in zip(range(0, width, step), engines):
+                cast(engine, grouped[:, c : c + step, :], raw[name][:, :, c : c + step])
             nc.vector.quantize_mx(codes[:].bitcast(FP8X4), scales[:], grouped[:].rearrange("p c j -> p (c j)"))
-            return codes, scales
+            quantised[name] = (codes, scales)
 
-        wa_q = [
-            quantise("wa0", raw["wa", 0], H, [cast_gpsimd] * 4),
-            quantise("wa1", raw["wa", 1], H, [cast_scalar, cast_scalar, cast_gpsimd, cast_gpsimd]),
-        ]
-        for j in range(TILES):
-            a_ps = product(j, lambda a: (wa_q[a][0][:].bitcast(FP8X4), wa_q[a][1][:]))
-            nc.vector.tensor_tensor(ab_sb[:, j], a_ps, b_sb[:, j], MULT)
-        wc_q = [quantise(f"wc{a}", raw["wc", a], H, [cast_gpsimd] * 4) for a in range(PASSES)]
-        for j in range(TILES // 2, TILES):
-            view_d(j)
-        w2_codes, w2_scales = quantise("w2", raw_w2, N, [cast_gpsimd] * 2)
-
-        def imaginary(j):
-            c_ps = product(j, lambda a: (wc_q[a][0][:].bitcast(FP8X4), wc_q[a][1][:]))
-            cd = ring.tile([P, PACK, P], F32, name="cd", bufs=4)
-            nc.vector.tensor_tensor(cd[:], c_ps, d_sb[:, j], MULT)
-            return cd
-
-        def turn(lo, hi, cds):
-            diff = ring.tile([P, PACK, hi - lo], F32, name="diff", bufs=4)
-            for j in range(lo // P, hi // P):
-                bank = psum.tile([P, PACK, P], F32, name="turned", bufs=2)
-                for t in range(PACK):
-                    nc.tensor.matmul(bank[:, t, :], ab_sb[:, j, t, :], ident[:], start=True, stop=False, is_transpose=True)
-                    nc.tensor.matmul(bank[:, t, :], cds[j][:, t, :], ident[:], start=False, stop=True, is_transpose=True)
-                nc.scalar.copy(diff[:, :, j * P - lo : (j + 1) * P - lo], bank[:])
-            return diff
-
-        def finish(lo, hi, diff, cast):
-            width = hi - lo
-            h = ring.tile([P, PACK, width], F32, name="h", bufs=4)
+        def turn(j, cd):
+            bank = psum.tile([P, PACK, P], F32, name="turned", bufs=1)
             for t in range(PACK):
-                nc.vector.tensor_tensor(
-                    h[:, t, :], gates[t][:].indirect(offsets[:, lo // 16 : hi // 16]), diff[:, t, :], MULT
-                )
-            grouped = ring.tile([P, width, PACK], BF16, name="h_grp", align_bytes=64)
-            cast(grouped[:], h[:].rearrange("p t c -> p c t"))
-            codes = ring.tile([P, width], U32, name="h_codes", align_bytes=64)
-            scales = ring.tile([P, width], U8, name="h_scales", align_bytes=64)
+                nc.tensor.matmul(bank[:, t, :], ab_sb[:, j, t, :], ident[:], start=True, stop=False, is_transpose=True)
+                nc.tensor.matmul(bank[:, t, :], cd[:, t, :], ident[:], start=False, stop=True, is_transpose=True)
+            return bank
+
+        def front(i):
+            lo, hi = CHUNKS[i]
+            width = hi - lo
+            tiles = range(lo // P, hi // P)
+            cds = {}
+            work = ring.tile([P, 2, PACK * width], F32, name="work", bufs=3)
+            for j in tiles:
+                if j in LATE_D:
+                    view_d(j)
+                c_ps = product("C", j)
+                cd = work[:, 0, PACK * (j * P - lo) : PACK * ((j + 1) * P - lo)].rearrange("p (t m) -> p t m", t=PACK)
+                nc.vector.tensor_tensor(cd, c_ps, d_sb[:, j], MULT)
+                cds[j] = cd
+            if STYLE[i] == "u":
+                first = lo - P if width == P and "pair" in state else lo
+                if first == lo:
+                    picked = keep.tile([P, PACK, max(width, 256)], F32, name=f"picked{i}")
+                else:
+                    picked = state.pop("pair")
+                grouped = ring.tile([P, width, PACK], BF16, name="h_grp", align_bytes=64, bufs=3)
+                if first == lo:
+                    for t in range(PACK):
+                        nc.vector.tensor_copy(
+                            picked[:, t, :], gates[t][:].indirect(offsets[:, lo // 16 : (lo + max(width, 256)) // 16])
+                        )
+                    if width == P:
+                        state["pair"] = picked
+                for j in tiles:
+                    bank = turn(j, cds[j])
+                    cols = slice(j * P - lo, (j + 1) * P - lo)
+                    nc.vector.tensor_tensor(
+                        grouped[:, cols, :],
+                        bank[:].rearrange("p t c -> p c t"),
+                        picked[:, :, j * P - first : (j + 1) * P - first].rearrange("p t c -> p c t"),
+                        MULT,
+                    )
+                state[i] = grouped
+                return
+            diff = work[:, 1, :].rearrange("p (t c) -> p t c", t=PACK)
+            for j in tiles:
+                nc.scalar.copy(diff[:, :, j * P - lo : (j + 1) * P - lo], turn(j, cds[j])[:])
+            state[i] = diff
+
+        def back(i):
+            lo, hi = CHUNKS[i]
+            width = hi - lo
+            grouped = state[i]
+            if STYLE[i] != "u":
+                h = ring.tile([P, PACK, width], F32, name="h", bufs=3)
+                for t in range(PACK):
+                    nc.vector.tensor_tensor(
+                        h[:, t, :], gates[t][:].indirect(offsets[:, lo // 16 : hi // 16]), state[i][:, t, :], MULT
+                    )
+                grouped = ring.tile([P, width, PACK], BF16, name="h_grp", align_bytes=64, bufs=3)
+                cast(STYLE[i], grouped[:], h[:])
+            codes = ring.tile([P, width], U32, name="h_codes", align_bytes=64, bufs=3)
+            scales = ring.tile([P, width], U8, name="h_scales", align_bytes=64, bufs=3)
             nc.vector.quantize_mx(codes[:].bitcast(FP8X4), scales[:], grouped[:].rearrange("p c t -> p (c t)"))
+            w2_codes, w2_scales = quantised["w2"]
             y = psum.tile([P, N // P, width], F32, name="y", bufs=1)
-            res = ring.tile([P, N // P, width], F32, name="res")
+            res = ring.tile([P, N // P, width], F32, name="res", bufs=3)
             for n in range(N // P):
                 cols = slice(n * P, (n + 1) * P)
                 nc.tensor.matmul_mx(
@@ -224,12 +223,67 @@ def tile_list_complex_triple_messages_kernel(
                 nc.scalar.activation(res[:, n, :], y[:, n, :], IDENTITY, bias=bias[:, n : n + 1])
             nc.sync.dma_start(out[:, lo:hi].rearrange("(n p) j -> p n j", p=P), res[:])
 
-        cds = {}
-        diffs = []
-        for i, (lo, hi) in enumerate(CHUNKS):
-            for j in range(lo // P, hi // P):
-                cds[j] = imaginary(j)
-            diffs.append(turn(lo, hi, cds))
-            if i >= 1:
-                finish(*CHUNKS[i - 1], diffs[i - 1], cast_scalar)
-        finish(*CHUNKS[-1], diffs[-1], cast_vector)
+        nc.sync.dma_start(offsets[:], offs)
+        nc.sync.dma_start(tab_w[0][:, 0:2048], tab_src[0][:, 0:2048])
+        nc.sync.dma_start(tab_w[1][:], tab_src[1])
+        load_fp4_words(nc.sync, 0, wb_words)
+        load_raw(nc.sync, "wa1", wa[512:1024, :], H)
+        load_raw(nc.sync, "wc0", wc[0:512, :], H)
+        load_raw(nc.sync, "wa0", wa[0:512, :], H)
+        load_fp4_words(nc.sync, 1, wd_words)
+        load_raw(nc.sync, "wc1", wc[512:1024, :], H)
+        nc.sync.dma_start(gates[0][:], gate_src[0])
+        make_identity(nc, ident[:])
+        load_fp4_scales(nc.scalar, 0, wb_scales)
+        load_tab_scales(nc.scalar)
+        load_bias(nc.scalar)
+        load_fp4_scales(nc.scalar, 1, wd_scales)
+        nc.sync.dma_start(gates[1][:], gate_src[1])
+        load_raw(nc.sync, "w2", w2, N)
+        nc.sync.dma_start(gates[2][:], gate_src[2])
+        nc.sync.dma_start(gates[3][:], gate_src[3])
+        gather_words(1, 0, 512)
+        gather_scales(1, 0, 256)
+        gather_scales(0, 0, 256)
+        gather_words(1, 512, 768)
+        gather_scales(0, 256, 512)
+        gather_scales(1, 256, 1024)
+        gather_scales(0, 512, 768)
+        gather_words(1, 768, 1024)
+        gather_scales(0, 768, 1024)
+        gather_words(0, 0, 512)
+        gather_words(0, 512, 1024)
+        view_d(0)
+        quantise("wa0", H, "v")
+        quantise("wa1", H, "sv")
+        view_b(0)
+        view_d(1)
+        quantise("w2", N, "ss")
+        view_b(1)
+        view_b(2)
+        view_b(3)
+        real_part(0)
+        real_part(1)
+        real_part(2)
+        view_b(4)
+        real_part(3)
+        quantise("wc0", H, "svvv")
+        quantise("wc1", H, "sssv")
+        view_b(5)
+        real_part(4)
+        real_part(5)
+        view_d(2)
+        view_b(6)
+        view_b(7)
+        real_part(6)
+        real_part(7)
+        front(0)
+        front(1)
+        front(2)
+        back(0)
+        front(3)
+        back(1)
+        front(4)
+        back(2)
+        back(3)
+        back(4)

@@ -20,12 +20,21 @@ IDENTITY = mybir.ActivationFunctionType.Identity
 
 P = 128
 PACK = 4
-PASSES = 2
+K_PASS = P * PACK
+PASSES = K // K_PASS
+QUADRANTS = 4
 TILES = S // P
-CHUNKS = [[0,256],[256,512],[512,768],[768,896],[896,1024]]
-STYLE = "ssuvv"
-LATE_D = [3,4,5,6,7]
-REVERSED = "ABC"
+PER_COLUMN = 16
+QUARTER = S // 4
+
+SCALAR_CHUNKS = [(0, 256), (256, 512)]
+VECTOR_QUARTERS = [[(512, 768)], [(768, 896), (896, 1024)]]
+EARLY_D = 3
+
+PRODUCT_BANKS = 5
+TURN_BANKS = 2
+CHUNKS_IN_FLIGHT = 2
+TAIL_BUFS = 3
 
 
 def tile_list_complex_triple_messages_kernel(
@@ -34,180 +43,174 @@ def tile_list_complex_triple_messages_kernel(
     nc = tc.nc
     with ExitStack() as ctx:
         keep = ctx.enter_context(tc.tile_pool(name="keep", bufs=1))
-        ring = ctx.enter_context(tc.tile_pool(name="ring", bufs=2))
+        ring = ctx.enter_context(tc.tile_pool(name="ring", bufs=CHUNKS_IN_FLIGHT))
         psum = ctx.enter_context(tc.psum_pool(name="psum", bufs=1))
 
-        offsets = keep.tile([P, S // 16], U16, name="offsets")
+        offsets = keep.tile([P, S // PER_COLUMN], U16, name="offsets")
         tab_w = [keep.tile([P, T], I32, name=f"tab_w{a}") for a in range(PASSES)]
-        tab_src = [tab_words[a].rearrange("p t i -> p (t i)").bitcast(I32) for a in range(PASSES)]
-        tab_sc = keep.tile([P, 2, T // 4], I32, name="tab_sc", align_bytes=64)
-        fp4_sc = keep.tile([P, 2, PASSES, H // 4], I32, name="fp4_sc", align_bytes=64)
-        fp4_w = [keep.tile([P, PASSES, H // 2], I32, name=f"fp4_w{w}", align_bytes=64) for w in range(2)]
+        tab_sc = keep.tile([P, PASSES, T // 4], I32, name="tab_sc", align_bytes=64)
+        fp4_sc = {w: keep.tile([P, PASSES, H // 4], I32, name=f"{w}_sc", align_bytes=64) for w in ("wb", "wd")}
+        fp4_w = {w: keep.tile([P, PASSES, H // 2], I32, name=f"{w}_w", align_bytes=64) for w in ("wb", "wd")}
+        rows = {(w, a): keep.tile([P, PACK, H], F32, name=f"{w}_rows{a}") for w in ("wa", "wc") for a in range(PASSES)}
+        rows["w2", 0] = keep.tile([P, PACK, N], F32, name="w2_rows")
         bias = keep.tile([P, N // P], F32, name="bias")
         gates = [keep.tile([P, T], F32, name=f"gate{t}") for t in range(PACK)]
-        gate_src = gT.rearrange("(p t) c -> t p c", t=PACK)
         ident = keep.tile([P, P], F32, name="ident")
         v_w = keep.tile([P, PASSES, S], U32, name="v_w", align_bytes=64)
-        v_sc = [keep.tile([P, S], U8, name=f"v_sc{a}", align_bytes=64) for a in range(PASSES)]
-        b_sb = keep.tile([P, TILES, PACK, P], F32, name="b_sb")
-        d_sb = keep.tile([P, TILES, PACK, P], F32, name="d_sb")
+        v_sc = keep.tile([P, PASSES, S], U8, name="v_sc", align_bytes=64)
+        b_sb = keep.tile([P, TILES, H], F32, name="b_sb")
+        minus_d_sb = keep.tile([P, TILES, H], F32, name="minus_d_sb")
         ab_sb = keep.tile([P, TILES, PACK, P], F32, name="ab_sb")
-        raw = {}
         quantised = {}
-        state = {}
+
+        def listed(lo, hi):
+            return offsets[:, lo // PER_COLUMN : hi // PER_COLUMN]
+
+        def load_scale_rows(dst, src):
+            for q in range(QUADRANTS):
+                nc.sync.dma_start(
+                    dst[32 * q : 32 * q + 4], src[:, 4 * q : 4 * q + 4, :].rearrange("a s c -> s a c").bitcast(I32)
+                )
+
+        def load_table_words(a):
+            nc.sync.dma_start(tab_w[a][:], tab_words[a].rearrange("p t i -> p (t i)").bitcast(I32))
+
+        def load_fp4_words(name, src):
+            nc.sync.dma_start(fp4_w[name][:], src.rearrange("a p n -> p a n").bitcast(I32))
+
+        def load_rows(name, src, a):
+            nc.sync.dma_start(rows[name, a][:], src[a * K_PASS : (a + 1) * K_PASS, :].rearrange("(p i) c -> p i c", i=PACK))
+
+        def load_gate(t):
+            nc.sync.dma_start(gates[t][:], gT.rearrange("(p t) c -> t p c", t=PACK)[t])
+
         nc.gpsimd.memset(tab_sc[:], 0)
-
-        def load_tab_scales(queue):
-            for q in range(4):
-                queue.dma_start(
-                    tab_sc[32 * q : 32 * q + 4, :, :],
-                    tab_scales[:, 4 * q : 4 * q + 4, :].rearrange("a r t -> r a t").bitcast(I32),
-                )
-
-        def load_fp4_scales(queue, w, src):
-            for q in range(4):
-                queue.dma_start(
-                    fp4_sc[32 * q : 32 * q + 4, w, :, :],
-                    src[:, 4 * q : 4 * q + 4, :].rearrange("a r c -> r a c").bitcast(I32),
-                )
-
-        def load_fp4_words(queue, w, src):
-            queue.dma_start(fp4_w[w][:], src.rearrange("a p n -> p a n").bitcast(I32))
-
-        def load_raw(queue, name, src, width):
-            raw[name] = keep.tile([P, PACK, width], F32, name=f"raw_{name}")
-            queue.dma_start(raw[name][:], src.rearrange("(p j) c -> p j c", j=PACK))
-
-        def load_bias(queue):
-            with nc.allow_non_contiguous_dma(reason="one bias value a partition"):
-                queue.dma_start(bias[:], b2.rearrange("(c p) -> p c", p=P))
-
-        def gather_scales(a, lo, hi):
-            nc.vector.tensor_copy(v_sc[a][:, lo:hi], tab_sc[:, a, :].bitcast(U8).indirect(offsets[:, lo // 16 : hi // 16]))
-
-        def move_scales(queue, lo, hi):
-            queue.dma_start(v_sc[1][0:112, lo:hi].bitcast(I32), v_sc[0][4:116, lo:hi].bitcast(I32))
+        nc.sync.dma_start(offsets[:], offs)
+        load_scale_rows(fp4_sc["wd"], wd_scales)
+        load_table_words(0)
+        load_scale_rows(tab_sc, tab_scales)
+        load_rows("wa", wa, 0)
+        load_fp4_words("wb", wb_words)
+        load_scale_rows(fp4_sc["wb"], wb_scales)
+        load_table_words(1)
+        load_rows("wa", wa, 1)
+        load_rows("wc", wc, 0)
+        with nc.allow_non_contiguous_dma(reason="one bias value for each partition and half of the outputs"):
+            nc.sync.dma_start(bias[:], b2.rearrange("(c p) -> p c", p=P))
+        load_rows("wc", wc, 1)
+        load_fp4_words("wd", wd_words)
+        for t in range(PACK - 1):
+            load_gate(t)
+        load_rows("w2", w2, 0)
+        load_gate(PACK - 1)
+        make_identity(nc, ident[:])
 
         def gather_words(a, lo, hi):
-            nc.vector.tensor_copy(v_w[:, a, lo:hi], tab_w[a][:].bitcast(U32).indirect(offsets[:, lo // 16 : hi // 16]))
+            nc.vector.tensor_copy(v_w[:, a, lo:hi], tab_w[a][:].bitcast(U32).indirect(listed(lo, hi)))
+
+        gather_words(0, 0, S)
+        for a in range(PASSES):
+            nc.vector.tensor_copy(v_sc[:, a, :], tab_sc[:, a, :].bitcast(U8).indirect(listed(0, S)))
+        for lo in range(0, S, QUARTER):
+            gather_words(1, lo, lo + QUARTER)
+
+        def interleave(copy, dst, src):
+            copy(dst.rearrange("p (c e) i -> p c i e", e=4), src.rearrange("p i (c e) -> p c i e", e=4))
+
+        def quantise(pool, name, grouped, width, bufs):
+            codes = pool.tile([P, width], U32, name=f"{name}_codes", align_bytes=64, bufs=bufs)
+            scales = pool.tile([P, width], U8, name=f"{name}_scales", align_bytes=64, bufs=bufs)
+            nc.vector.quantize_mx(codes[:].bitcast(FP8X4), scales[:], grouped[:].rearrange("p c i -> p (c i)"))
+            return codes, scales
+
+        def quantise_weight(name, a, copies):
+            width = rows[name, a].shape[2]
+            grouped = keep.tile([P, width, PACK], BF16, name=f"{name}_grouped{a}", align_bytes=64)
+            share = width // len(copies)
+            for c, copy in zip(range(0, width, share), copies):
+                interleave(copy, grouped[:, c : c + share, :], rows[name, a][:, :, c : c + share])
+            quantised[name, a] = quantise(keep, f"{name}{a}", grouped, width, 1)
 
         def product(name, j):
-            acc = psum.tile([P, H], F32, name="acc", bufs=6)
+            acc = psum.tile([P, H], F32, name="acc", bufs=PRODUCT_BANKS)
             cols = slice(j * P, (j + 1) * P)
-            order = (1, 0) if name in REVERSED else (0, 1)
-            for a in order:
-                plane = v_sc[a][:, cols]
-                if name in "BD":
-                    w = "BD".index(name)
-                    codes, scales = fp4_w[w][:, a, :].bitcast(FP4X4), fp4_sc[:, w, a, :].bitcast(U8)
+            for a in range(PASSES):
+                if name in fp4_w:
+                    codes, scales = fp4_w[name][:, a, :].bitcast(FP4X4), fp4_sc[name][:, a, :].bitcast(U8)
                 else:
-                    codes, scales = quantised[("wa" if name == "A" else "wc") + str(a)]
-                    codes, scales = codes[:].bitcast(FP8X4), scales[:]
+                    codes, scales = quantised[name, a][0][:].bitcast(FP8X4), quantised[name, a][1][:]
                 nc.tensor.matmul_mx(
                     acc[:],
                     lhsT=v_w[:, a, cols].bitcast(FP8X4),
-                    lhsT_scale=plane,
+                    lhsT_scale=v_sc[:, a, cols],
                     rhs=codes,
                     rhs_scale=scales,
-                    start=(a == order[0]),
-                    stop=(a == order[1]),
+                    start=(a == 0),
+                    stop=(a == PASSES - 1),
                 )
-            return acc[:].rearrange("p (m t) -> p t m", t=PACK)
+            return acc
 
-        def view_b(j):
-            nc.scalar.copy(b_sb[:, j], product("B", j))
+        def make_b(j):
+            nc.scalar.copy(b_sb[:, j, :], product("wb", j)[:])
 
-        def view_d(j):
-            nc.scalar.activation(d_sb[:, j], product("D", j), COPY, scale=-1.0)
+        def make_minus_d(j):
+            nc.scalar.activation(minus_d_sb[:, j, :], product("wd", j)[:], COPY, scale=-1.0)
 
-        def real_part(j):
-            nc.vector.tensor_tensor(ab_sb[:, j], product("A", j), b_sb[:, j], MULT)
+        def multiply_into_planes(planes, acc, other):
+            nc.vector.tensor_tensor(
+                planes.rearrange("p (u e) m -> p u m e", e=2),
+                acc[:].rearrange("p (m u e) -> p u m e", u=2, e=2),
+                other.rearrange("p (m u e) -> p u m e", u=2, e=2),
+                MULT,
+            )
 
-        def cast(engine, dst, src):
-            src = src.rearrange("p t c -> p c t")
-            if engine == "v":
-                nc.vector.tensor_copy(dst, src)
-            else:
-                nc.scalar.copy(dst, src)
+        def make_ab(j):
+            multiply_into_planes(ab_sb[:, j], product("wa", j), b_sb[:, j, :])
 
-        def quantise(name, width, engines):
-            grouped = keep.tile([P, width, PACK], BF16, name=f"grp_{name}", align_bytes=64)
-            codes = keep.tile([P, width], U32, name=f"codes_{name}", align_bytes=64)
-            scales = keep.tile([P, width], U8, name=f"scales_{name}", align_bytes=64)
-            step = width // len(engines)
-            for c, engine in zip(range(0, width, step), engines):
-                cast(engine, grouped[:, c : c + step, :], raw[name][:, :, c : c + step])
-            nc.vector.quantize_mx(codes[:].bitcast(FP8X4), scales[:], grouped[:].rearrange("p c j -> p (c j)"))
-            quantised[name] = (codes, scales)
+        for j in range(TILES // 2):
+            make_b(j)
+        quantise_weight("wa", 0, [nc.scalar.copy])
+        quantise_weight("wa", 1, [nc.vector.tensor_copy])
+        for j in range(TILES // 2, TILES - 1):
+            make_b(j)
+        for j in range(TILES - 2):
+            make_ab(j)
+        quantise_weight("wc", 0, [nc.scalar.copy, nc.vector.tensor_copy])
+        make_minus_d(0)
+        make_ab(TILES - 2)
+        for j in range(1, EARLY_D):
+            make_minus_d(j)
+        make_b(TILES - 1)
+        quantise_weight("wc", 1, [nc.scalar.copy])
+        make_ab(TILES - 1)
+        quantise_weight("w2", 0, [nc.scalar.copy, nc.scalar.copy])
 
-        def turn(j, cd):
-            bank = psum.tile([P, PACK, P], F32, name="turned", bufs=1)
+        def make_minus_cd(lo, hi):
+            buffer = ring.tile([P, 2, PACK * (hi - lo)], F32, name="chunk")
+            planes = {}
+            for n, j in enumerate(range(lo // P, hi // P)):
+                if j >= EARLY_D:
+                    make_minus_d(j)
+                planes[j] = buffer[:, 0, n * H : (n + 1) * H].rearrange("p (t m) -> p t m", t=PACK)
+                multiply_into_planes(planes[j], product("wc", j), minus_d_sb[:, j, :])
+            return buffer, planes
+
+        def difference(j, minus_cd):
+            bank = psum.tile([P, PACK, P], F32, name="turned", bufs=TURN_BANKS)
             for t in range(PACK):
-                nc.tensor.matmul(bank[:, t, :], ab_sb[:, j, t, :], ident[:], start=True, stop=False, is_transpose=True)
-                nc.tensor.matmul(bank[:, t, :], cd[:, t, :], ident[:], start=False, stop=True, is_transpose=True)
+                nc.tensor.matmul(bank[:, t, :], minus_cd[:, t, :], ident[:], start=True, stop=False, is_transpose=True)
+                nc.tensor.matmul(bank[:, t, :], ab_sb[:, j, t, :], ident[:], start=False, stop=True, is_transpose=True)
             return bank
 
-        def front(i):
-            lo, hi = CHUNKS[i]
-            width = hi - lo
-            tiles = range(lo // P, hi // P)
-            cds = {}
-            work = ring.tile([P, 2, PACK * width], F32, name="work", bufs=3)
-            for j in tiles:
-                if j in LATE_D:
-                    view_d(j)
-                c_ps = product("C", j)
-                cd = work[:, 0, PACK * (j * P - lo) : PACK * ((j + 1) * P - lo)].rearrange("p (t m) -> p t m", t=PACK)
-                nc.vector.tensor_tensor(cd, c_ps, d_sb[:, j], MULT)
-                cds[j] = cd
-            if STYLE[i] == "u":
-                first = lo - P if width == P and "pair" in state else lo
-                if first == lo:
-                    picked = keep.tile([P, PACK, max(width, 256)], F32, name=f"picked{i}")
-                else:
-                    picked = state.pop("pair")
-                grouped = ring.tile([P, width, PACK], BF16, name="h_grp", align_bytes=64, bufs=3)
-                if first == lo:
-                    for t in range(PACK):
-                        nc.vector.tensor_copy(
-                            picked[:, t, :], gates[t][:].indirect(offsets[:, lo // 16 : (lo + max(width, 256)) // 16])
-                        )
-                    if width == P:
-                        state["pair"] = picked
-                for j in tiles:
-                    bank = turn(j, cds[j])
-                    cols = slice(j * P - lo, (j + 1) * P - lo)
-                    nc.vector.tensor_tensor(
-                        grouped[:, cols, :],
-                        bank[:].rearrange("p t c -> p c t"),
-                        picked[:, :, j * P - first : (j + 1) * P - first].rearrange("p t c -> p c t"),
-                        MULT,
-                    )
-                state[i] = grouped
-                return
-            diff = work[:, 1, :].rearrange("p (t c) -> p t c", t=PACK)
-            for j in tiles:
-                nc.scalar.copy(diff[:, :, j * P - lo : (j + 1) * P - lo], turn(j, cds[j])[:])
-            state[i] = diff
+        def new_grouped_h(width):
+            return ring.tile([P, width, PACK], BF16, name="h_grouped", align_bytes=64, bufs=TAIL_BUFS)
 
-        def back(i):
-            lo, hi = CHUNKS[i]
+        def finish(lo, hi, grouped):
             width = hi - lo
-            grouped = state[i]
-            if STYLE[i] != "u":
-                h = ring.tile([P, PACK, width], F32, name="h", bufs=3)
-                for t in range(PACK):
-                    nc.vector.tensor_tensor(
-                        h[:, t, :], gates[t][:].indirect(offsets[:, lo // 16 : hi // 16]), state[i][:, t, :], MULT
-                    )
-                grouped = ring.tile([P, width, PACK], BF16, name="h_grp", align_bytes=64, bufs=3)
-                cast(STYLE[i], grouped[:], h[:])
-            codes = ring.tile([P, width], U32, name="h_codes", align_bytes=64, bufs=3)
-            scales = ring.tile([P, width], U8, name="h_scales", align_bytes=64, bufs=3)
-            nc.vector.quantize_mx(codes[:].bitcast(FP8X4), scales[:], grouped[:].rearrange("p c t -> p (c t)"))
-            w2_codes, w2_scales = quantised["w2"]
-            y = psum.tile([P, N // P, width], F32, name="y", bufs=1)
-            res = ring.tile([P, N // P, width], F32, name="res", bufs=3)
+            codes, scales = quantise(ring, "h", grouped, width, TAIL_BUFS)
+            w2_codes, w2_scales = quantised["w2", 0]
+            y = psum.tile([P, N // P, width], F32, name="y")
+            result = ring.tile([P, N // P, width], F32, name="result", bufs=TAIL_BUFS)
             for n in range(N // P):
                 cols = slice(n * P, (n + 1) * P)
                 nc.tensor.matmul_mx(
@@ -220,70 +223,35 @@ def tile_list_complex_triple_messages_kernel(
                     stop=True,
                 )
             for n in range(N // P):
-                nc.scalar.activation(res[:, n, :], y[:, n, :], IDENTITY, bias=bias[:, n : n + 1])
-            nc.sync.dma_start(out[:, lo:hi].rearrange("(n p) j -> p n j", p=P), res[:])
+                nc.scalar.activation(result[:, n, :], y[:, n, :], IDENTITY, bias=bias[:, n : n + 1])
+            nc.sync.dma_start(out[:, lo:hi].rearrange("(n p) j -> p n j", p=P), result[:])
 
-        nc.sync.dma_start(offsets[:], offs)
-        nc.sync.dma_start(tab_w[0][:, 0:2048], tab_src[0][:, 0:2048])
-        nc.sync.dma_start(tab_w[1][:], tab_src[1])
-        load_fp4_words(nc.sync, 0, wb_words)
-        load_raw(nc.sync, "wa1", wa[512:1024, :], H)
-        load_raw(nc.sync, "wc0", wc[0:512, :], H)
-        load_raw(nc.sync, "wa0", wa[0:512, :], H)
-        load_fp4_words(nc.sync, 1, wd_words)
-        load_raw(nc.sync, "wc1", wc[512:1024, :], H)
-        nc.sync.dma_start(gates[0][:], gate_src[0])
-        make_identity(nc, ident[:])
-        load_fp4_scales(nc.scalar, 0, wb_scales)
-        load_tab_scales(nc.scalar)
-        load_bias(nc.scalar)
-        load_fp4_scales(nc.scalar, 1, wd_scales)
-        nc.sync.dma_start(gates[1][:], gate_src[1])
-        load_raw(nc.sync, "w2", w2, N)
-        nc.sync.dma_start(gates[2][:], gate_src[2])
-        nc.sync.dma_start(gates[3][:], gate_src[3])
-        gather_words(1, 0, 512)
-        gather_scales(1, 0, 256)
-        gather_scales(0, 0, 256)
-        gather_words(1, 512, 768)
-        gather_scales(0, 256, 512)
-        gather_scales(1, 256, 1024)
-        gather_scales(0, 512, 768)
-        gather_words(1, 768, 1024)
-        gather_scales(0, 768, 1024)
-        gather_words(0, 0, 512)
-        gather_words(0, 512, 1024)
-        view_d(0)
-        quantise("wa0", H, "v")
-        quantise("wa1", H, "sv")
-        view_b(0)
-        view_d(1)
-        quantise("w2", N, "ss")
-        view_b(1)
-        view_b(2)
-        view_b(3)
-        real_part(0)
-        real_part(1)
-        real_part(2)
-        view_b(4)
-        real_part(3)
-        quantise("wc0", H, "svvv")
-        quantise("wc1", H, "sssv")
-        view_b(5)
-        real_part(4)
-        real_part(5)
-        view_d(2)
-        view_b(6)
-        view_b(7)
-        real_part(6)
-        real_part(7)
-        front(0)
-        front(1)
-        front(2)
-        back(0)
-        front(3)
-        back(1)
-        front(4)
-        back(2)
-        back(3)
-        back(4)
+        for lo, hi in SCALAR_CHUNKS:
+            buffer, planes = make_minus_cd(lo, hi)
+            diff = buffer[:, 1, :].rearrange("p (t c) -> p t c", t=PACK)
+            for j in planes:
+                nc.scalar.copy(diff[:, :, j * P - lo : (j + 1) * P - lo], difference(j, planes[j])[:])
+            h = ring.tile([P, PACK, hi - lo], F32, name="h")
+            for t in range(PACK):
+                nc.vector.tensor_tensor(h[:, t, :], gates[t][:].indirect(listed(lo, hi)), diff[:, t, :], MULT)
+            grouped = new_grouped_h(hi - lo)
+            interleave(nc.scalar.copy, grouped[:], h[:])
+            finish(lo, hi, grouped)
+
+        for chunks in VECTOR_QUARTERS:
+            first = chunks[0][0]
+            picked = keep.tile([P, PACK, QUARTER], F32, name=f"picked{first}")
+            for lo, hi in chunks:
+                buffer, planes = make_minus_cd(lo, hi)
+                grouped = new_grouped_h(hi - lo)
+                if lo == first:
+                    for t in range(PACK):
+                        nc.vector.tensor_copy(picked[:, t, :], gates[t][:].indirect(listed(first, first + QUARTER)))
+                for j in planes:
+                    nc.vector.tensor_tensor(
+                        grouped[:, j * P - lo : (j + 1) * P - lo, :].rearrange("p (c e) t -> p c t e", e=2),
+                        difference(j, planes[j])[:].rearrange("p t (c e) -> p c t e", e=2),
+                        picked[:, :, j * P - first : (j + 1) * P - first].rearrange("p t (c e) -> p c t e", e=2),
+                        MULT,
+                    )
+                finish(lo, hi, grouped)

@@ -15,6 +15,7 @@ U8 = mybir.dt.uint8
 FP8X4 = mybir.dt.float8_e4m3fn_x4
 FP4X4 = mybir.dt.float4_e2m1fn_x4
 MULT = mybir.AluOpType.mult
+ADD = mybir.AluOpType.add
 COPY = mybir.ActivationFunctionType.Copy
 IDENTITY = mybir.ActivationFunctionType.Identity
 
@@ -27,13 +28,14 @@ TILES = S // P
 PER_COLUMN = 16
 QUARTER = S // 4
 
-SCALAR_CHUNKS = [(0, 256), (256, 512)]
-VECTOR_QUARTERS = [[(512, 768)], [(768, 896), (896, 1024)]]
-EARLY_D = 3
+SCALAR_CHUNKS = [(0, 256), (256, 512), (512, 768)]
+VECTOR_CHUNK = (768, 1024)
+EARLY_D = 2
+H_BUFS = 2
+SECOND = 4
 
-PRODUCT_BANKS = 5
-TURN_BANKS = 2
-CHUNKS_IN_FLIGHT = 2
+MOVED = 112
+WORK_BANKS = 8
 TAIL_BUFS = 3
 
 
@@ -43,12 +45,12 @@ def tile_list_complex_triple_messages_kernel(
     nc = tc.nc
     with ExitStack() as ctx:
         keep = ctx.enter_context(tc.tile_pool(name="keep", bufs=1))
-        ring = ctx.enter_context(tc.tile_pool(name="ring", bufs=CHUNKS_IN_FLIGHT))
+        ring = ctx.enter_context(tc.tile_pool(name="ring", bufs=TAIL_BUFS))
         psum = ctx.enter_context(tc.psum_pool(name="psum", bufs=1))
 
         offsets = keep.tile([P, S // PER_COLUMN], U16, name="offsets")
         tab_w = [keep.tile([P, T], I32, name=f"tab_w{a}") for a in range(PASSES)]
-        tab_sc = keep.tile([P, PASSES, T // 4], I32, name="tab_sc", align_bytes=64)
+        tab_sc = keep.tile([P, T // 4], I32, name="tab_sc", align_bytes=64)
         fp4_sc = {w: keep.tile([P, PASSES, H // 4], I32, name=f"{w}_sc", align_bytes=64) for w in ("wb", "wd")}
         fp4_w = {w: keep.tile([P, PASSES, H // 2], I32, name=f"{w}_w", align_bytes=64) for w in ("wb", "wd")}
         rows = {(w, a): keep.tile([P, PACK, H], F32, name=f"{w}_rows{a}") for w in ("wa", "wc") for a in range(PASSES)}
@@ -56,21 +58,27 @@ def tile_list_complex_triple_messages_kernel(
         bias = keep.tile([P, N // P], F32, name="bias")
         gates = [keep.tile([P, T], F32, name=f"gate{t}") for t in range(PACK)]
         ident = keep.tile([P, P], F32, name="ident")
-        v_w = keep.tile([P, PASSES, S], U32, name="v_w", align_bytes=64)
-        v_sc = keep.tile([P, PASSES, S], U8, name="v_sc", align_bytes=64)
-        b_sb = keep.tile([P, TILES, H], F32, name="b_sb")
-        minus_d_sb = keep.tile([P, TILES, H], F32, name="minus_d_sb")
-        ab_sb = keep.tile([P, TILES, PACK, P], F32, name="ab_sb")
+        v_w = [keep.tile([P, S], U32, name=f"v_w{a}", align_bytes=64) for a in range(PASSES)]
+        v_sc = [keep.tile([P, S], U8, name=f"v_sc{a}", align_bytes=64) for a in range(PASSES)]
+        b_sb = [keep.tile([P, H], F32, name=f"b_sb{j}") for j in range(TILES)]
+        minus_d_sb = [keep.tile([P, H], F32, name=f"d_sb{j}") for j in range(TILES)]
+        ab_sb = [keep.tile([P, PACK, P], F32, name=f"ab_sb{j}") for j in range(TILES)]
+        cd_sb = [keep.tile([P, PACK, P], F32, name=f"cd_sb{j}") for j in range(TILES)]
+        picked = keep.tile([P, PACK, QUARTER], F32, name="picked")
         quantised = {}
 
         def listed(lo, hi):
             return offsets[:, lo // PER_COLUMN : hi // PER_COLUMN]
 
-        def load_scale_rows(dst, src):
-            for q in range(QUADRANTS):
+        def load_scale_rows(dst, src, quadrants=range(QUADRANTS)):
+            for q in quadrants:
                 nc.sync.dma_start(
                     dst[32 * q : 32 * q + 4], src[:, 4 * q : 4 * q + 4, :].rearrange("a s c -> s a c").bitcast(I32)
                 )
+
+        def load_table_scales():
+            for q in range(QUADRANTS):
+                nc.sync.dma_start(tab_sc[32 * q : 32 * q + 8], tab_scales[:, 4 * q : 4 * q + 4, :].bitcast(I32))
 
         def load_table_words(a):
             nc.sync.dma_start(tab_w[a][:], tab_words[a].rearrange("p t i -> p (t i)").bitcast(I32))
@@ -86,33 +94,35 @@ def tile_list_complex_triple_messages_kernel(
 
         nc.gpsimd.memset(tab_sc[:], 0)
         nc.sync.dma_start(offsets[:], offs)
-        load_scale_rows(fp4_sc["wd"], wd_scales)
+        load_scale_rows(fp4_sc["wb"], wb_scales, (0, 1))
+        load_table_scales()
         load_table_words(0)
-        load_scale_rows(tab_sc, tab_scales)
-        load_rows("wa", wa, 0)
-        load_fp4_words("wb", wb_words)
-        load_scale_rows(fp4_sc["wb"], wb_scales)
+        nc.vector.tensor_copy(v_sc[0][:], tab_sc[:].bitcast(U8).indirect(listed(0, S)))
         load_table_words(1)
+        load_scale_rows(fp4_sc["wb"], wb_scales, (2, 3))
+        load_fp4_words("wb", wb_words)
+        load_fp4_words("wd", wd_words)
+        nc.sync.dma_start(v_sc[1][0:MOVED].bitcast(I32), v_sc[0][SECOND : SECOND + MOVED].bitcast(I32))
+        load_rows("wa", wa, 0)
+        load_scale_rows(fp4_sc["wd"], wd_scales)
         load_rows("wa", wa, 1)
         load_rows("wc", wc, 0)
+        load_rows("wc", wc, 1)
         with nc.allow_non_contiguous_dma(reason="one bias value for each partition and half of the outputs"):
             nc.sync.dma_start(bias[:], b2.rearrange("(c p) -> p c", p=P))
-        load_rows("wc", wc, 1)
-        load_fp4_words("wd", wd_words)
-        for t in range(PACK - 1):
-            load_gate(t)
+        load_gate(0)
+        load_gate(1)
         load_rows("w2", w2, 0)
-        load_gate(PACK - 1)
+        load_gate(2)
+        load_gate(3)
         make_identity(nc, ident[:])
 
         def gather_words(a, lo, hi):
-            nc.vector.tensor_copy(v_w[:, a, lo:hi], tab_w[a][:].bitcast(U32).indirect(listed(lo, hi)))
+            nc.vector.tensor_copy(v_w[a][:, lo:hi], tab_w[a][:].bitcast(U32).indirect(listed(lo, hi)))
 
         gather_words(0, 0, S)
-        for a in range(PASSES):
-            nc.vector.tensor_copy(v_sc[:, a, :], tab_sc[:, a, :].bitcast(U8).indirect(listed(0, S)))
-        for lo in range(0, S, QUARTER):
-            gather_words(1, lo, lo + QUARTER)
+        for lo, hi in ((0, QUARTER), (QUARTER, 2 * QUARTER), (2 * QUARTER, S)):
+            gather_words(1, lo, hi)
 
         def interleave(copy, dst, src):
             copy(dst.rearrange("p (c e) i -> p c i e", e=4), src.rearrange("p i (c e) -> p c i e", e=4))
@@ -132,7 +142,7 @@ def tile_list_complex_triple_messages_kernel(
             quantised[name, a] = quantise(keep, f"{name}{a}", grouped, width, 1)
 
         def product(name, j):
-            acc = psum.tile([P, H], F32, name="acc", bufs=PRODUCT_BANKS)
+            acc = psum.tile([P, H], F32, name="work", bufs=WORK_BANKS)
             cols = slice(j * P, (j + 1) * P)
             for a in range(PASSES):
                 if name in fp4_w:
@@ -141,20 +151,14 @@ def tile_list_complex_triple_messages_kernel(
                     codes, scales = quantised[name, a][0][:].bitcast(FP8X4), quantised[name, a][1][:]
                 nc.tensor.matmul_mx(
                     acc[:],
-                    lhsT=v_w[:, a, cols].bitcast(FP8X4),
-                    lhsT_scale=v_sc[:, a, cols],
+                    lhsT=v_w[a][:, cols].bitcast(FP8X4),
+                    lhsT_scale=v_sc[a][:, cols],
                     rhs=codes,
                     rhs_scale=scales,
                     start=(a == 0),
                     stop=(a == PASSES - 1),
                 )
             return acc
-
-        def make_b(j):
-            nc.scalar.copy(b_sb[:, j, :], product("wb", j)[:])
-
-        def make_minus_d(j):
-            nc.scalar.activation(minus_d_sb[:, j, :], product("wd", j)[:], COPY, scale=-1.0)
 
         def multiply_into_planes(planes, acc, other):
             nc.vector.tensor_tensor(
@@ -164,57 +168,42 @@ def tile_list_complex_triple_messages_kernel(
                 MULT,
             )
 
-        def make_ab(j):
-            multiply_into_planes(ab_sb[:, j], product("wa", j), b_sb[:, j, :])
+        def make_minus_d(j):
+            nc.scalar.activation(minus_d_sb[j][:], product("wd", j)[:], COPY, scale=-1.0)
 
-        for j in range(TILES // 2):
-            make_b(j)
-        quantise_weight("wa", 0, [nc.scalar.copy])
+        for j in range(TILES):
+            nc.scalar.copy(b_sb[j][:], product("wb", j)[:])
+        quantise_weight("wa", 0, [nc.vector.tensor_copy])
         quantise_weight("wa", 1, [nc.vector.tensor_copy])
-        for j in range(TILES // 2, TILES - 1):
-            make_b(j)
-        for j in range(TILES - 2):
-            make_ab(j)
-        quantise_weight("wc", 0, [nc.scalar.copy, nc.vector.tensor_copy])
-        make_minus_d(0)
-        make_ab(TILES - 2)
-        for j in range(1, EARLY_D):
+        for j in range(EARLY_D):
             make_minus_d(j)
-        make_b(TILES - 1)
+        quantise_weight("wc", 0, [nc.scalar.copy])
         quantise_weight("wc", 1, [nc.scalar.copy])
-        make_ab(TILES - 1)
-        quantise_weight("w2", 0, [nc.scalar.copy, nc.scalar.copy])
+        for j in range(TILES):
+            multiply_into_planes(ab_sb[j][:], product("wa", j), b_sb[j][:])
+        for j in range(EARLY_D, TILES):
+            make_minus_d(j)
+        for j in range(TILES):
+            multiply_into_planes(cd_sb[j][:], product("wc", j), minus_d_sb[j][:])
+        quantise_weight("w2", 0, [nc.scalar.copy])
 
-        def make_minus_cd(lo, hi):
-            buffer = ring.tile([P, 2, PACK * (hi - lo)], F32, name="chunk")
-            planes = {}
-            for n, j in enumerate(range(lo // P, hi // P)):
-                if j >= EARLY_D:
-                    make_minus_d(j)
-                planes[j] = buffer[:, 0, n * H : (n + 1) * H].rearrange("p (t m) -> p t m", t=PACK)
-                multiply_into_planes(planes[j], product("wc", j), minus_d_sb[:, j, :])
-            return buffer, planes
-
-        def difference(j, minus_cd):
-            bank = psum.tile([P, PACK, P], F32, name="turned", bufs=TURN_BANKS)
+        def difference(j):
+            bank = psum.tile([P, PACK, P], F32, name="work", bufs=WORK_BANKS)
             for t in range(PACK):
-                nc.tensor.matmul(bank[:, t, :], minus_cd[:, t, :], ident[:], start=True, stop=False, is_transpose=True)
-                nc.tensor.matmul(bank[:, t, :], ab_sb[:, j, t, :], ident[:], start=False, stop=True, is_transpose=True)
+                nc.tensor.matmul(bank[:, t, :], ab_sb[j][:, t, :], ident[:], start=True, stop=False, is_transpose=True)
+                nc.tensor.matmul(bank[:, t, :], cd_sb[j][:, t, :], ident[:], start=False, stop=True, is_transpose=True)
             return bank
 
-        def new_grouped_h(width):
-            return ring.tile([P, width, PACK], BF16, name="h_grouped", align_bytes=64, bufs=TAIL_BUFS)
-
-        def finish(lo, hi, grouped):
+        def finish(lo, hi, grouped, shared):
             width = hi - lo
             codes, scales = quantise(ring, "h", grouped, width, TAIL_BUFS)
             w2_codes, w2_scales = quantised["w2", 0]
-            y = psum.tile([P, N // P, width], F32, name="y")
             result = ring.tile([P, N // P, width], F32, name="result", bufs=TAIL_BUFS)
             for n in range(N // P):
                 cols = slice(n * P, (n + 1) * P)
+                y = psum.tile([P, width], F32, name="work", bufs=WORK_BANKS)
                 nc.tensor.matmul_mx(
-                    y[:, n, :],
+                    y[:],
                     lhsT=w2_codes[:, cols].bitcast(FP8X4),
                     lhsT_scale=w2_scales[:, cols],
                     rhs=codes[:].bitcast(FP8X4),
@@ -222,36 +211,39 @@ def tile_list_complex_triple_messages_kernel(
                     start=True,
                     stop=True,
                 )
-            for n in range(N // P):
-                nc.scalar.activation(result[:, n, :], y[:, n, :], IDENTITY, bias=bias[:, n : n + 1])
+                if shared and n == 1:
+                    nc.vector.tensor_scalar(result[:, n, :], y[:], bias[:, n : n + 1], None, op0=ADD)
+                else:
+                    nc.scalar.activation(result[:, n, :], y[:], IDENTITY, bias=bias[:, n : n + 1])
             nc.sync.dma_start(out[:, lo:hi].rearrange("(n p) j -> p n j", p=P), result[:])
 
+        def new_grouped_h(width):
+            return ring.tile([P, width, PACK], BF16, name="h_grouped", align_bytes=64, bufs=TAIL_BUFS)
+
+        diffs = {}
         for lo, hi in SCALAR_CHUNKS:
-            buffer, planes = make_minus_cd(lo, hi)
-            diff = buffer[:, 1, :].rearrange("p (t c) -> p t c", t=PACK)
-            for j in planes:
-                nc.scalar.copy(diff[:, :, j * P - lo : (j + 1) * P - lo], difference(j, planes[j])[:])
-            h = ring.tile([P, PACK, hi - lo], F32, name="h")
+            diffs[lo] = keep.tile([P, PACK, hi - lo], F32, name=f"diff{lo}")
+            for j in range(lo // P, hi // P):
+                nc.scalar.copy(diffs[lo][:, :, j * P - lo : (j + 1) * P - lo], difference(j)[:])
+        first, last = VECTOR_CHUNK
+        held = {j: difference(j) for j in range(first // P, last // P)}
+        for t in range(PACK):
+            nc.vector.tensor_copy(picked[:, t, :], gates[t][:].indirect(listed(first, last)))
+        for lo, hi in SCALAR_CHUNKS:
+            h = ring.tile([P, PACK, hi - lo], F32, name="h", bufs=H_BUFS)
             for t in range(PACK):
-                nc.vector.tensor_tensor(h[:, t, :], gates[t][:].indirect(listed(lo, hi)), diff[:, t, :], MULT)
+                nc.vector.tensor_tensor(h[:, t, :], gates[t][:].indirect(listed(lo, hi)), diffs[lo][:, t, :], MULT)
             grouped = new_grouped_h(hi - lo)
             interleave(nc.scalar.copy, grouped[:], h[:])
-            finish(lo, hi, grouped)
+            finish(lo, hi, grouped, hi == first)
 
-        for chunks in VECTOR_QUARTERS:
-            first = chunks[0][0]
-            picked = keep.tile([P, PACK, QUARTER], F32, name=f"picked{first}")
-            for lo, hi in chunks:
-                buffer, planes = make_minus_cd(lo, hi)
-                grouped = new_grouped_h(hi - lo)
-                if lo == first:
-                    for t in range(PACK):
-                        nc.vector.tensor_copy(picked[:, t, :], gates[t][:].indirect(listed(first, first + QUARTER)))
-                for j in planes:
-                    nc.vector.tensor_tensor(
-                        grouped[:, j * P - lo : (j + 1) * P - lo, :].rearrange("p (c e) t -> p c t e", e=2),
-                        difference(j, planes[j])[:].rearrange("p t (c e) -> p c t e", e=2),
-                        picked[:, :, j * P - first : (j + 1) * P - first].rearrange("p t (c e) -> p c t e", e=2),
-                        MULT,
-                    )
-                finish(lo, hi, grouped)
+        grouped = new_grouped_h(last - first)
+        for j in held:
+            cols = slice(j * P - first, (j + 1) * P - first)
+            nc.vector.tensor_tensor(
+                grouped[:, cols, :].rearrange("p (c e) t -> p c t e", e=2),
+                held[j][:].rearrange("p t (c e) -> p c t e", e=2),
+                picked[:, :, cols].rearrange("p t (c e) -> p c t e", e=2),
+                MULT,
+            )
+        finish(first, last, grouped, True)

@@ -28,15 +28,24 @@ TILES = S // P
 PER_COLUMN = 16
 QUARTER = S // 4
 
-SCALAR_CHUNKS = [(0, 256), (256, 512), (512, 768)]
-VECTOR_CHUNK = (768, 1024)
-EARLY_D = 2
+W1_PIECES = ((0, 512), (512, 1024))
+GATHERS = [(0, 512, [(0, 256, [(0, 256)]), (256, 512, [(256, 512)])])]
+HELD_FROM = 512
+VECTOR_ROUNDS_FROM = 768
+SHARED_FROM = 512
+AB_ON_GPSIMD = ()
+TURN_LAG = 8
+MID_D = 6
+DIRECT_FROM = 768
+ON_GPSIMD = (6, 7)
+C_ORDER = (6, 7, 0, 1, 2, 3, 4, 5)
+EARLY_D = 0
 H_BUFS = 2
 SECOND = 4
 
 MOVED = 112
 WORK_BANKS = 8
-TAIL_BUFS = 3
+TAIL_BUFS = 4
 
 
 def tile_list_complex_triple_messages_kernel(
@@ -63,8 +72,7 @@ def tile_list_complex_triple_messages_kernel(
         b_sb = [keep.tile([P, H], F32, name=f"b_sb{j}") for j in range(TILES)]
         minus_d_sb = [keep.tile([P, H], F32, name=f"d_sb{j}") for j in range(TILES)]
         ab_sb = [keep.tile([P, PACK, P], F32, name=f"ab_sb{j}") for j in range(TILES)]
-        cd_sb = [keep.tile([P, PACK, P], F32, name=f"cd_sb{j}") for j in range(TILES)]
-        picked = keep.tile([P, PACK, QUARTER], F32, name="picked")
+        cd_sb = [b_sb[j][:].rearrange("p (t m) -> p t m", t=PACK) for j in range(TILES)]
         quantised = {}
 
         def listed(lo, hi):
@@ -101,13 +109,13 @@ def tile_list_complex_triple_messages_kernel(
         load_table_words(1)
         load_scale_rows(fp4_sc["wb"], wb_scales, (2, 3))
         load_fp4_words("wb", wb_words)
-        load_fp4_words("wd", wd_words)
         nc.sync.dma_start(v_sc[1][0:MOVED].bitcast(I32), v_sc[0][SECOND : SECOND + MOVED].bitcast(I32))
         load_rows("wa", wa, 0)
-        load_scale_rows(fp4_sc["wd"], wd_scales)
         load_rows("wa", wa, 1)
         load_rows("wc", wc, 0)
         load_rows("wc", wc, 1)
+        load_fp4_words("wd", wd_words)
+        load_scale_rows(fp4_sc["wd"], wd_scales)
         with nc.allow_non_contiguous_dma(reason="one bias value for each partition and half of the outputs"):
             nc.sync.dma_start(bias[:], b2.rearrange("(c p) -> p c", p=P))
         load_gate(0)
@@ -121,7 +129,7 @@ def tile_list_complex_triple_messages_kernel(
             nc.vector.tensor_copy(v_w[a][:, lo:hi], tab_w[a][:].bitcast(U32).indirect(listed(lo, hi)))
 
         gather_words(0, 0, S)
-        for lo, hi in ((0, QUARTER), (QUARTER, 2 * QUARTER), (2 * QUARTER, S)):
+        for lo, hi in W1_PIECES:
             gather_words(1, lo, hi)
 
         def interleave(copy, dst, src):
@@ -168,23 +176,48 @@ def tile_list_complex_triple_messages_kernel(
                 MULT,
             )
 
+        def copy_into_planes(flat, acc, scale):
+            nc.scalar.activation(
+                flat.rearrange("p (u e m) -> p u m e", u=2, e=2),
+                acc[:].rearrange("p (m u e) -> p u m e", u=2, e=2),
+                COPY,
+                scale=scale,
+            )
+
         def make_minus_d(j):
-            nc.scalar.activation(minus_d_sb[j][:], product("wd", j)[:], COPY, scale=-1.0)
+            if j in ON_GPSIMD:
+                copy_into_planes(minus_d_sb[j][:], product("wd", j), -1.0)
+            else:
+                nc.scalar.activation(minus_d_sb[j][:], product("wd", j)[:], COPY, scale=-1.0)
+
+        def make_minus_cd(j):
+            if j in ON_GPSIMD:
+                c_sb = keep.tile([P, H], F32, name=f"c_sb{j}")
+                copy_into_planes(c_sb[:], product("wc", j), 1.0)
+                nc.gpsimd.tensor_tensor(b_sb[j][:], c_sb[:], minus_d_sb[j][:], MULT)
+            else:
+                multiply_into_planes(cd_sb[j][:], product("wc", j), minus_d_sb[j][:])
 
         for j in range(TILES):
-            nc.scalar.copy(b_sb[j][:], product("wb", j)[:])
+            if j in AB_ON_GPSIMD:
+                copy_into_planes(b_sb[j][:], product("wb", j), 1.0)
+            else:
+                nc.scalar.copy(b_sb[j][:], product("wb", j)[:])
         quantise_weight("wa", 0, [nc.vector.tensor_copy])
         quantise_weight("wa", 1, [nc.vector.tensor_copy])
-        for j in range(EARLY_D):
+        for j in C_ORDER[:EARLY_D]:
             make_minus_d(j)
         quantise_weight("wc", 0, [nc.scalar.copy])
         quantise_weight("wc", 1, [nc.scalar.copy])
         for j in range(TILES):
-            multiply_into_planes(ab_sb[j][:], product("wa", j), b_sb[j][:])
-        for j in range(EARLY_D, TILES):
+            if j in AB_ON_GPSIMD:
+                a_sb = keep.tile([P, H], F32, name=f"a_sb{j}")
+                copy_into_planes(a_sb[:], product("wa", j), 1.0)
+                nc.gpsimd.tensor_tensor(ab_sb[j][:].rearrange("p t m -> p (t m)"), a_sb[:], b_sb[j][:], MULT)
+            else:
+                multiply_into_planes(ab_sb[j][:], product("wa", j), b_sb[j][:])
+        for j in C_ORDER[EARLY_D:MID_D]:
             make_minus_d(j)
-        for j in range(TILES):
-            multiply_into_planes(cd_sb[j][:], product("wc", j), minus_d_sb[j][:])
         quantise_weight("w2", 0, [nc.scalar.copy])
 
         def difference(j):
@@ -220,30 +253,52 @@ def tile_list_complex_triple_messages_kernel(
         def new_grouped_h(width):
             return ring.tile([P, width, PACK], BF16, name="h_grouped", align_bytes=64, bufs=TAIL_BUFS)
 
-        diffs = {}
-        for lo, hi in SCALAR_CHUNKS:
-            diffs[lo] = keep.tile([P, PACK, hi - lo], F32, name=f"diff{lo}")
-            for j in range(lo // P, hi // P):
-                nc.scalar.copy(diffs[lo][:, :, j * P - lo : (j + 1) * P - lo], difference(j)[:])
-        first, last = VECTOR_CHUNK
-        held = {j: difference(j) for j in range(first // P, last // P)}
-        for t in range(PACK):
-            nc.vector.tensor_copy(picked[:, t, :], gates[t][:].indirect(listed(first, last)))
-        for lo, hi in SCALAR_CHUNKS:
-            h = ring.tile([P, PACK, hi - lo], F32, name="h", bufs=H_BUFS)
+        diff = keep.tile([P, PACK, HELD_FROM], F32, name="diff")
+        h = keep.tile([P, PACK, S], F32, name="h")
+        held = {}
+        for step in range(TILES + TURN_LAG):
+            if step < TILES:
+                if step + MID_D < TILES:
+                    make_minus_d(C_ORDER[step + MID_D])
+                make_minus_cd(C_ORDER[step])
+            j = step - TURN_LAG
+            if j >= HELD_FROM // P:
+                held[j] = difference(j)
+            elif j >= 0:
+                nc.scalar.copy(diff[:, :, j * P : (j + 1) * P], difference(j)[:])
+        if held:
             for t in range(PACK):
-                nc.vector.tensor_tensor(h[:, t, :], gates[t][:].indirect(listed(lo, hi)), diffs[lo][:, t, :], MULT)
-            grouped = new_grouped_h(hi - lo)
-            interleave(nc.scalar.copy, grouped[:], h[:])
-            finish(lo, hi, grouped, hi == first)
+                nc.vector.tensor_copy(h[:, t, HELD_FROM:S], gates[t][:].indirect(listed(HELD_FROM, S)))
 
-        grouped = new_grouped_h(last - first)
-        for j in held:
-            cols = slice(j * P - first, (j + 1) * P - first)
-            nc.vector.tensor_tensor(
-                grouped[:, cols, :].rearrange("p (c e) t -> p c t e", e=2),
-                held[j][:].rearrange("p t (c e) -> p c t e", e=2),
-                picked[:, :, cols].rearrange("p t (c e) -> p c t e", e=2),
-                MULT,
-            )
-        finish(first, last, grouped, True)
+        def weigh(t, lo, hi):
+            nc.vector.tensor_tensor(h[:, t, lo:hi], gates[t][:].indirect(listed(lo, hi)), diff[:, t, lo:hi], MULT)
+
+        for lo, hi, pieces in GATHERS:
+            for t in range(PACK - 1):
+                weigh(t, lo, hi)
+            for a, b, parts in pieces:
+                weigh(PACK - 1, a, b)
+                for c, d in parts:
+                    grouped = new_grouped_h(d - c)
+                    interleave(nc.vector.tensor_copy if c >= VECTOR_ROUNDS_FROM else nc.scalar.copy, grouped[:], h[:, :, c:d])
+                    finish(c, d, grouped, c >= SHARED_FROM)
+
+        for lo in range(HELD_FROM, S, QUARTER):
+            grouped = new_grouped_h(QUARTER)
+            tiles = range(lo // P, (lo + QUARTER) // P)
+            if lo < DIRECT_FROM:
+                weighed = keep.tile([P, PACK, QUARTER], F32, name=f"weighed{lo}")
+                for j in tiles:
+                    nc.vector.tensor_tensor(
+                        weighed[:, :, j * P - lo : (j + 1) * P - lo], held[j][:], h[:, :, j * P : (j + 1) * P], MULT
+                    )
+                interleave(nc.scalar.copy, grouped[:], weighed[:])
+            else:
+                for j in tiles:
+                    nc.vector.tensor_tensor(
+                        grouped[:, j * P - lo : (j + 1) * P - lo, :].rearrange("p (c e) t -> p c t e", e=2),
+                        held[j][:].rearrange("p t (c e) -> p c t e", e=2),
+                        h[:, :, j * P : (j + 1) * P].rearrange("p t (c e) -> p c t e", e=2),
+                        MULT,
+                    )
+            finish(lo, lo + QUARTER, grouped, lo >= SHARED_FROM)

@@ -23,29 +23,20 @@ P = 128
 PACK = 4
 K_PASS = P * PACK
 PASSES = K // K_PASS
-QUADRANTS = 4
+QUADRANT = 32
+SCALE_ROWS = 4
 TILES = S // P
 PER_COLUMN = 16
-QUARTER = S // 4
 
-W1_PIECES = ((0, 512), (512, 1024))
-GATHERS = [(0, 512, [(0, 256, [(0, 256)]), (256, 512, [(256, 512)])])]
-HELD_FROM = 512
-VECTOR_ROUNDS_FROM = 768
-SHARED_FROM = 512
-AB_ON_GPSIMD = ()
-TURN_LAG = 8
-MID_D = 6
-DIRECT_FROM = 768
-ON_GPSIMD = (6, 7)
-C_ORDER = (6, 7, 0, 1, 2, 3, 4, 5)
-EARLY_D = 0
-H_BUFS = 2
-SECOND = 4
+PASS_SHIFT = QUADRANT // PASSES
 
-MOVED = 112
-WORK_BANKS = 8
-TAIL_BUFS = 4
+CHUNK = S // 4
+HALF = S // 2
+
+GPSIMD_TILES = list(range(TILES - 2, TILES))
+VECTOR_TILES = list(range(TILES - 2))
+
+BANKS = 8
 
 
 def tile_list_complex_triple_messages_kernel(
@@ -54,8 +45,8 @@ def tile_list_complex_triple_messages_kernel(
     nc = tc.nc
     with ExitStack() as ctx:
         keep = ctx.enter_context(tc.tile_pool(name="keep", bufs=1))
-        ring = ctx.enter_context(tc.tile_pool(name="ring", bufs=TAIL_BUFS))
-        psum = ctx.enter_context(tc.psum_pool(name="psum", bufs=1))
+        ring = ctx.enter_context(tc.tile_pool(name="ring", bufs=S // CHUNK))
+        psum = ctx.enter_context(tc.psum_pool(name="psum", bufs=BANKS))
 
         offsets = keep.tile([P, S // PER_COLUMN], U16, name="offsets")
         tab_w = [keep.tile([P, T], I32, name=f"tab_w{a}") for a in range(PASSES)]
@@ -70,23 +61,25 @@ def tile_list_complex_triple_messages_kernel(
         v_w = [keep.tile([P, S], U32, name=f"v_w{a}", align_bytes=64) for a in range(PASSES)]
         v_sc = [keep.tile([P, S], U8, name=f"v_sc{a}", align_bytes=64) for a in range(PASSES)]
         b_sb = [keep.tile([P, H], F32, name=f"b_sb{j}") for j in range(TILES)]
-        minus_d_sb = [keep.tile([P, H], F32, name=f"d_sb{j}") for j in range(TILES)]
-        ab_sb = [keep.tile([P, PACK, P], F32, name=f"ab_sb{j}") for j in range(TILES)]
-        cd_sb = [b_sb[j][:].rearrange("p (t m) -> p t m", t=PACK) for j in range(TILES)]
+        minus_d_sb = [keep.tile([P, H], F32, name=f"minus_d_sb{j}") for j in range(TILES)]
+        ab_planes = [keep.tile([P, H], F32, name=f"ab_planes{j}") for j in range(TILES)]
+        minus_cd_planes = b_sb
         quantised = {}
 
         def listed(lo, hi):
             return offsets[:, lo // PER_COLUMN : hi // PER_COLUMN]
 
-        def load_scale_rows(dst, src, quadrants=range(QUADRANTS)):
+        def load_fp4_scales(name, src, quadrants):
             for q in quadrants:
                 nc.sync.dma_start(
-                    dst[32 * q : 32 * q + 4], src[:, 4 * q : 4 * q + 4, :].rearrange("a s c -> s a c").bitcast(I32)
+                    fp4_sc[name][QUADRANT * q : QUADRANT * q + SCALE_ROWS],
+                    src[:, SCALE_ROWS * q : SCALE_ROWS * (q + 1), :].rearrange("a s c -> s a c").bitcast(I32),
                 )
 
         def load_table_scales():
-            for q in range(QUADRANTS):
-                nc.sync.dma_start(tab_sc[32 * q : 32 * q + 8], tab_scales[:, 4 * q : 4 * q + 4, :].bitcast(I32))
+            by_row = tab_scales.rearrange("a (q s) c -> s q a c", s=SCALE_ROWS)
+            for s in range(SCALE_ROWS):
+                nc.sync.dma_start(tab_sc[s:P:PASS_SHIFT], by_row[s].bitcast(I32))
 
         def load_table_words(a):
             nc.sync.dma_start(tab_w[a][:], tab_words[a].rearrange("p t i -> p (t i)").bitcast(I32))
@@ -102,55 +95,48 @@ def tile_list_complex_triple_messages_kernel(
 
         nc.gpsimd.memset(tab_sc[:], 0)
         nc.sync.dma_start(offsets[:], offs)
-        load_scale_rows(fp4_sc["wb"], wb_scales, (0, 1))
+        load_fp4_scales("wb", wb_scales, (0, 1))
         load_table_scales()
         load_table_words(0)
         nc.vector.tensor_copy(v_sc[0][:], tab_sc[:].bitcast(U8).indirect(listed(0, S)))
         load_table_words(1)
-        load_scale_rows(fp4_sc["wb"], wb_scales, (2, 3))
+        load_fp4_scales("wb", wb_scales, (2, 3))
         load_fp4_words("wb", wb_words)
-        nc.sync.dma_start(v_sc[1][0:MOVED].bitcast(I32), v_sc[0][SECOND : SECOND + MOVED].bitcast(I32))
         load_rows("wa", wa, 0)
+        nc.sync.dma_start(v_sc[1][0 : P - PASS_SHIFT].bitcast(I32), v_sc[0][PASS_SHIFT:P].bitcast(I32))
         load_rows("wa", wa, 1)
         load_rows("wc", wc, 0)
-        load_rows("wc", wc, 1)
         load_fp4_words("wd", wd_words)
-        load_scale_rows(fp4_sc["wd"], wd_scales)
-        with nc.allow_non_contiguous_dma(reason="one bias value for each partition and half of the outputs"):
-            nc.sync.dma_start(bias[:], b2.rearrange("(c p) -> p c", p=P))
-        load_gate(0)
-        load_gate(1)
+        load_rows("wc", wc, 1)
+        load_fp4_scales("wd", wd_scales, (0, 1, 2, 3))
+        for t in range(PACK - 1):
+            load_gate(t)
         load_rows("w2", w2, 0)
-        load_gate(2)
-        load_gate(3)
+        load_gate(PACK - 1)
+        with nc.allow_non_contiguous_dma(reason="one bias value for each partition and half of the outputs"):
+            nc.sync.dma_start(bias[:], b2.rearrange("(n p) -> p n", p=P))
         make_identity(nc, ident[:])
 
-        def gather_words(a, lo, hi):
-            nc.vector.tensor_copy(v_w[a][:, lo:hi], tab_w[a][:].bitcast(U32).indirect(listed(lo, hi)))
-
-        gather_words(0, 0, S)
-        for lo, hi in W1_PIECES:
-            gather_words(1, lo, hi)
+        for a in range(PASSES):
+            nc.vector.tensor_copy(v_w[a][:], tab_w[a][:].bitcast(U32).indirect(listed(0, S)))
 
         def interleave(copy, dst, src):
             copy(dst.rearrange("p (c e) i -> p c i e", e=4), src.rearrange("p i (c e) -> p c i e", e=4))
 
-        def quantise(pool, name, grouped, width, bufs):
-            codes = pool.tile([P, width], U32, name=f"{name}_codes", align_bytes=64, bufs=bufs)
-            scales = pool.tile([P, width], U8, name=f"{name}_scales", align_bytes=64, bufs=bufs)
+        def quantise(pool, name, grouped):
+            width = grouped.shape[1]
+            codes = pool.tile([P, width], U32, name=f"{name}_codes", align_bytes=64)
+            scales = pool.tile([P, width], U8, name=f"{name}_scales", align_bytes=64)
             nc.vector.quantize_mx(codes[:].bitcast(FP8X4), scales[:], grouped[:].rearrange("p c i -> p (c i)"))
             return codes, scales
 
-        def quantise_weight(name, a, copies):
-            width = rows[name, a].shape[2]
-            grouped = keep.tile([P, width, PACK], BF16, name=f"{name}_grouped{a}", align_bytes=64)
-            share = width // len(copies)
-            for c, copy in zip(range(0, width, share), copies):
-                interleave(copy, grouped[:, c : c + share, :], rows[name, a][:, :, c : c + share])
-            quantised[name, a] = quantise(keep, f"{name}{a}", grouped, width, 1)
+        def quantise_weight(name, a, copy):
+            grouped = keep.tile([P, rows[name, a].shape[2], PACK], BF16, name=f"{name}{a}_grouped", align_bytes=64)
+            interleave(copy, grouped[:], rows[name, a][:])
+            quantised[name, a] = quantise(keep, f"{name}{a}", grouped)
 
         def product(name, j):
-            acc = psum.tile([P, H], F32, name="work", bufs=WORK_BANKS)
+            acc = psum.tile([P, H], F32, name="bank")
             cols = slice(j * P, (j + 1) * P)
             for a in range(PASSES):
                 if name in fp4_w:
@@ -168,73 +154,70 @@ def tile_list_complex_triple_messages_kernel(
                 )
             return acc
 
+        def by_channel(tile):
+            return tile[:].rearrange("p (m u e) -> p u m e", u=2, e=2)
+
+        def by_plane(tile):
+            return tile[:].rearrange("p (u e m) -> p u m e", u=2, e=2)
+
         def multiply_into_planes(planes, acc, other):
-            nc.vector.tensor_tensor(
-                planes.rearrange("p (u e) m -> p u m e", e=2),
-                acc[:].rearrange("p (m u e) -> p u m e", u=2, e=2),
-                other.rearrange("p (m u e) -> p u m e", u=2, e=2),
-                MULT,
-            )
+            nc.vector.tensor_tensor(by_plane(planes), by_channel(acc), by_channel(other), MULT)
 
-        def copy_into_planes(flat, acc, scale):
-            nc.scalar.activation(
-                flat.rearrange("p (u e m) -> p u m e", u=2, e=2),
-                acc[:].rearrange("p (m u e) -> p u m e", u=2, e=2),
-                COPY,
-                scale=scale,
-            )
-
-        def make_minus_d(j):
-            if j in ON_GPSIMD:
-                copy_into_planes(minus_d_sb[j][:], product("wd", j), -1.0)
-            else:
-                nc.scalar.activation(minus_d_sb[j][:], product("wd", j)[:], COPY, scale=-1.0)
-
-        def make_minus_cd(j):
-            if j in ON_GPSIMD:
-                c_sb = keep.tile([P, H], F32, name=f"c_sb{j}")
-                copy_into_planes(c_sb[:], product("wc", j), 1.0)
-                nc.gpsimd.tensor_tensor(b_sb[j][:], c_sb[:], minus_d_sb[j][:], MULT)
-            else:
-                multiply_into_planes(cd_sb[j][:], product("wc", j), minus_d_sb[j][:])
+        def copy_into_planes(planes, acc, scale):
+            nc.scalar.activation(by_plane(planes), by_channel(acc), COPY, scale=scale)
 
         for j in range(TILES):
-            if j in AB_ON_GPSIMD:
-                copy_into_planes(b_sb[j][:], product("wb", j), 1.0)
-            else:
-                nc.scalar.copy(b_sb[j][:], product("wb", j)[:])
-        quantise_weight("wa", 0, [nc.vector.tensor_copy])
-        quantise_weight("wa", 1, [nc.vector.tensor_copy])
-        for j in C_ORDER[:EARLY_D]:
-            make_minus_d(j)
-        quantise_weight("wc", 0, [nc.scalar.copy])
-        quantise_weight("wc", 1, [nc.scalar.copy])
+            nc.scalar.copy(b_sb[j][:], product("wb", j)[:])
+        for a in range(PASSES):
+            quantise_weight("wa", a, nc.vector.tensor_copy)
+        for a in range(PASSES):
+            quantise_weight("wc", a, nc.scalar.copy)
         for j in range(TILES):
-            if j in AB_ON_GPSIMD:
-                a_sb = keep.tile([P, H], F32, name=f"a_sb{j}")
-                copy_into_planes(a_sb[:], product("wa", j), 1.0)
-                nc.gpsimd.tensor_tensor(ab_sb[j][:].rearrange("p t m -> p (t m)"), a_sb[:], b_sb[j][:], MULT)
-            else:
-                multiply_into_planes(ab_sb[j][:], product("wa", j), b_sb[j][:])
-        for j in C_ORDER[EARLY_D:MID_D]:
-            make_minus_d(j)
-        quantise_weight("w2", 0, [nc.scalar.copy])
+            multiply_into_planes(ab_planes[j], product("wa", j), b_sb[j])
+        for j in GPSIMD_TILES:
+            copy_into_planes(minus_d_sb[j], product("wd", j), -1.0)
+        for j in VECTOR_TILES:
+            nc.scalar.activation(minus_d_sb[j][:], product("wd", j)[:], COPY, scale=-1.0)
+        quantise_weight("w2", 0, nc.scalar.copy)
+        for j in GPSIMD_TILES:
+            c_planes = keep.tile([P, H], F32, name=f"c_planes{j}")
+            copy_into_planes(c_planes, product("wc", j), 1.0)
+            nc.gpsimd.tensor_tensor(minus_cd_planes[j][:], c_planes[:], minus_d_sb[j][:], MULT)
+        for j in VECTOR_TILES:
+            multiply_into_planes(minus_cd_planes[j], product("wc", j), minus_d_sb[j])
 
         def difference(j):
-            bank = psum.tile([P, PACK, P], F32, name="work", bufs=WORK_BANKS)
+            bank = psum.tile([P, PACK, P], F32, name="bank")
             for t in range(PACK):
-                nc.tensor.matmul(bank[:, t, :], ab_sb[j][:, t, :], ident[:], start=True, stop=False, is_transpose=True)
-                nc.tensor.matmul(bank[:, t, :], cd_sb[j][:, t, :], ident[:], start=False, stop=True, is_transpose=True)
+                plane = slice(t * P, (t + 1) * P)
+                nc.tensor.matmul(bank[:, t, :], ab_planes[j][:, plane], ident[:], start=True, stop=False, is_transpose=True)
+                nc.tensor.matmul(
+                    bank[:, t, :], minus_cd_planes[j][:, plane], ident[:], start=False, stop=True, is_transpose=True
+                )
             return bank
 
-        def finish(lo, hi, grouped, shared):
-            width = hi - lo
-            codes, scales = quantise(ring, "h", grouped, width, TAIL_BUFS)
+        diff = keep.tile([P, PACK, HALF], F32, name="diff")
+        for j in range(HALF // P):
+            nc.scalar.copy(diff[:, :, j * P : (j + 1) * P], difference(j)[:])
+        held = {j: difference(j) for j in range(HALF // P, TILES)}
+
+        picked = keep.tile([P, PACK, S], F32, name="picked")
+        for t in range(PACK):
+            nc.vector.tensor_copy(picked[:, t, HALF:S], gates[t][:].indirect(listed(HALF, S)))
+
+        def gather_and_weigh(t, lo, hi):
+            nc.vector.tensor_tensor(picked[:, t, lo:hi], gates[t][:].indirect(listed(lo, hi)), diff[:, t, lo:hi], MULT)
+
+        def new_grouped_h():
+            return ring.tile([P, CHUNK, PACK], BF16, name="h_grouped", align_bytes=64)
+
+        def finish(chunk, grouped):
+            codes, scales = quantise(ring, "h", grouped)
             w2_codes, w2_scales = quantised["w2", 0]
-            result = ring.tile([P, N // P, width], F32, name="result", bufs=TAIL_BUFS)
+            result = ring.tile([P, N // P, CHUNK], F32, name="result")
             for n in range(N // P):
                 cols = slice(n * P, (n + 1) * P)
-                y = psum.tile([P, width], F32, name="work", bufs=WORK_BANKS)
+                y = psum.tile([P, CHUNK], F32, name="bank")
                 nc.tensor.matmul_mx(
                     y[:],
                     lhsT=w2_codes[:, cols].bitcast(FP8X4),
@@ -244,61 +227,35 @@ def tile_list_complex_triple_messages_kernel(
                     start=True,
                     stop=True,
                 )
-                if shared and n == 1:
+                if chunk % 2 == 1 and n == 1:
                     nc.vector.tensor_scalar(result[:, n, :], y[:], bias[:, n : n + 1], None, op0=ADD)
                 else:
                     nc.scalar.activation(result[:, n, :], y[:], IDENTITY, bias=bias[:, n : n + 1])
-            nc.sync.dma_start(out[:, lo:hi].rearrange("(n p) j -> p n j", p=P), result[:])
+            nc.sync.dma_start(
+                out[:, chunk * CHUNK : (chunk + 1) * CHUNK].rearrange("(n p) j -> p n j", p=P), result[:]
+            )
 
-        def new_grouped_h(width):
-            return ring.tile([P, width, PACK], BF16, name="h_grouped", align_bytes=64, bufs=TAIL_BUFS)
+        for t in range(PACK - 1):
+            gather_and_weigh(t, 0, HALF)
+        for chunk in (0, 1):
+            gather_and_weigh(PACK - 1, chunk * CHUNK, (chunk + 1) * CHUNK)
+            grouped = new_grouped_h()
+            interleave(nc.scalar.copy, grouped[:], picked[:, :, chunk * CHUNK : (chunk + 1) * CHUNK])
+            finish(chunk, grouped)
 
-        diff = keep.tile([P, PACK, HELD_FROM], F32, name="diff")
-        h = keep.tile([P, PACK, S], F32, name="h")
-        held = {}
-        for step in range(TILES + TURN_LAG):
-            if step < TILES:
-                if step + MID_D < TILES:
-                    make_minus_d(C_ORDER[step + MID_D])
-                make_minus_cd(C_ORDER[step])
-            j = step - TURN_LAG
-            if j >= HELD_FROM // P:
-                held[j] = difference(j)
-            elif j >= 0:
-                nc.scalar.copy(diff[:, :, j * P : (j + 1) * P], difference(j)[:])
-        if held:
-            for t in range(PACK):
-                nc.vector.tensor_copy(h[:, t, HELD_FROM:S], gates[t][:].indirect(listed(HELD_FROM, S)))
+        weighed = keep.tile([P, PACK, CHUNK], F32, name="weighed")
+        for n, j in enumerate(range(2 * CHUNK // P, 3 * CHUNK // P)):
+            nc.vector.tensor_tensor(weighed[:, :, n * P : (n + 1) * P], held[j][:], picked[:, :, j * P : (j + 1) * P], MULT)
+        grouped = new_grouped_h()
+        interleave(nc.scalar.copy, grouped[:], weighed[:])
+        finish(2, grouped)
 
-        def weigh(t, lo, hi):
-            nc.vector.tensor_tensor(h[:, t, lo:hi], gates[t][:].indirect(listed(lo, hi)), diff[:, t, lo:hi], MULT)
-
-        for lo, hi, pieces in GATHERS:
-            for t in range(PACK - 1):
-                weigh(t, lo, hi)
-            for a, b, parts in pieces:
-                weigh(PACK - 1, a, b)
-                for c, d in parts:
-                    grouped = new_grouped_h(d - c)
-                    interleave(nc.vector.tensor_copy if c >= VECTOR_ROUNDS_FROM else nc.scalar.copy, grouped[:], h[:, :, c:d])
-                    finish(c, d, grouped, c >= SHARED_FROM)
-
-        for lo in range(HELD_FROM, S, QUARTER):
-            grouped = new_grouped_h(QUARTER)
-            tiles = range(lo // P, (lo + QUARTER) // P)
-            if lo < DIRECT_FROM:
-                weighed = keep.tile([P, PACK, QUARTER], F32, name=f"weighed{lo}")
-                for j in tiles:
-                    nc.vector.tensor_tensor(
-                        weighed[:, :, j * P - lo : (j + 1) * P - lo], held[j][:], h[:, :, j * P : (j + 1) * P], MULT
-                    )
-                interleave(nc.scalar.copy, grouped[:], weighed[:])
-            else:
-                for j in tiles:
-                    nc.vector.tensor_tensor(
-                        grouped[:, j * P - lo : (j + 1) * P - lo, :].rearrange("p (c e) t -> p c t e", e=2),
-                        held[j][:].rearrange("p t (c e) -> p c t e", e=2),
-                        h[:, :, j * P : (j + 1) * P].rearrange("p t (c e) -> p c t e", e=2),
-                        MULT,
-                    )
-            finish(lo, lo + QUARTER, grouped, lo >= SHARED_FROM)
+        grouped = new_grouped_h()
+        for n, j in enumerate(range(3 * CHUNK // P, TILES)):
+            nc.vector.tensor_tensor(
+                grouped[:, n * P : (n + 1) * P, :].rearrange("p (c e) t -> p c t e", e=2),
+                held[j][:].rearrange("p t (c e) -> p c t e", e=2),
+                picked[:, :, j * P : (j + 1) * P].rearrange("p t (c e) -> p c t e", e=2),
+                MULT,
+            )
+        finish(3, grouped)

@@ -33,8 +33,13 @@ PASS_SHIFT = QUADRANT // PASSES
 CHUNK = S // 4
 HALF = S // 2
 
-GPSIMD_TILES = list(range(TILES - 2, TILES))
-VECTOR_TILES = list(range(TILES - 2))
+GPSIMD_TILES = list(range(TILES))
+
+GPSIMD_AB_TILES = (0, 1)
+EARLY_A = 4
+
+GPSIMD_WEIGHS = ()
+CHUNKS = ((0, 512), (512, 768), (768, 1024))
 
 BANKS = 8
 
@@ -45,11 +50,11 @@ def tile_list_complex_triple_messages_kernel(
     nc = tc.nc
     with ExitStack() as ctx:
         keep = ctx.enter_context(tc.tile_pool(name="keep", bufs=1))
-        ring = ctx.enter_context(tc.tile_pool(name="ring", bufs=S // CHUNK))
+        ring = ctx.enter_context(tc.tile_pool(name="ring", bufs=3))
         psum = ctx.enter_context(tc.psum_pool(name="psum", bufs=BANKS))
 
         offsets = keep.tile([P, S // PER_COLUMN], U16, name="offsets")
-        tab_w = [keep.tile([P, T], I32, name=f"tab_w{a}") for a in range(PASSES)]
+        tab_w = [keep.tile([P, T], I32, name=f"tab_w{a}", align_bytes=64) for a in range(PASSES)]
         tab_sc = keep.tile([P, T // 4], I32, name="tab_sc", align_bytes=64)
         fp4_sc = {w: keep.tile([P, PASSES, H // 4], I32, name=f"{w}_sc", align_bytes=64) for w in ("wb", "wd")}
         fp4_w = {w: keep.tile([P, PASSES, H // 2], I32, name=f"{w}_w", align_bytes=64) for w in ("wb", "wd")}
@@ -95,13 +100,13 @@ def tile_list_complex_triple_messages_kernel(
 
         nc.gpsimd.memset(tab_sc[:], 0)
         nc.sync.dma_start(offsets[:], offs)
-        load_fp4_scales("wb", wb_scales, (0, 1))
+        load_fp4_words("wb", wb_words)
+        load_fp4_scales("wb", wb_scales, (0,))
         load_table_scales()
         load_table_words(0)
         nc.vector.tensor_copy(v_sc[0][:], tab_sc[:].bitcast(U8).indirect(listed(0, S)))
+        load_fp4_scales("wb", wb_scales, (1, 2, 3))
         load_table_words(1)
-        load_fp4_scales("wb", wb_scales, (2, 3))
-        load_fp4_words("wb", wb_words)
         load_rows("wa", wa, 0)
         nc.sync.dma_start(v_sc[1][0 : P - PASS_SHIFT].bitcast(I32), v_sc[0][PASS_SHIFT:P].bitcast(I32))
         load_rows("wa", wa, 1)
@@ -109,16 +114,16 @@ def tile_list_complex_triple_messages_kernel(
         load_fp4_words("wd", wd_words)
         load_rows("wc", wc, 1)
         load_fp4_scales("wd", wd_scales, (0, 1, 2, 3))
-        for t in range(PACK - 1):
-            load_gate(t)
         load_rows("w2", w2, 0)
-        load_gate(PACK - 1)
+        for t in range(PACK):
+            load_gate(t)
         with nc.allow_non_contiguous_dma(reason="one bias value for each partition and half of the outputs"):
             nc.sync.dma_start(bias[:], b2.rearrange("(n p) -> p n", p=P))
         make_identity(nc, ident[:])
 
         for a in range(PASSES):
-            nc.vector.tensor_copy(v_w[a][:], tab_w[a][:].bitcast(U32).indirect(listed(0, S)))
+            for lo in (0, HALF):
+                nc.vector.tensor_copy(v_w[a][:, lo : lo + HALF], tab_w[a][:].bitcast(U32).indirect(listed(lo, lo + HALF)))
 
         def interleave(copy, dst, src):
             copy(dst.rearrange("p (c e) i -> p c i e", e=4), src.rearrange("p i (c e) -> p c i e", e=4))
@@ -130,15 +135,25 @@ def tile_list_complex_triple_messages_kernel(
             nc.vector.quantize_mx(codes[:].bitcast(FP8X4), scales[:], grouped[:].rearrange("p c i -> p (c i)"))
             return codes, scales
 
-        def quantise_weight(name, a, copy):
-            grouped = keep.tile([P, rows[name, a].shape[2], PACK], BF16, name=f"{name}{a}_grouped", align_bytes=64)
-            interleave(copy, grouped[:], rows[name, a][:])
+        def on_gpsimd(dst, src):
+            nc.gpsimd.tensor_scalar(dst, src.rearrange("p i c -> p c i"), 1.0, 0.0, op0=MULT, op1=ADD)
+
+        def on_vector(dst, src):
+            interleave(nc.vector.tensor_copy, dst, src)
+
+        def on_scalar(dst, src):
+            interleave(nc.scalar.copy, dst, src)
+
+        def quantise_weight(name, a, shares, buffer):
+            grouped = keep.tile([P, rows[name, a].shape[2], PACK], BF16, name=buffer, align_bytes=64)
+            for rounder, lo, hi in shares:
+                rounder(grouped[:, lo:hi, :], rows[name, a][:, :, lo:hi])
             quantised[name, a] = quantise(keep, f"{name}{a}", grouped)
 
-        def product(name, j):
+        def product(name, j, passes=(0, 1)):
             acc = psum.tile([P, H], F32, name="bank")
             cols = slice(j * P, (j + 1) * P)
-            for a in range(PASSES):
+            for a in passes:
                 if name in fp4_w:
                     codes, scales = fp4_w[name][:, a, :].bitcast(FP4X4), fp4_sc[name][:, a, :].bitcast(U8)
                 else:
@@ -149,8 +164,8 @@ def tile_list_complex_triple_messages_kernel(
                     lhsT_scale=v_sc[a][:, cols],
                     rhs=codes,
                     rhs_scale=scales,
-                    start=(a == 0),
-                    stop=(a == PASSES - 1),
+                    start=(a == passes[0]),
+                    stop=(a == passes[-1]),
                 )
             return acc
 
@@ -166,25 +181,56 @@ def tile_list_complex_triple_messages_kernel(
         def copy_into_planes(planes, acc, scale):
             nc.scalar.activation(by_plane(planes), by_channel(acc), COPY, scale=scale)
 
+        quantise_weight("wa", 0, [(on_vector, 0, H)], "grouped_a0")
+        quantise_weight("wa", 1, [(on_vector, 0, H)], "grouped_a1")
         for j in range(TILES):
-            nc.scalar.copy(b_sb[j][:], product("wb", j)[:])
-        for a in range(PASSES):
-            quantise_weight("wa", a, nc.vector.tensor_copy)
-        for a in range(PASSES):
-            quantise_weight("wc", a, nc.scalar.copy)
+            if j in GPSIMD_AB_TILES:
+                copy_into_planes(b_sb[j], product("wb", j), 1.0)
+            else:
+                nc.scalar.copy(b_sb[j][:], product("wb", j)[:])
+        wc_grouped = keep.tile([P, PASSES * H, PACK], BF16, name="tab_w0", align_bytes=64)
+        on_vector(wc_grouped[:, 0:H, :], rows["wc", 0][:])
+        a_planes = keep.tile([P, len(GPSIMD_AB_TILES), H], F32, name="wc_codes", align_bytes=64)
         for j in range(TILES):
-            multiply_into_planes(ab_planes[j], product("wa", j), b_sb[j])
-        for j in GPSIMD_TILES:
-            copy_into_planes(minus_d_sb[j], product("wd", j), -1.0)
-        for j in VECTOR_TILES:
-            nc.scalar.activation(minus_d_sb[j][:], product("wd", j)[:], COPY, scale=-1.0)
-        quantise_weight("w2", 0, nc.scalar.copy)
-        for j in GPSIMD_TILES:
-            c_planes = keep.tile([P, H], F32, name=f"c_planes{j}")
-            copy_into_planes(c_planes, product("wc", j), 1.0)
-            nc.gpsimd.tensor_tensor(minus_cd_planes[j][:], c_planes[:], minus_d_sb[j][:], MULT)
-        for j in VECTOR_TILES:
-            multiply_into_planes(minus_cd_planes[j], product("wc", j), minus_d_sb[j])
+            acc = product("wa", j, (0, 1) if j < EARLY_A else (1, 0))
+            if j in GPSIMD_AB_TILES:
+                planes = a_planes[:, GPSIMD_AB_TILES.index(j), :]
+                copy_into_planes(planes, acc, 1.0)
+                nc.gpsimd.tensor_tensor(ab_planes[j][:], planes, b_sb[j][:], MULT)
+            else:
+                multiply_into_planes(ab_planes[j], acc, b_sb[j])
+        on_scalar(wc_grouped[:, H : 2 * H, :], rows["wc", 1][:])
+        wc_codes, wc_scales = quantise(keep, "wc", wc_grouped)
+        for a in range(PASSES):
+            quantised["wc", a] = (wc_codes[:, a * H : (a + 1) * H], wc_scales[:, a * H : (a + 1) * H])
+        quantise_weight("w2", 0, [(on_gpsimd, 0, N)], "grouped_w2")
+
+        def make_minus_d(j):
+            if j in GPSIMD_TILES:
+                copy_into_planes(minus_d_sb[j], product("wd", j), -1.0)
+            else:
+                nc.scalar.activation(minus_d_sb[j][:], product("wd", j)[:], COPY, scale=-1.0)
+
+        def make_minus_cd(j):
+            if j in GPSIMD_TILES:
+                c_planes = ring.tile([P, H], F32, name="c_planes")
+                copy_into_planes(c_planes, product("wc", j), 1.0)
+                nc.gpsimd.tensor_tensor(minus_cd_planes[j][:], c_planes[:], minus_d_sb[j][:], MULT)
+            else:
+                multiply_into_planes(minus_cd_planes[j], product("wc", j), minus_d_sb[j])
+
+        pairs = [(0, 1), (2, 3), (4, 5), (6, 7)]
+        for j in pairs[0] + pairs[1]:
+            make_minus_d(j)
+        for n, pair in enumerate(pairs):
+            for j in pair:
+                make_minus_cd(j)
+            for j in pairs[n + 2] if n + 2 < len(pairs) else ():
+                make_minus_d(j)
+
+        picked = keep.tile([P, PACK, S], F32, name="picked")
+        for t in range(PACK):
+            nc.vector.tensor_copy(picked[:, t, :], gates[t][:].indirect(listed(0, S)))
 
         def difference(j):
             bank = psum.tile([P, PACK, P], F32, name="bank")
@@ -196,28 +242,15 @@ def tile_list_complex_triple_messages_kernel(
                 )
             return bank
 
-        diff = keep.tile([P, PACK, HALF], F32, name="diff")
-        for j in range(HALF // P):
-            nc.scalar.copy(diff[:, :, j * P : (j + 1) * P], difference(j)[:])
-        held = {j: difference(j) for j in range(HALF // P, TILES)}
+        held = {j: difference(j) for j in range(TILES)}
 
-        picked = keep.tile([P, PACK, S], F32, name="picked")
-        for t in range(PACK):
-            nc.vector.tensor_copy(picked[:, t, HALF:S], gates[t][:].indirect(listed(HALF, S)))
-
-        def gather_and_weigh(t, lo, hi):
-            nc.vector.tensor_tensor(picked[:, t, lo:hi], gates[t][:].indirect(listed(lo, hi)), diff[:, t, lo:hi], MULT)
-
-        def new_grouped_h():
-            return ring.tile([P, CHUNK, PACK], BF16, name="h_grouped", align_bytes=64)
-
-        def finish(chunk, grouped):
+        def mix(lo, hi, grouped, vector_shares):
             codes, scales = quantise(ring, "h", grouped)
             w2_codes, w2_scales = quantised["w2", 0]
-            result = ring.tile([P, N // P, CHUNK], F32, name="result")
+            result = ring.tile([P, N // P, hi - lo], F32, name="result")
             for n in range(N // P):
                 cols = slice(n * P, (n + 1) * P)
-                y = psum.tile([P, CHUNK], F32, name="bank")
+                y = psum.tile([P, hi - lo], F32, name="bank")
                 nc.tensor.matmul_mx(
                     y[:],
                     lhsT=w2_codes[:, cols].bitcast(FP8X4),
@@ -227,35 +260,28 @@ def tile_list_complex_triple_messages_kernel(
                     start=True,
                     stop=True,
                 )
-                if chunk % 2 == 1 and n == 1:
+                if vector_shares and n == 1:
                     nc.vector.tensor_scalar(result[:, n, :], y[:], bias[:, n : n + 1], None, op0=ADD)
                 else:
                     nc.scalar.activation(result[:, n, :], y[:], IDENTITY, bias=bias[:, n : n + 1])
-            nc.sync.dma_start(
-                out[:, chunk * CHUNK : (chunk + 1) * CHUNK].rearrange("(n p) j -> p n j", p=P), result[:]
-            )
+            nc.sync.dma_start(out[:, lo:hi].rearrange("(n p) j -> p n j", p=P), result[:])
 
-        for t in range(PACK - 1):
-            gather_and_weigh(t, 0, HALF)
-        for chunk in (0, 1):
-            gather_and_weigh(PACK - 1, chunk * CHUNK, (chunk + 1) * CHUNK)
-            grouped = new_grouped_h()
-            interleave(nc.scalar.copy, grouped[:], picked[:, :, chunk * CHUNK : (chunk + 1) * CHUNK])
-            finish(chunk, grouped)
+        def weigh_on_gpsimd(dst, j):
+            diff = ring.tile([P, P, PACK], F32, name="diff")
+            nc.scalar.copy(diff[:], held[j][:].rearrange("p t c -> p c t"))
+            nc.gpsimd.tensor_tensor(dst, diff[:], picked[:, :, j * P : (j + 1) * P].rearrange("p t c -> p c t"), MULT)
 
-        weighed = keep.tile([P, PACK, CHUNK], F32, name="weighed")
-        for n, j in enumerate(range(2 * CHUNK // P, 3 * CHUNK // P)):
-            nc.vector.tensor_tensor(weighed[:, :, n * P : (n + 1) * P], held[j][:], picked[:, :, j * P : (j + 1) * P], MULT)
-        grouped = new_grouped_h()
-        interleave(nc.scalar.copy, grouped[:], weighed[:])
-        finish(2, grouped)
-
-        grouped = new_grouped_h()
-        for n, j in enumerate(range(3 * CHUNK // P, TILES)):
+        def weigh_out_of_psum(dst, j):
             nc.vector.tensor_tensor(
-                grouped[:, n * P : (n + 1) * P, :].rearrange("p (c e) t -> p c t e", e=2),
+                dst.rearrange("p (c e) t -> p c t e", e=2),
                 held[j][:].rearrange("p t (c e) -> p c t e", e=2),
                 picked[:, :, j * P : (j + 1) * P].rearrange("p t (c e) -> p c t e", e=2),
                 MULT,
             )
-        finish(3, grouped)
+
+        for lo, hi in CHUNKS:
+            grouped = ring.tile([P, hi - lo, PACK], BF16, name="h_grouped", align_bytes=64)
+            for j in range(lo // P, hi // P):
+                weigh = weigh_on_gpsimd if j in GPSIMD_WEIGHS else weigh_out_of_psum
+                weigh(grouped[:, j * P - lo : (j + 1) * P - lo, :], j)
+            mix(lo, hi, grouped, hi == S)

@@ -38,9 +38,6 @@ GPSIMD_TILES = list(range(TILES))
 GPSIMD_AB_TILES = (0, 1)
 EARLY_A = 4
 
-GPSIMD_WEIGHS = ()
-CHUNKS = ((0, 512), (512, 768), (768, 1024))
-
 BANKS = 8
 
 
@@ -51,6 +48,7 @@ def tile_list_complex_triple_messages_kernel(
     with ExitStack() as ctx:
         keep = ctx.enter_context(tc.tile_pool(name="keep", bufs=1))
         ring = ctx.enter_context(tc.tile_pool(name="ring", bufs=3))
+        tail = ctx.enter_context(tc.tile_pool(name="tail", bufs=6))
         psum = ctx.enter_context(tc.psum_pool(name="psum", bufs=BANKS))
 
         offsets = keep.tile([P, S // PER_COLUMN], U16, name="offsets")
@@ -111,19 +109,19 @@ def tile_list_complex_triple_messages_kernel(
         nc.sync.dma_start(v_sc[1][0 : P - PASS_SHIFT].bitcast(I32), v_sc[0][PASS_SHIFT:P].bitcast(I32))
         load_rows("wa", wa, 1)
         load_rows("wc", wc, 0)
-        load_fp4_words("wd", wd_words)
         load_rows("wc", wc, 1)
+        load_fp4_words("wd", wd_words)
         load_fp4_scales("wd", wd_scales, (0, 1, 2, 3))
-        load_rows("w2", w2, 0)
         for t in range(PACK):
             load_gate(t)
+        load_rows("w2", w2, 0)
         with nc.allow_non_contiguous_dma(reason="one bias value for each partition and half of the outputs"):
             nc.sync.dma_start(bias[:], b2.rearrange("(n p) -> p n", p=P))
         make_identity(nc, ident[:])
 
         for a in range(PASSES):
-            for lo in (0, HALF):
-                nc.vector.tensor_copy(v_w[a][:, lo : lo + HALF], tab_w[a][:].bitcast(U32).indirect(listed(lo, lo + HALF)))
+            for lo, hi in ((0, HALF), (HALF, S)) if a == 0 else ((0, S),):
+                nc.vector.tensor_copy(v_w[a][:, lo:hi], tab_w[a][:].bitcast(U32).indirect(listed(lo, hi)))
 
         def interleave(copy, dst, src):
             copy(dst.rearrange("p (c e) i -> p c i e", e=4), src.rearrange("p i (c e) -> p c i e", e=4))
@@ -134,9 +132,6 @@ def tile_list_complex_triple_messages_kernel(
             scales = pool.tile([P, width], U8, name=f"{name}_scales", align_bytes=64)
             nc.vector.quantize_mx(codes[:].bitcast(FP8X4), scales[:], grouped[:].rearrange("p c i -> p (c i)"))
             return codes, scales
-
-        def on_gpsimd(dst, src):
-            nc.gpsimd.tensor_scalar(dst, src.rearrange("p i c -> p c i"), 1.0, 0.0, op0=MULT, op1=ADD)
 
         def on_vector(dst, src):
             interleave(nc.vector.tensor_copy, dst, src)
@@ -203,7 +198,6 @@ def tile_list_complex_triple_messages_kernel(
         wc_codes, wc_scales = quantise(keep, "wc", wc_grouped)
         for a in range(PASSES):
             quantised["wc", a] = (wc_codes[:, a * H : (a + 1) * H], wc_scales[:, a * H : (a + 1) * H])
-        quantise_weight("w2", 0, [(on_gpsimd, 0, N)], "grouped_w2")
 
         def make_minus_d(j):
             if j in GPSIMD_TILES:
@@ -245,8 +239,9 @@ def tile_list_complex_triple_messages_kernel(
         held = {j: difference(j) for j in range(TILES)}
 
         def mix(lo, hi, grouped, vector_shares):
-            codes, scales = quantise(ring, "h", grouped)
-            w2_codes, w2_scales = quantised["w2", 0]
+            codes = tail.tile([P, hi - lo], U32, name="staged", align_bytes=64)
+            scales = ring.tile([P, hi - lo], U8, name="h_scales", align_bytes=64)
+            nc.vector.quantize_mx(codes[:].bitcast(FP8X4), scales[:], grouped.rearrange("p c t -> p (c t)"))
             result = ring.tile([P, N // P, hi - lo], F32, name="result")
             for n in range(N // P):
                 cols = slice(n * P, (n + 1) * P)
@@ -264,24 +259,35 @@ def tile_list_complex_triple_messages_kernel(
                     nc.vector.tensor_scalar(result[:, n, :], y[:], bias[:, n : n + 1], None, op0=ADD)
                 else:
                     nc.scalar.activation(result[:, n, :], y[:], IDENTITY, bias=bias[:, n : n + 1])
-            nc.sync.dma_start(out[:, lo:hi].rearrange("(n p) j -> p n j", p=P), result[:])
+                if lo == 0:
+                    nc.sync.dma_start(out[cols, lo:hi], result[:, n, :])
+            if lo > 0:
+                nc.sync.dma_start(out[:, lo:hi].rearrange("(n p) j -> p n j", p=P), result[:])
 
-        def weigh_on_gpsimd(dst, j):
-            diff = ring.tile([P, P, PACK], F32, name="diff")
-            nc.scalar.copy(diff[:], held[j][:].rearrange("p t c -> p c t"))
-            nc.gpsimd.tensor_tensor(dst, diff[:], picked[:, :, j * P : (j + 1) * P].rearrange("p t c -> p c t"), MULT)
+        grouped = keep.tile([P, S, PACK], BF16, name="tab_w1", align_bytes=64)
 
-        def weigh_out_of_psum(dst, j):
+        def weigh(j):
+            weighed = tail.tile([P, PACK, P], F32, name="staged", align_bytes=64)
+            nc.vector.tensor_tensor(weighed[:], held[j][:], picked[:, :, j * P : (j + 1) * P], MULT)
+            on_scalar(grouped[:, j * P : (j + 1) * P, :], weighed[:])
+
+        def weigh_and_round(j):
             nc.vector.tensor_tensor(
-                dst.rearrange("p (c e) t -> p c t e", e=2),
+                grouped[:, j * P : (j + 1) * P, :].rearrange("p (c e) t -> p c t e", e=2),
                 held[j][:].rearrange("p t (c e) -> p c t e", e=2),
                 picked[:, :, j * P : (j + 1) * P].rearrange("p t (c e) -> p c t e", e=2),
                 MULT,
             )
 
-        for lo, hi in CHUNKS:
-            grouped = ring.tile([P, hi - lo, PACK], BF16, name="h_grouped", align_bytes=64)
-            for j in range(lo // P, hi // P):
-                weigh = weigh_on_gpsimd if j in GPSIMD_WEIGHS else weigh_out_of_psum
-                weigh(grouped[:, j * P - lo : (j + 1) * P - lo, :], j)
-            mix(lo, hi, grouped, hi == S)
+        for j in range(6):
+            weigh(j)
+        w2_grouped = keep.tile([P, N, PACK], BF16, name="grouped_a0", align_bytes=64)
+        on_scalar(w2_grouped[:], rows["w2", 0][:])
+        w2_codes = tail.tile([P, N], U32, name="staged", align_bytes=64)
+        w2_scales = keep.tile([P, N], U8, name="w2_scales", align_bytes=64)
+        nc.vector.quantize_mx(w2_codes[:].bitcast(FP8X4), w2_scales[:], w2_grouped[:].rearrange("p c i -> p (c i)"))
+        mix(0, 512, grouped[:, 0:512, :], False)
+        weigh(6)
+        mix(512, 768, grouped[:, 512:768, :], False)
+        weigh_and_round(7)
+        mix(768, S, grouped[:, 768:S, :], True)

@@ -47,7 +47,7 @@ def tile_list_complex_triple_messages_kernel(
     nc = tc.nc
     with ExitStack() as ctx:
         keep = ctx.enter_context(tc.tile_pool(name="keep", bufs=1))
-        ring = ctx.enter_context(tc.tile_pool(name="ring", bufs=3))
+        ring = ctx.enter_context(tc.tile_pool(name="ring", bufs=4))
         tail = ctx.enter_context(tc.tile_pool(name="tail", bufs=6))
         psum = ctx.enter_context(tc.psum_pool(name="psum", bufs=BANKS))
 
@@ -165,13 +165,13 @@ def tile_list_complex_triple_messages_kernel(
             return acc
 
         def by_channel(tile):
-            return tile[:].rearrange("p (m u e) -> p u m e", u=2, e=2)
+            return tile[:].rearrange("p (b m t) -> p b t m", m=4, t=PACK)
 
         def by_plane(tile):
-            return tile[:].rearrange("p (u e m) -> p u m e", u=2, e=2)
+            return tile[:].rearrange("p (t b m) -> p b t m", m=4, t=PACK)
 
-        def multiply_into_planes(planes, acc, other):
-            nc.vector.tensor_tensor(by_plane(planes), by_channel(acc), by_channel(other), MULT)
+        def multiply_into_planes(planes, acc, other_planes):
+            nc.vector.tensor_tensor(by_plane(planes), by_channel(acc), by_plane(other_planes), MULT)
 
         def copy_into_planes(planes, acc, scale):
             nc.scalar.activation(by_plane(planes), by_channel(acc), COPY, scale=scale)
@@ -179,10 +179,7 @@ def tile_list_complex_triple_messages_kernel(
         quantise_weight("wa", 0, [(on_vector, 0, H)], "grouped_a0")
         quantise_weight("wa", 1, [(on_vector, 0, H)], "grouped_a1")
         for j in range(TILES):
-            if j in GPSIMD_AB_TILES:
-                copy_into_planes(b_sb[j], product("wb", j), 1.0)
-            else:
-                nc.scalar.copy(b_sb[j][:], product("wb", j)[:])
+            copy_into_planes(b_sb[j], product("wb", j), 1.0)
         wc_grouped = keep.tile([P, PASSES * H, PACK], BF16, name="tab_w0", align_bytes=64)
         on_vector(wc_grouped[:, 0:H, :], rows["wc", 0][:])
         a_planes = keep.tile([P, len(GPSIMD_AB_TILES), H], F32, name="wc_codes", align_bytes=64)
@@ -200,18 +197,12 @@ def tile_list_complex_triple_messages_kernel(
             quantised["wc", a] = (wc_codes[:, a * H : (a + 1) * H], wc_scales[:, a * H : (a + 1) * H])
 
         def make_minus_d(j):
-            if j in GPSIMD_TILES:
-                copy_into_planes(minus_d_sb[j], product("wd", j), -1.0)
-            else:
-                nc.scalar.activation(minus_d_sb[j][:], product("wd", j)[:], COPY, scale=-1.0)
+            copy_into_planes(minus_d_sb[j], product("wd", j), -1.0)
 
         def make_minus_cd(j):
-            if j in GPSIMD_TILES:
-                c_planes = ring.tile([P, H], F32, name="c_planes")
-                copy_into_planes(c_planes, product("wc", j), 1.0)
-                nc.gpsimd.tensor_tensor(minus_cd_planes[j][:], c_planes[:], minus_d_sb[j][:], MULT)
-            else:
-                multiply_into_planes(minus_cd_planes[j], product("wc", j), minus_d_sb[j])
+            c_planes = ring.tile([P, H], F32, name="c_planes")
+            copy_into_planes(c_planes, product("wc", j), 1.0)
+            nc.gpsimd.tensor_tensor(minus_cd_planes[j][:], c_planes[:], minus_d_sb[j][:], MULT)
 
         pairs = [(0, 1), (2, 3), (4, 5), (6, 7)]
         for j in pairs[0] + pairs[1]:

@@ -35,7 +35,9 @@ HALF = S // 2
 
 GPSIMD_TILES = list(range(TILES))
 
-GPSIMD_AB_TILES = (0, 1)
+GPSIMD_AB_EARLY = (0, 1)
+GPSIMD_AB_LATE = (7,)
+GPSIMD_AB_TILES = GPSIMD_AB_EARLY + GPSIMD_AB_LATE
 EARLY_A = 4
 
 BANKS = 8
@@ -48,7 +50,7 @@ def tile_list_complex_triple_messages_kernel(
     with ExitStack() as ctx:
         keep = ctx.enter_context(tc.tile_pool(name="keep", bufs=1))
         ring = ctx.enter_context(tc.tile_pool(name="ring", bufs=4))
-        tail = ctx.enter_context(tc.tile_pool(name="tail", bufs=6))
+        tail = ctx.enter_context(tc.tile_pool(name="tail", bufs=5))
         psum = ctx.enter_context(tc.psum_pool(name="psum", bufs=BANKS))
 
         offsets = keep.tile([P, S // PER_COLUMN], U16, name="offsets")
@@ -124,7 +126,7 @@ def tile_list_complex_triple_messages_kernel(
                 nc.vector.tensor_copy(v_w[a][:, lo:hi], tab_w[a][:].bitcast(U32).indirect(listed(lo, hi)))
 
         def interleave(copy, dst, src):
-            copy(dst.rearrange("p (c e) i -> p c i e", e=4), src.rearrange("p i (c e) -> p c i e", e=4))
+            copy(dst.rearrange("p (c e) i -> p c i e", e=2), src.rearrange("p i (c e) -> p c i e", e=2))
 
         def quantise(pool, name, grouped):
             width = grouped.shape[1]
@@ -176,25 +178,30 @@ def tile_list_complex_triple_messages_kernel(
         def copy_into_planes(planes, acc, scale):
             nc.scalar.activation(by_plane(planes), by_channel(acc), COPY, scale=scale)
 
-        quantise_weight("wa", 0, [(on_vector, 0, H)], "grouped_a0")
+        quantise_weight("wa", 0, [(on_vector, 0, H // 2), (on_scalar, H // 2, H)], "grouped_a0")
         quantise_weight("wa", 1, [(on_vector, 0, H)], "grouped_a1")
         for j in range(TILES):
             copy_into_planes(b_sb[j], product("wb", j), 1.0)
         wc_grouped = keep.tile([P, PASSES * H, PACK], BF16, name="tab_w0", align_bytes=64)
         on_vector(wc_grouped[:, 0:H, :], rows["wc", 0][:])
-        a_planes = keep.tile([P, len(GPSIMD_AB_TILES), H], F32, name="wc_codes", align_bytes=64)
+        acc_a = {j: product("wa", j, (0, 1) if j < EARLY_A else (1, 0)) for j in range(TILES)}
+        for j in GPSIMD_AB_EARLY:
+            a_planes = ring.tile([P, H], F32, name="c_planes")
+            copy_into_planes(a_planes, acc_a[j], 1.0)
+            nc.gpsimd.tensor_tensor(ab_planes[j][:], a_planes[:], b_sb[j][:], MULT)
         for j in range(TILES):
-            acc = product("wa", j, (0, 1) if j < EARLY_A else (1, 0))
-            if j in GPSIMD_AB_TILES:
-                planes = a_planes[:, GPSIMD_AB_TILES.index(j), :]
-                copy_into_planes(planes, acc, 1.0)
-                nc.gpsimd.tensor_tensor(ab_planes[j][:], planes, b_sb[j][:], MULT)
-            else:
-                multiply_into_planes(ab_planes[j], acc, b_sb[j])
+            if j not in GPSIMD_AB_TILES:
+                multiply_into_planes(ab_planes[j], acc_a[j], b_sb[j])
         on_scalar(wc_grouped[:, H : 2 * H, :], rows["wc", 1][:])
         wc_codes, wc_scales = quantise(keep, "wc", wc_grouped)
         for a in range(PASSES):
             quantised["wc", a] = (wc_codes[:, a * H : (a + 1) * H], wc_scales[:, a * H : (a + 1) * H])
+        late_ab = keep.tile([P, len(GPSIMD_AB_LATE), H], F32, name="tab_w0", align_bytes=64)
+        for n, j in enumerate(GPSIMD_AB_LATE):
+            a_planes = rows["wc", 1][:, n, :]
+            copy_into_planes(a_planes, acc_a[j], 1.0)
+            nc.gpsimd.tensor_tensor(late_ab[:, n, :], a_planes, b_sb[j][:], MULT)
+            ab_planes[j] = late_ab[:, n, :]
 
         def make_minus_d(j):
             copy_into_planes(minus_d_sb[j], product("wd", j), -1.0)
@@ -255,30 +262,28 @@ def tile_list_complex_triple_messages_kernel(
             if lo > 0:
                 nc.sync.dma_start(out[:, lo:hi].rearrange("(n p) j -> p n j", p=P), result[:])
 
-        grouped = keep.tile([P, S, PACK], BF16, name="tab_w1", align_bytes=64)
-
-        def weigh(j):
-            weighed = tail.tile([P, PACK, P], F32, name="staged", align_bytes=64)
-            nc.vector.tensor_tensor(weighed[:], held[j][:], picked[:, :, j * P : (j + 1) * P], MULT)
-            on_scalar(grouped[:, j * P : (j + 1) * P, :], weighed[:])
-
-        def weigh_and_round(j):
+        def weigh(grouped, lo, j):
             nc.vector.tensor_tensor(
-                grouped[:, j * P : (j + 1) * P, :].rearrange("p (c e) t -> p c t e", e=2),
+                grouped[:, j * P - lo : (j + 1) * P - lo, :].rearrange("p (c e) t -> p c t e", e=2),
                 held[j][:].rearrange("p t (c e) -> p c t e", e=2),
                 picked[:, :, j * P : (j + 1) * P].rearrange("p t (c e) -> p c t e", e=2),
                 MULT,
             )
 
-        for j in range(6):
-            weigh(j)
+        first = tail.tile([P, 512, PACK], BF16, name="staged", align_bytes=64)
+        for j in range(4):
+            weigh(first, 0, j)
+        second = tail.tile([P, 256, PACK], BF16, name="staged", align_bytes=64)
+        weigh(second, 512, 4)
         w2_grouped = keep.tile([P, N, PACK], BF16, name="grouped_a0", align_bytes=64)
         on_scalar(w2_grouped[:], rows["w2", 0][:])
         w2_codes = tail.tile([P, N], U32, name="staged", align_bytes=64)
         w2_scales = keep.tile([P, N], U8, name="w2_scales", align_bytes=64)
         nc.vector.quantize_mx(w2_codes[:].bitcast(FP8X4), w2_scales[:], w2_grouped[:].rearrange("p c i -> p (c i)"))
-        mix(0, 512, grouped[:, 0:512, :], False)
-        weigh(6)
-        mix(512, 768, grouped[:, 512:768, :], False)
-        weigh_and_round(7)
-        mix(768, S, grouped[:, 768:S, :], True)
+        mix(0, 512, first[:], False)
+        weigh(second, 512, 5)
+        third = tail.tile([P, 256, PACK], BF16, name="staged", align_bytes=64)
+        weigh(third, 768, 6)
+        mix(512, 768, second[:], False)
+        weigh(third, 768, 7)
+        mix(768, S, third[:], True)

@@ -30,16 +30,15 @@ PER_COLUMN = 16
 
 PASS_SHIFT = QUADRANT // PASSES
 
-CHUNK = S // 4
 HALF = S // 2
+HALF_TILES = TILES // 2
+CHUNK = 2 * P
+CHUNKS = S // CHUNK
 
-GPSIMD_TILES = list(range(TILES))
+GPSIMD_AB_TILES = 2
 
-GPSIMD_AB_EARLY = (0, 1)
-GPSIMD_AB_LATE = (7,)
-GPSIMD_AB_TILES = GPSIMD_AB_EARLY + GPSIMD_AB_LATE
-EARLY_A = 4
-
+RING = 4
+STAGED = 6
 BANKS = 8
 
 
@@ -49,8 +48,8 @@ def tile_list_complex_triple_messages_kernel(
     nc = tc.nc
     with ExitStack() as ctx:
         keep = ctx.enter_context(tc.tile_pool(name="keep", bufs=1))
-        ring = ctx.enter_context(tc.tile_pool(name="ring", bufs=4))
-        tail = ctx.enter_context(tc.tile_pool(name="tail", bufs=5))
+        ring = ctx.enter_context(tc.tile_pool(name="ring", bufs=RING))
+        tail = ctx.enter_context(tc.tile_pool(name="tail", bufs=STAGED))
         psum = ctx.enter_context(tc.psum_pool(name="psum", bufs=BANKS))
 
         offsets = keep.tile([P, S // PER_COLUMN], U16, name="offsets")
@@ -65,10 +64,10 @@ def tile_list_complex_triple_messages_kernel(
         ident = keep.tile([P, P], F32, name="ident")
         v_w = [keep.tile([P, S], U32, name=f"v_w{a}", align_bytes=64) for a in range(PASSES)]
         v_sc = [keep.tile([P, S], U8, name=f"v_sc{a}", align_bytes=64) for a in range(PASSES)]
-        b_sb = [keep.tile([P, H], F32, name=f"b_sb{j}") for j in range(TILES)]
-        minus_d_sb = [keep.tile([P, H], F32, name=f"minus_d_sb{j}") for j in range(TILES)]
+        b_planes = [keep.tile([P, H], F32, name=f"b_planes{j}") for j in range(TILES)]
+        minus_d_planes = [keep.tile([P, H], F32, name=f"minus_d_planes{j}") for j in range(TILES)]
         ab_planes = [keep.tile([P, H], F32, name=f"ab_planes{j}") for j in range(TILES)]
-        minus_cd_planes = b_sb
+        minus_cd_planes = b_planes
         quantised = {}
 
         def listed(lo, hi):
@@ -121,31 +120,20 @@ def tile_list_complex_triple_messages_kernel(
             nc.sync.dma_start(bias[:], b2.rearrange("(n p) -> p n", p=P))
         make_identity(nc, ident[:])
 
-        for a in range(PASSES):
-            for lo, hi in ((0, HALF), (HALF, S)) if a == 0 else ((0, S),):
-                nc.vector.tensor_copy(v_w[a][:, lo:hi], tab_w[a][:].bitcast(U32).indirect(listed(lo, hi)))
+        for a, lo, hi in ((0, 0, HALF), (0, HALF, S), (1, 0, S)):
+            nc.vector.tensor_copy(v_w[a][:, lo:hi], tab_w[a][:].bitcast(U32).indirect(listed(lo, hi)))
 
-        def interleave(copy, dst, src):
+        def round_rows(copy, dst, src):
             copy(dst.rearrange("p (c e) i -> p c i e", e=2), src.rearrange("p i (c e) -> p c i e", e=2))
 
-        def quantise(pool, name, grouped):
-            width = grouped.shape[1]
-            codes = pool.tile([P, width], U32, name=f"{name}_codes", align_bytes=64)
-            scales = pool.tile([P, width], U8, name=f"{name}_scales", align_bytes=64)
+        def quantise(codes, scales, grouped):
             nc.vector.quantize_mx(codes[:].bitcast(FP8X4), scales[:], grouped[:].rearrange("p c i -> p (c i)"))
+
+        def quantise_and_keep(name, grouped):
+            codes = keep.tile([P, grouped.shape[1]], U32, name=f"{name}_codes", align_bytes=64)
+            scales = keep.tile([P, grouped.shape[1]], U8, name=f"{name}_scales", align_bytes=64)
+            quantise(codes, scales, grouped)
             return codes, scales
-
-        def on_vector(dst, src):
-            interleave(nc.vector.tensor_copy, dst, src)
-
-        def on_scalar(dst, src):
-            interleave(nc.scalar.copy, dst, src)
-
-        def quantise_weight(name, a, shares, buffer):
-            grouped = keep.tile([P, rows[name, a].shape[2], PACK], BF16, name=buffer, align_bytes=64)
-            for rounder, lo, hi in shares:
-                rounder(grouped[:, lo:hi, :], rows[name, a][:, :, lo:hi])
-            quantised[name, a] = quantise(keep, f"{name}{a}", grouped)
 
         def product(name, j, passes=(0, 1)):
             acc = psum.tile([P, H], F32, name="bank")
@@ -178,72 +166,91 @@ def tile_list_complex_triple_messages_kernel(
         def copy_into_planes(planes, acc, scale):
             nc.scalar.activation(by_plane(planes), by_channel(acc), COPY, scale=scale)
 
-        quantise_weight("wa", 0, [(on_vector, 0, H // 2), (on_scalar, H // 2, H)], "grouped_a0")
-        quantise_weight("wa", 1, [(on_vector, 0, H)], "grouped_a1")
+        wa_grouped = [keep.tile([P, H, PACK], BF16, name=f"wa_grouped{a}", align_bytes=64) for a in range(PASSES)]
+        round_rows(nc.vector.tensor_copy, wa_grouped[0][:, 0 : H // 2, :], rows["wa", 0][:, :, 0 : H // 2])
+        round_rows(nc.scalar.copy, wa_grouped[0][:, H // 2 : H, :], rows["wa", 0][:, :, H // 2 : H])
+        quantised["wa", 0] = quantise_and_keep("wa0", wa_grouped[0])
+        round_rows(nc.vector.tensor_copy, wa_grouped[1][:], rows["wa", 1][:])
+        quantised["wa", 1] = quantise_and_keep("wa1", wa_grouped[1])
         for j in range(TILES):
-            copy_into_planes(b_sb[j], product("wb", j), 1.0)
+            copy_into_planes(b_planes[j], product("wb", j), 1.0)
         wc_grouped = keep.tile([P, PASSES * H, PACK], BF16, name="tab_w0", align_bytes=64)
-        on_vector(wc_grouped[:, 0:H, :], rows["wc", 0][:])
-        acc_a = {j: product("wa", j, (0, 1) if j < EARLY_A else (1, 0)) for j in range(TILES)}
-        for j in GPSIMD_AB_EARLY:
-            a_planes = ring.tile([P, H], F32, name="c_planes")
-            copy_into_planes(a_planes, acc_a[j], 1.0)
-            nc.gpsimd.tensor_tensor(ab_planes[j][:], a_planes[:], b_sb[j][:], MULT)
+        round_rows(nc.vector.tensor_copy, wc_grouped[:, 0:H, :], rows["wc", 0][:])
+        a_planes = keep.tile([P, GPSIMD_AB_TILES, H], F32, name="wc_codes", align_bytes=64)
         for j in range(TILES):
-            if j not in GPSIMD_AB_TILES:
-                multiply_into_planes(ab_planes[j], acc_a[j], b_sb[j])
-        on_scalar(wc_grouped[:, H : 2 * H, :], rows["wc", 1][:])
-        wc_codes, wc_scales = quantise(keep, "wc", wc_grouped)
+            acc = product("wa", j, (0, 1) if j < HALF_TILES else (1, 0))
+            if j < GPSIMD_AB_TILES:
+                copy_into_planes(a_planes[:, j, :], acc, 1.0)
+                nc.gpsimd.tensor_tensor(ab_planes[j][:], a_planes[:, j, :], b_planes[j][:], MULT)
+            else:
+                multiply_into_planes(ab_planes[j], acc, b_planes[j])
+        round_rows(nc.scalar.copy, wc_grouped[:, H : 2 * H, :], rows["wc", 1][:])
+        wc_codes, wc_scales = quantise_and_keep("wc", wc_grouped)
         for a in range(PASSES):
             quantised["wc", a] = (wc_codes[:, a * H : (a + 1) * H], wc_scales[:, a * H : (a + 1) * H])
-        late_ab = keep.tile([P, len(GPSIMD_AB_LATE), H], F32, name="tab_w0", align_bytes=64)
-        for n, j in enumerate(GPSIMD_AB_LATE):
-            a_planes = rows["wc", 1][:, n, :]
-            copy_into_planes(a_planes, acc_a[j], 1.0)
-            nc.gpsimd.tensor_tensor(late_ab[:, n, :], a_planes, b_sb[j][:], MULT)
-            ab_planes[j] = late_ab[:, n, :]
 
         def make_minus_d(j):
-            copy_into_planes(minus_d_sb[j], product("wd", j), -1.0)
+            copy_into_planes(minus_d_planes[j], product("wd", j), -1.0)
 
         def make_minus_cd(j):
             c_planes = ring.tile([P, H], F32, name="c_planes")
             copy_into_planes(c_planes, product("wc", j), 1.0)
-            nc.gpsimd.tensor_tensor(minus_cd_planes[j][:], c_planes[:], minus_d_sb[j][:], MULT)
+            nc.gpsimd.tensor_tensor(minus_cd_planes[j][:], c_planes[:], minus_d_planes[j][:], MULT)
 
-        pairs = [(0, 1), (2, 3), (4, 5), (6, 7)]
-        for j in pairs[0] + pairs[1]:
+        def difference(j):
+            bank = psum.tile([P, PACK, P], F32, name="bank")
+            for n, planes in enumerate((ab_planes[j], minus_cd_planes[j])):
+                for t in range(PACK):
+                    nc.tensor.matmul(
+                        bank[:, t, :],
+                        planes[:, t * P : (t + 1) * P],
+                        ident[:],
+                        start=(n == 0 and t == 0),
+                        stop=(n == 1 and t == PACK - 1),
+                        is_transpose=True,
+                    )
+            return bank
+
+        held = {}
+        for j in range(HALF_TILES):
             make_minus_d(j)
-        for n, pair in enumerate(pairs):
-            for j in pair:
-                make_minus_cd(j)
-            for j in pairs[n + 2] if n + 2 < len(pairs) else ():
-                make_minus_d(j)
+        for j in range(TILES):
+            make_minus_cd(j)
+            if j < HALF_TILES:
+                make_minus_d(j + HALF_TILES)
+            else:
+                held[j - HALF_TILES] = difference(j - HALF_TILES)
+        for j in range(HALF_TILES, TILES):
+            held[j] = difference(j)
 
         picked = keep.tile([P, PACK, S], F32, name="picked")
         for t in range(PACK):
             nc.vector.tensor_copy(picked[:, t, :], gates[t][:].indirect(listed(0, S)))
 
-        def difference(j):
-            bank = psum.tile([P, PACK, P], F32, name="bank")
-            for t in range(PACK):
-                plane = slice(t * P, (t + 1) * P)
-                nc.tensor.matmul(bank[:, t, :], ab_planes[j][:, plane], ident[:], start=True, stop=False, is_transpose=True)
-                nc.tensor.matmul(
-                    bank[:, t, :], minus_cd_planes[j][:, plane], ident[:], start=False, stop=True, is_transpose=True
-                )
-            return bank
+        def staged(shape, dtype):
+            return tail.tile(shape, dtype, name="staged", align_bytes=64)
 
-        held = {j: difference(j) for j in range(TILES)}
+        h_grouped = {}
 
-        def mix(lo, hi, grouped, vector_shares):
-            codes = tail.tile([P, hi - lo], U32, name="staged", align_bytes=64)
-            scales = ring.tile([P, hi - lo], U8, name="h_scales", align_bytes=64)
-            nc.vector.quantize_mx(codes[:].bitcast(FP8X4), scales[:], grouped.rearrange("p c t -> p (c t)"))
-            result = ring.tile([P, N // P, hi - lo], F32, name="result")
+        def weigh(j):
+            chunk, lo = divmod(j * P, CHUNK)
+            if lo == 0:
+                h_grouped[chunk] = staged([P, CHUNK, PACK], BF16)
+            nc.vector.tensor_tensor(
+                h_grouped[chunk][:, lo : lo + P, :].rearrange("p (c e) t -> p c t e", e=2),
+                held[j][:].rearrange("p t (c e) -> p c t e", e=2),
+                picked[:, :, j * P : (j + 1) * P].rearrange("p t (c e) -> p c t e", e=2),
+                MULT,
+            )
+
+        def finish(chunk):
+            codes = staged([P, CHUNK], U32)
+            scales = ring.tile([P, CHUNK], U8, name="h_scales", align_bytes=64)
+            quantise(codes, scales, h_grouped[chunk])
+            result = ring.tile([P, N // P, CHUNK], F32, name="result")
             for n in range(N // P):
                 cols = slice(n * P, (n + 1) * P)
-                y = psum.tile([P, hi - lo], F32, name="bank")
+                y = psum.tile([P, CHUNK], F32, name="bank")
                 nc.tensor.matmul_mx(
                     y[:],
                     lhsT=w2_codes[:, cols].bitcast(FP8X4),
@@ -253,37 +260,25 @@ def tile_list_complex_triple_messages_kernel(
                     start=True,
                     stop=True,
                 )
-                if vector_shares and n == 1:
+                if chunk == CHUNKS - 1 and n == 1:
                     nc.vector.tensor_scalar(result[:, n, :], y[:], bias[:, n : n + 1], None, op0=ADD)
                 else:
                     nc.scalar.activation(result[:, n, :], y[:], IDENTITY, bias=bias[:, n : n + 1])
-                if lo == 0:
-                    nc.sync.dma_start(out[cols, lo:hi], result[:, n, :])
-            if lo > 0:
-                nc.sync.dma_start(out[:, lo:hi].rearrange("(n p) j -> p n j", p=P), result[:])
-
-        def weigh(grouped, lo, j):
-            nc.vector.tensor_tensor(
-                grouped[:, j * P - lo : (j + 1) * P - lo, :].rearrange("p (c e) t -> p c t e", e=2),
-                held[j][:].rearrange("p t (c e) -> p c t e", e=2),
-                picked[:, :, j * P : (j + 1) * P].rearrange("p t (c e) -> p c t e", e=2),
-                MULT,
+            nc.sync.dma_start(
+                out[:, chunk * CHUNK : (chunk + 1) * CHUNK].rearrange("(n p) j -> p n j", p=P), result[:]
             )
 
-        first = tail.tile([P, 512, PACK], BF16, name="staged", align_bytes=64)
-        for j in range(4):
-            weigh(first, 0, j)
-        second = tail.tile([P, 256, PACK], BF16, name="staged", align_bytes=64)
-        weigh(second, 512, 4)
-        w2_grouped = keep.tile([P, N, PACK], BF16, name="grouped_a0", align_bytes=64)
-        on_scalar(w2_grouped[:], rows["w2", 0][:])
-        w2_codes = tail.tile([P, N], U32, name="staged", align_bytes=64)
+        for j in range(HALF_TILES + 1):
+            weigh(j)
+        w2_grouped = keep.tile([P, N, PACK], BF16, name="wa_grouped0", align_bytes=64)
+        round_rows(nc.scalar.copy, w2_grouped[:], rows["w2", 0][:])
+        w2_codes = staged([P, N], U32)
         w2_scales = keep.tile([P, N], U8, name="w2_scales", align_bytes=64)
-        nc.vector.quantize_mx(w2_codes[:].bitcast(FP8X4), w2_scales[:], w2_grouped[:].rearrange("p c i -> p (c i)"))
-        mix(0, 512, first[:], False)
-        weigh(second, 512, 5)
-        third = tail.tile([P, 256, PACK], BF16, name="staged", align_bytes=64)
-        weigh(third, 768, 6)
-        mix(512, 768, second[:], False)
-        weigh(third, 768, 7)
-        mix(768, S, third[:], True)
+        quantise(w2_codes, w2_scales, w2_grouped)
+        finish(0)
+        finish(1)
+        weigh(TILES - 3)
+        weigh(TILES - 2)
+        finish(2)
+        weigh(TILES - 1)
+        finish(3)

@@ -31,6 +31,8 @@ PER_COLUMN = 16
 PASS_SHIFT = QUADRANT // PASSES
 
 HALF = S // 2
+FIRST = 3 * P
+EARLY_A_TILES = 6
 HALF_TILES = TILES // 2
 CHUNK = 2 * P
 CHUNKS = S // CHUNK
@@ -73,12 +75,10 @@ def tile_list_complex_triple_messages_kernel(
         def listed(lo, hi):
             return offsets[:, lo // PER_COLUMN : hi // PER_COLUMN]
 
-        def load_fp4_scales(name, src, quadrants):
-            for q in quadrants:
-                nc.sync.dma_start(
-                    fp4_sc[name][QUADRANT * q : QUADRANT * q + SCALE_ROWS],
-                    src[:, SCALE_ROWS * q : SCALE_ROWS * (q + 1), :].rearrange("a s c -> s a c").bitcast(I32),
-                )
+        def load_fp4_scales(name, src, which):
+            by_row = src.rearrange("a (q s) c -> s q a c", s=SCALE_ROWS)
+            for s in which:
+                nc.sync.dma_start(fp4_sc[name][s:P:QUADRANT], by_row[s].bitcast(I32))
 
         def load_table_scales():
             by_row = tab_scales.rearrange("a (q s) c -> s q a c", s=SCALE_ROWS)
@@ -120,7 +120,7 @@ def tile_list_complex_triple_messages_kernel(
             nc.sync.dma_start(bias[:], b2.rearrange("(n p) -> p n", p=P))
         make_identity(nc, ident[:])
 
-        for a, lo, hi in ((0, 0, HALF), (0, HALF, S), (1, 0, S)):
+        for a, lo, hi in ((0, 0, FIRST), (0, FIRST, S), (1, 0, S)):
             nc.vector.tensor_copy(v_w[a][:, lo:hi], tab_w[a][:].bitcast(U32).indirect(listed(lo, hi)))
 
         def round_rows(copy, dst, src):
@@ -167,8 +167,8 @@ def tile_list_complex_triple_messages_kernel(
             nc.scalar.activation(by_plane(planes), by_channel(acc), COPY, scale=scale)
 
         wa_grouped = [keep.tile([P, H, PACK], BF16, name=f"wa_grouped{a}", align_bytes=64) for a in range(PASSES)]
-        round_rows(nc.vector.tensor_copy, wa_grouped[0][:, 0 : H // 2, :], rows["wa", 0][:, :, 0 : H // 2])
-        round_rows(nc.scalar.copy, wa_grouped[0][:, H // 2 : H, :], rows["wa", 0][:, :, H // 2 : H])
+        round_rows(nc.vector.tensor_copy, wa_grouped[0][:, H // 4 : H, :], rows["wa", 0][:, :, H // 4 : H])
+        round_rows(nc.scalar.copy, wa_grouped[0][:, 0 : H // 4, :], rows["wa", 0][:, :, 0 : H // 4])
         quantised["wa", 0] = quantise_and_keep("wa0", wa_grouped[0])
         round_rows(nc.vector.tensor_copy, wa_grouped[1][:], rows["wa", 1][:])
         quantised["wa", 1] = quantise_and_keep("wa1", wa_grouped[1])
@@ -176,56 +176,70 @@ def tile_list_complex_triple_messages_kernel(
             copy_into_planes(b_planes[j], product("wb", j), 1.0)
         wc_grouped = keep.tile([P, PASSES * H, PACK], BF16, name="tab_w0", align_bytes=64)
         round_rows(nc.vector.tensor_copy, wc_grouped[:, 0:H, :], rows["wc", 0][:])
-        a_planes = keep.tile([P, GPSIMD_AB_TILES, H], F32, name="wc_codes", align_bytes=64)
+        a_planes = keep.tile([P, GPSIMD_AB_TILES, H], F32, name="wc0_codes", align_bytes=64)
         for j in range(TILES):
-            acc = product("wa", j, (0, 1) if j < HALF_TILES else (1, 0))
+            acc = product("wa", j, (0, 1) if j < EARLY_A_TILES else (1, 0))
             if j < GPSIMD_AB_TILES:
                 copy_into_planes(a_planes[:, j, :], acc, 1.0)
                 nc.gpsimd.tensor_tensor(ab_planes[j][:], a_planes[:, j, :], b_planes[j][:], MULT)
             else:
                 multiply_into_planes(ab_planes[j], acc, b_planes[j])
         round_rows(nc.scalar.copy, wc_grouped[:, H : 2 * H, :], rows["wc", 1][:])
-        wc_codes, wc_scales = quantise_and_keep("wc", wc_grouped)
         for a in range(PASSES):
-            quantised["wc", a] = (wc_codes[:, a * H : (a + 1) * H], wc_scales[:, a * H : (a + 1) * H])
+            quantised["wc", a] = quantise_and_keep(f"wc{a}", wc_grouped[:, a * H : (a + 1) * H, :])
 
         def make_minus_d(j):
             copy_into_planes(minus_d_planes[j], product("wd", j), -1.0)
 
         def make_minus_cd(j):
-            c_planes = ring.tile([P, H], F32, name="c_planes")
+            c_planes = ring.tile([P, H], F32, name="c_planes", bufs=6)
             copy_into_planes(c_planes, product("wc", j), 1.0)
             nc.gpsimd.tensor_tensor(minus_cd_planes[j][:], c_planes[:], minus_d_planes[j][:], MULT)
 
-        def difference(j):
-            bank = psum.tile([P, PACK, P], F32, name="bank")
-            for n, planes in enumerate((ab_planes[j], minus_cd_planes[j])):
-                for t in range(PACK):
-                    nc.tensor.matmul(
-                        bank[:, t, :],
-                        planes[:, t * P : (t + 1) * P],
-                        ident[:],
-                        start=(n == 0 and t == 0),
-                        stop=(n == 1 and t == PACK - 1),
-                        is_transpose=True,
-                    )
-            return bank
-
         held = {}
-        for j in range(HALF_TILES):
+
+        def turn(j, planes, first):
+            if first:
+                held[j] = psum.tile([P, PACK, P], F32, name="bank")
+            for t in range(PACK):
+                nc.tensor.matmul(
+                    held[j][:, t, :],
+                    planes[j][:, t * P : (t + 1) * P],
+                    ident[:],
+                    start=(first and t == 0),
+                    stop=(not first and t == PACK - 1),
+                    is_transpose=True,
+                )
+
+        def turn_ab(tiles):
+            for j in tiles:
+                turn(j, ab_planes, True)
+
+        def turn_cd(tiles):
+            for j in tiles:
+                turn(j, minus_cd_planes, False)
+
+        order = (2, 3, 0, 1, 4, 5, 6, 7)
+        turn_ab(order[0:2])
+        for j in order[0:HALF_TILES]:
             make_minus_d(j)
-        for j in range(TILES):
-            make_minus_cd(j)
-            if j < HALF_TILES:
-                make_minus_d(j + HALF_TILES)
-            else:
-                held[j - HALF_TILES] = difference(j - HALF_TILES)
-        for j in range(HALF_TILES, TILES):
-            held[j] = difference(j)
+        for n in range(TILES - 1):
+            make_minus_cd(order[n])
+            if n < HALF_TILES:
+                make_minus_d(order[n + HALF_TILES])
+        turn_cd(order[0:2])
+        turn_ab(order[2:3])
+        turn_cd(order[2:3])
+        make_minus_cd(order[7])
+        for n in (3, 4):
+            turn_ab(order[n : n + 1])
+            turn_cd(order[n : n + 1])
+        turn_ab(order[5:8])
+        turn_cd(order[5:8])
 
         picked = keep.tile([P, PACK, S], F32, name="picked")
-        for t in range(PACK):
-            nc.vector.tensor_copy(picked[:, t, :], gates[t][:].indirect(listed(0, S)))
+        for t, lo, hi in ((0, 0, S), (1, 0, S), (2, 0, S), (3, 0, HALF), (3, HALF, S)):
+            nc.vector.tensor_copy(picked[:, t, lo:hi], gates[t][:].indirect(listed(lo, hi)))
 
         def staged(shape, dtype):
             return tail.tile(shape, dtype, name="staged", align_bytes=64)
@@ -268,15 +282,15 @@ def tile_list_complex_triple_messages_kernel(
                 out[:, chunk * CHUNK : (chunk + 1) * CHUNK].rearrange("(n p) j -> p n j", p=P), result[:]
             )
 
-        for j in range(HALF_TILES + 1):
+        for j in order[0 : HALF_TILES + 1]:
             weigh(j)
         w2_grouped = keep.tile([P, N, PACK], BF16, name="wa_grouped0", align_bytes=64)
         round_rows(nc.scalar.copy, w2_grouped[:], rows["w2", 0][:])
         w2_codes = staged([P, N], U32)
         w2_scales = keep.tile([P, N], U8, name="w2_scales", align_bytes=64)
         quantise(w2_codes, w2_scales, w2_grouped)
-        finish(0)
         finish(1)
+        finish(0)
         weigh(TILES - 3)
         weigh(TILES - 2)
         finish(2)

@@ -31,8 +31,10 @@ PER_COLUMN = 16
 PASS_SHIFT = QUADRANT // PASSES
 
 HALF = S // 2
+HALVES = (slice(0, H // 2), slice(H // 2, H))
 FIRST = 3 * P
 EARLY_A_TILES = 6
+LATE_AB_TILES = 2
 HALF_TILES = TILES // 2
 CHUNK = 2 * P
 CHUNKS = S // CHUNK
@@ -66,10 +68,10 @@ def tile_list_complex_triple_messages_kernel(
         ident = keep.tile([P, P], F32, name="ident")
         v_w = [keep.tile([P, S], U32, name=f"v_w{a}", align_bytes=64) for a in range(PASSES)]
         v_sc = [keep.tile([P, S], U8, name=f"v_sc{a}", align_bytes=64) for a in range(PASSES)]
-        b_planes = [keep.tile([P, H], F32, name=f"b_planes{j}") for j in range(TILES)]
+        b_planes = [keep.tile([P, H], F32, name=("tab_w1" if j == 3 else f"b_planes{j}"), align_bytes=64) for j in range(TILES)]
         minus_d_planes = [keep.tile([P, H], F32, name=f"minus_d_planes{j}") for j in range(TILES)]
-        ab_planes = [keep.tile([P, H], F32, name=f"ab_planes{j}") for j in range(TILES)]
-        minus_cd_planes = b_planes
+        ab_planes = [keep.tile([P, H], F32, name=f"ab_planes{j}") for j in range(TILES - LATE_AB_TILES)]
+        minus_cd_planes = b_planes[0:3] + [keep.tile([P, H], F32, name="cd3")] + b_planes[4:]
         quantised = {}
 
         def listed(lo, hi):
@@ -120,7 +122,7 @@ def tile_list_complex_triple_messages_kernel(
             nc.sync.dma_start(bias[:], b2.rearrange("(n p) -> p n", p=P))
         make_identity(nc, ident[:])
 
-        for a, lo, hi in ((0, 0, FIRST), (0, FIRST, S), (1, 0, S)):
+        for a, lo, hi in ((0, 0, FIRST), (0, FIRST, S), (1, 0, HALF), (1, HALF, S)):
             nc.vector.tensor_copy(v_w[a][:, lo:hi], tab_w[a][:].bitcast(U32).indirect(listed(lo, hi)))
 
         def round_rows(copy, dst, src):
@@ -130,9 +132,16 @@ def tile_list_complex_triple_messages_kernel(
             nc.vector.quantize_mx(codes[:].bitcast(FP8X4), scales[:], grouped[:].rearrange("p c i -> p (c i)"))
 
         def quantise_and_keep(name, grouped):
-            codes = keep.tile([P, grouped.shape[1]], U32, name=f"{name}_codes", align_bytes=64)
+            codes = keep.tile([P, grouped.shape[1]], U32, name=("tab_w1" if name == "wc0" else f"{name}_codes"), align_bytes=64)
             scales = keep.tile([P, grouped.shape[1]], U8, name=f"{name}_scales", align_bytes=64)
             quantise(codes, scales, grouped)
+            return codes, scales
+
+        def quantise_in_halves(name, grouped):
+            codes = keep.tile([P, H], U32, name=f"{name}_codes", align_bytes=64)
+            scales = keep.tile([P, H], U8, name=f"{name}_scales", align_bytes=64)
+            for half in HALVES:
+                quantise(codes[:, half], scales[:, half], grouped[:, half, :])
             return codes, scales
 
         def product(name, j, passes=(0, 1)):
@@ -167,26 +176,37 @@ def tile_list_complex_triple_messages_kernel(
             nc.scalar.activation(by_plane(planes), by_channel(acc), COPY, scale=scale)
 
         wa_grouped = [keep.tile([P, H, PACK], BF16, name=f"wa_grouped{a}", align_bytes=64) for a in range(PASSES)]
-        round_rows(nc.vector.tensor_copy, wa_grouped[0][:, H // 4 : H, :], rows["wa", 0][:, :, H // 4 : H])
-        round_rows(nc.scalar.copy, wa_grouped[0][:, 0 : H // 4, :], rows["wa", 0][:, :, 0 : H // 4])
+        round_rows(nc.vector.tensor_copy, wa_grouped[0][:, H // 2 : H, :], rows["wa", 0][:, :, H // 2 : H])
+        round_rows(nc.scalar.copy, wa_grouped[0][:, 0 : H // 2, :], rows["wa", 0][:, :, 0 : H // 2])
         quantised["wa", 0] = quantise_and_keep("wa0", wa_grouped[0])
-        round_rows(nc.vector.tensor_copy, wa_grouped[1][:], rows["wa", 1][:])
-        quantised["wa", 1] = quantise_and_keep("wa1", wa_grouped[1])
+        for half in HALVES:
+            round_rows(nc.vector.tensor_copy, wa_grouped[1][:, half, :], rows["wa", 1][:, :, half])
+        quantised["wa", 1] = quantise_in_halves("wa1", wa_grouped[1])
         for j in range(TILES):
             copy_into_planes(b_planes[j], product("wb", j), 1.0)
         wc_grouped = keep.tile([P, PASSES * H, PACK], BF16, name="tab_w0", align_bytes=64)
         round_rows(nc.vector.tensor_copy, wc_grouped[:, 0:H, :], rows["wc", 0][:])
-        a_planes = keep.tile([P, GPSIMD_AB_TILES, H], F32, name="wc0_codes", align_bytes=64)
+        a_planes = keep.tile([P, GPSIMD_AB_TILES, H], F32, name="a_planes", align_bytes=64)
+        late_a = {}
         for j in range(TILES):
             acc = product("wa", j, (0, 1) if j < EARLY_A_TILES else (1, 0))
             if j < GPSIMD_AB_TILES:
                 copy_into_planes(a_planes[:, j, :], acc, 1.0)
                 nc.gpsimd.tensor_tensor(ab_planes[j][:], a_planes[:, j, :], b_planes[j][:], MULT)
-            else:
+            elif j < TILES - LATE_AB_TILES:
                 multiply_into_planes(ab_planes[j], acc, b_planes[j])
+            else:
+                late_a[j] = acc
         round_rows(nc.scalar.copy, wc_grouped[:, H : 2 * H, :], rows["wc", 1][:])
         for a in range(PASSES):
             quantised["wc", a] = quantise_and_keep(f"wc{a}", wc_grouped[:, a * H : (a + 1) * H, :])
+
+        late_a_planes = keep.tile([P, LATE_AB_TILES, H], F32, name="wc_rows1")
+        late_ab_planes = keep.tile([P, LATE_AB_TILES, H], F32, name="tab_w0", align_bytes=64)
+        for n, j in enumerate(late_a):
+            copy_into_planes(late_a_planes[:, n, :], late_a[j], 1.0)
+            ab_planes.append(late_ab_planes[:, n, :])
+            nc.gpsimd.tensor_tensor(ab_planes[j], late_a_planes[:, n, :], b_planes[j][:], MULT)
 
         def make_minus_d(j):
             copy_into_planes(minus_d_planes[j], product("wd", j), -1.0)
@@ -219,23 +239,39 @@ def tile_list_complex_triple_messages_kernel(
             for j in tiles:
                 turn(j, minus_cd_planes, False)
 
-        order = (2, 3, 0, 1, 4, 5, 6, 7)
-        turn_ab(order[0:2])
-        for j in order[0:HALF_TILES]:
-            make_minus_d(j)
-        for n in range(TILES - 1):
-            make_minus_cd(order[n])
-            if n < HALF_TILES:
-                make_minus_d(order[n + HALF_TILES])
-        turn_cd(order[0:2])
-        turn_ab(order[2:3])
-        turn_cd(order[2:3])
-        make_minus_cd(order[7])
-        for n in (3, 4):
-            turn_ab(order[n : n + 1])
-            turn_cd(order[n : n + 1])
-        turn_ab(order[5:8])
-        turn_cd(order[5:8])
+        order = (2, 3, 4, 5, 0, 1, 6, 7)
+        turn_ab((2,))
+        turn_ab((3,))
+        make_minus_d(2)
+        make_minus_d(3)
+        turn_ab((4,))
+        turn_ab((5,))
+        make_minus_cd(2)
+        make_minus_d(4)
+        make_minus_cd(3)
+        make_minus_d(5)
+        make_minus_cd(4)
+        make_minus_d(0)
+        make_minus_cd(5)
+        make_minus_d(1)
+        make_minus_cd(0)
+        make_minus_d(6)
+        make_minus_cd(1)
+        make_minus_d(7)
+        make_minus_cd(6)
+        turn_cd((2,))
+        turn_cd((3,))
+        turn_cd((4,))
+        make_minus_cd(7)
+        turn_cd((5,))
+        turn_ab((0,))
+        turn_cd((0,))
+        turn_ab((1,))
+        turn_cd((1,))
+        turn_ab((6,))
+        turn_ab((7,))
+        turn_cd((6,))
+        turn_cd((7,))
 
         picked = keep.tile([P, PACK, S], F32, name="picked")
         for t, lo, hi in ((0, 0, S), (1, 0, S), (2, 0, S), (3, 0, HALF), (3, HALF, S)):
@@ -289,10 +325,10 @@ def tile_list_complex_triple_messages_kernel(
         w2_codes = staged([P, N], U32)
         w2_scales = keep.tile([P, N], U8, name="w2_scales", align_bytes=64)
         quantise(w2_codes, w2_scales, w2_grouped)
-        finish(1)
-        finish(0)
-        weigh(TILES - 3)
-        weigh(TILES - 2)
-        finish(2)
-        weigh(TILES - 1)
-        finish(3)
+        finish(order[0] // 2)
+        finish(order[2] // 2)
+        weigh(order[5])
+        weigh(order[6])
+        finish(order[4] // 2)
+        weigh(order[7])
+        finish(order[6] // 2)

@@ -34,7 +34,7 @@ HALF = S // 2
 HALVES = (slice(0, H // 2), slice(H // 2, H))
 FIRST = 3 * P
 EARLY_A_TILES = 6
-LATE_AB_TILES = 2
+LATE_AB_TILES = 1
 HALF_TILES = TILES // 2
 CHUNK = 2 * P
 CHUNKS = S // CHUNK
@@ -42,7 +42,7 @@ CHUNKS = S // CHUNK
 GPSIMD_AB_TILES = 2
 
 RING = 4
-STAGED = 6
+STAGED = 1
 BANKS = 8
 
 
@@ -68,10 +68,16 @@ def tile_list_complex_triple_messages_kernel(
         ident = keep.tile([P, P], F32, name="ident")
         v_w = [keep.tile([P, S], U32, name=f"v_w{a}", align_bytes=64) for a in range(PASSES)]
         v_sc = [keep.tile([P, S], U8, name=f"v_sc{a}", align_bytes=64) for a in range(PASSES)]
-        b_planes = [keep.tile([P, H], F32, name=("tab_w1" if j == 3 else f"b_planes{j}"), align_bytes=64) for j in range(TILES)]
-        minus_d_planes = [keep.tile([P, H], F32, name=f"minus_d_planes{j}") for j in range(TILES)]
-        ab_planes = [keep.tile([P, H], F32, name=f"ab_planes{j}") for j in range(TILES - LATE_AB_TILES)]
-        minus_cd_planes = b_planes[0:3] + [keep.tile([P, H], F32, name="cd3")] + b_planes[4:]
+        b_pairs = [keep.tile([P, 2, H], F32, name=("tab_w1" if n == 1 else f"b_planes{n}"), align_bytes=64) for n in range(4)]
+        d_pairs = [keep.tile([P, 2, H], F32, name=f"minus_d_planes{n}") for n in range(4)]
+        c_pairs = [keep.tile([P, 2, H], F32, name=f"c_planes{n}") for n in range(4)]
+        ab_pairs = [keep.tile([P, 2, H], F32, name=f"ab_planes{n}") for n in range(4)]
+        cd_pairs = [b_pairs[0], keep.tile([P, 2, H], F32, name="cd1"), b_pairs[2], b_pairs[3]]
+        b_planes = [b_pairs[j // 2][:, j % 2, :] for j in range(TILES)]
+        minus_d_planes = [d_pairs[j // 2][:, j % 2, :] for j in range(TILES)]
+        c_planes = [c_pairs[j // 2][:, j % 2, :] for j in range(TILES)]
+        ab_planes = [ab_pairs[j // 2][:, j % 2, :] for j in range(TILES - LATE_AB_TILES)]
+        minus_cd_planes = [cd_pairs[j // 2][:, j % 2, :] for j in range(TILES)]
         quantised = {}
 
         def listed(lo, hi):
@@ -212,9 +218,14 @@ def tile_list_complex_triple_messages_kernel(
             copy_into_planes(minus_d_planes[j], product("wd", j), -1.0)
 
         def make_minus_cd(j):
-            c_planes = ring.tile([P, H], F32, name="c_planes", bufs=6)
-            copy_into_planes(c_planes, product("wc", j), 1.0)
-            nc.gpsimd.tensor_tensor(minus_cd_planes[j][:], c_planes[:], minus_d_planes[j][:], MULT)
+            copy_into_planes(c_planes[j], product("wc", j), 1.0)
+            nc.gpsimd.tensor_tensor(minus_cd_planes[j][:], c_planes[j][:], minus_d_planes[j][:], MULT)
+
+        def make_c(j):
+            copy_into_planes(c_planes[j], product("wc", j), 1.0)
+
+        def make_pair(n):
+            nc.gpsimd.tensor_tensor(cd_pairs[n][:], c_pairs[n][:], d_pairs[n][:], MULT)
 
         held = {}
 
@@ -239,7 +250,7 @@ def tile_list_complex_triple_messages_kernel(
             for j in tiles:
                 turn(j, minus_cd_planes, False)
 
-        order = (2, 3, 4, 5, 0, 1, 6, 7)
+        c_banks = {}
         turn_ab((2,))
         turn_ab((3,))
         make_minus_d(2)
@@ -277,15 +288,18 @@ def tile_list_complex_triple_messages_kernel(
         for t, lo, hi in ((0, 0, S), (1, 0, S), (2, 0, S), (3, 0, HALF), (3, HALF, S)):
             nc.vector.tensor_copy(picked[:, t, lo:hi], gates[t][:].indirect(listed(lo, hi)))
 
-        def staged(shape, dtype):
-            return tail.tile(shape, dtype, name="staged", align_bytes=64)
 
+        def staged(shape, dtype):
+            return tail.tile(shape, dtype, name="staged", align_bytes=64, bufs=9)
+
+        chunks = [(0, 2), (2, 4), (4, 6), (6, 7), (7, 8)]
         h_grouped = {}
 
         def weigh(j):
-            chunk, lo = divmod(j * P, CHUNK)
-            if lo == 0:
-                h_grouped[chunk] = staged([P, CHUNK, PACK], BF16)
+            chunk = [c for c in chunks if c[0] <= j < c[1]][0]
+            if chunk not in h_grouped:
+                h_grouped[chunk] = staged([P, (chunk[1] - chunk[0]) * P, PACK], BF16)
+            lo = (j - chunk[0]) * P
             nc.vector.tensor_tensor(
                 h_grouped[chunk][:, lo : lo + P, :].rearrange("p (c e) t -> p c t e", e=2),
                 held[j][:].rearrange("p t (c e) -> p c t e", e=2),
@@ -293,14 +307,16 @@ def tile_list_complex_triple_messages_kernel(
                 MULT,
             )
 
-        def finish(chunk):
-            codes = staged([P, CHUNK], U32)
-            scales = ring.tile([P, CHUNK], U8, name="h_scales", align_bytes=64)
+        def finish(index, engines):
+            chunk = chunks[index]
+            width = (chunk[1] - chunk[0]) * P
+            codes = staged([P, width], U32)
+            scales = tail.tile([P, width], U8, name="h_scales", align_bytes=64, bufs=5)
             quantise(codes, scales, h_grouped[chunk])
-            result = ring.tile([P, N // P, CHUNK], F32, name="result")
+            result = tail.tile([P, N // P, width], F32, name="result", bufs=5)
             for n in range(N // P):
                 cols = slice(n * P, (n + 1) * P)
-                y = psum.tile([P, CHUNK], F32, name="bank")
+                y = psum.tile([P, width], F32, name="bank")
                 nc.tensor.matmul_mx(
                     y[:],
                     lhsT=w2_codes[:, cols].bitcast(FP8X4),
@@ -310,25 +326,29 @@ def tile_list_complex_triple_messages_kernel(
                     start=True,
                     stop=True,
                 )
-                if chunk == CHUNKS - 1 and n == 1:
+                if engines[n] == "V":
                     nc.vector.tensor_scalar(result[:, n, :], y[:], bias[:, n : n + 1], None, op0=ADD)
                 else:
                     nc.scalar.activation(result[:, n, :], y[:], IDENTITY, bias=bias[:, n : n + 1])
             nc.sync.dma_start(
-                out[:, chunk * CHUNK : (chunk + 1) * CHUNK].rearrange("(n p) j -> p n j", p=P), result[:]
+                out[:, chunk[0] * P : chunk[1] * P].rearrange("(n p) j -> p n j", p=P), result[:]
             )
 
-        for j in order[0 : HALF_TILES + 1]:
-            weigh(j)
+        weigh(2)
+        weigh(3)
+        weigh(4)
+        weigh(5)
+        weigh(0)
         w2_grouped = keep.tile([P, N, PACK], BF16, name="wa_grouped0", align_bytes=64)
         round_rows(nc.scalar.copy, w2_grouped[:], rows["w2", 0][:])
         w2_codes = staged([P, N], U32)
         w2_scales = keep.tile([P, N], U8, name="w2_scales", align_bytes=64)
         quantise(w2_codes, w2_scales, w2_grouped)
-        finish(order[0] // 2)
-        finish(order[2] // 2)
-        weigh(order[5])
-        weigh(order[6])
-        finish(order[4] // 2)
-        weigh(order[7])
-        finish(order[6] // 2)
+        finish(1, "SS")
+        finish(2, "SS")
+        weigh(1)
+        weigh(6)
+        finish(0, "SS")
+        weigh(7)
+        finish(3, "SS")
+        finish(4, "SV")

@@ -30,20 +30,22 @@ PER_COLUMN = 16
 
 PASS_SHIFT = QUADRANT // PASSES
 
-HALF = S // 2
-HALVES = (slice(0, H // 2), slice(H // 2, H))
-FIRST = 3 * P
+LIST_HALVES = ((0, S // 2), (S // 2, S))
+FIRST_GATHER = 3 * P
+COLUMN_HALVES = (slice(0, H // 2), slice(H // 2, H))
+
+GPSIMD_FIRST = (0, 1)
+GPSIMD_LAST = TILES - 1
+TURNED_EARLY = (2, 3, 4, 5)
+ORDER = TURNED_EARLY + GPSIMD_FIRST + (TILES - 2, GPSIMD_LAST)
 EARLY_A_TILES = 6
-LATE_AB_TILES = 1
-HALF_TILES = TILES // 2
-CHUNK = 2 * P
-CHUNKS = S // CHUNK
+D_AHEAD = 2
 
-GPSIMD_AB_TILES = 2
+CHUNKS = (ORDER[0:2], ORDER[2:4], ORDER[4:6], ORDER[6:7], ORDER[7:8])
+WEIGHED_FIRST = 5
 
-RING = 4
-STAGED = 1
 BANKS = 8
+STAGED = 2 * len(CHUNKS) + 1
 
 
 def tile_list_complex_triple_messages_kernel(
@@ -52,8 +54,7 @@ def tile_list_complex_triple_messages_kernel(
     nc = tc.nc
     with ExitStack() as ctx:
         keep = ctx.enter_context(tc.tile_pool(name="keep", bufs=1))
-        ring = ctx.enter_context(tc.tile_pool(name="ring", bufs=RING))
-        tail = ctx.enter_context(tc.tile_pool(name="tail", bufs=STAGED))
+        tail = ctx.enter_context(tc.tile_pool(name="tail", bufs=len(CHUNKS)))
         psum = ctx.enter_context(tc.psum_pool(name="psum", bufs=BANKS))
 
         offsets = keep.tile([P, S // PER_COLUMN], U16, name="offsets")
@@ -68,16 +69,17 @@ def tile_list_complex_triple_messages_kernel(
         ident = keep.tile([P, P], F32, name="ident")
         v_w = [keep.tile([P, S], U32, name=f"v_w{a}", align_bytes=64) for a in range(PASSES)]
         v_sc = [keep.tile([P, S], U8, name=f"v_sc{a}", align_bytes=64) for a in range(PASSES)]
-        b_pairs = [keep.tile([P, 2, H], F32, name=("tab_w1" if n == 1 else f"b_planes{n}"), align_bytes=64) for n in range(4)]
-        d_pairs = [keep.tile([P, 2, H], F32, name=f"minus_d_planes{n}") for n in range(4)]
-        c_pairs = [keep.tile([P, 2, H], F32, name=f"c_planes{n}") for n in range(4)]
-        ab_pairs = [keep.tile([P, 2, H], F32, name=f"ab_planes{n}") for n in range(4)]
-        cd_pairs = [b_pairs[0], keep.tile([P, 2, H], F32, name="cd1"), b_pairs[2], b_pairs[3]]
+        b_pairs = [
+            keep.tile([P, 2, H], F32, name=("tab_w1" if n == 1 else f"b_planes{n}"), align_bytes=64)
+            for n in range(TILES // 2)
+        ]
         b_planes = [b_pairs[j // 2][:, j % 2, :] for j in range(TILES)]
-        minus_d_planes = [d_pairs[j // 2][:, j % 2, :] for j in range(TILES)]
-        c_planes = [c_pairs[j // 2][:, j % 2, :] for j in range(TILES)]
-        ab_planes = [ab_pairs[j // 2][:, j % 2, :] for j in range(TILES - LATE_AB_TILES)]
-        minus_cd_planes = [cd_pairs[j // 2][:, j % 2, :] for j in range(TILES)]
+        minus_d_planes = [keep.tile([P, H], F32, name=f"minus_d_planes{j}") for j in range(TILES)]
+        c_planes = [keep.tile([P, H], F32, name=f"c_planes{j}") for j in range(TILES)]
+        ab_planes = [keep.tile([P, H], F32, name=f"ab_planes{j}") for j in range(GPSIMD_LAST)]
+        minus_cd_planes = [
+            keep.tile([P, H], F32, name=f"minus_cd_planes{j}") if j // 2 == 1 else b_planes[j] for j in range(TILES)
+        ]
         quantised = {}
 
         def listed(lo, hi):
@@ -105,7 +107,7 @@ def tile_list_complex_triple_messages_kernel(
         def load_gate(t):
             nc.sync.dma_start(gates[t][:], gT.rearrange("(p t) c -> t p c", t=PACK)[t])
 
-        nc.gpsimd.memset(tab_sc[:], 0)
+        nc.vector.memset(tab_sc[:], 0)
         nc.sync.dma_start(offsets[:], offs)
         load_fp4_words("wb", wb_words)
         load_fp4_scales("wb", wb_scales, (0,))
@@ -128,8 +130,9 @@ def tile_list_complex_triple_messages_kernel(
             nc.sync.dma_start(bias[:], b2.rearrange("(n p) -> p n", p=P))
         make_identity(nc, ident[:])
 
-        for a, lo, hi in ((0, 0, FIRST), (0, FIRST, S), (1, 0, HALF), (1, HALF, S)):
-            nc.vector.tensor_copy(v_w[a][:, lo:hi], tab_w[a][:].bitcast(U32).indirect(listed(lo, hi)))
+        for a, pieces in enumerate((((0, FIRST_GATHER), (FIRST_GATHER, S)), LIST_HALVES)):
+            for lo, hi in pieces:
+                nc.vector.tensor_copy(v_w[a][:, lo:hi], tab_w[a][:].bitcast(U32).indirect(listed(lo, hi)))
 
         def round_rows(copy, dst, src):
             copy(dst.rearrange("p (c e) i -> p c i e", e=2), src.rearrange("p i (c e) -> p c i e", e=2))
@@ -137,17 +140,12 @@ def tile_list_complex_triple_messages_kernel(
         def quantise(codes, scales, grouped):
             nc.vector.quantize_mx(codes[:].bitcast(FP8X4), scales[:], grouped[:].rearrange("p c i -> p (c i)"))
 
-        def quantise_and_keep(name, grouped):
-            codes = keep.tile([P, grouped.shape[1]], U32, name=("tab_w1" if name == "wc0" else f"{name}_codes"), align_bytes=64)
-            scales = keep.tile([P, grouped.shape[1]], U8, name=f"{name}_scales", align_bytes=64)
-            quantise(codes, scales, grouped)
-            return codes, scales
-
-        def quantise_in_halves(name, grouped):
-            codes = keep.tile([P, H], U32, name=f"{name}_codes", align_bytes=64)
-            scales = keep.tile([P, H], U8, name=f"{name}_scales", align_bytes=64)
-            for half in HALVES:
-                quantise(codes[:, half], scales[:, half], grouped[:, half, :])
+        def quantise_and_keep(name, grouped, pieces=(slice(None),), codes_in=None):
+            width = grouped.shape[1]
+            codes = keep.tile([P, width], U32, name=codes_in or f"{name}_codes", align_bytes=64)
+            scales = keep.tile([P, width], U8, name=f"{name}_scales", align_bytes=64)
+            for piece in pieces:
+                quantise(codes[:, piece], scales[:, piece], grouped[:, piece, :])
             return codes, scales
 
         def product(name, j, passes=(0, 1)):
@@ -182,37 +180,34 @@ def tile_list_complex_triple_messages_kernel(
             nc.scalar.activation(by_plane(planes), by_channel(acc), COPY, scale=scale)
 
         wa_grouped = [keep.tile([P, H, PACK], BF16, name=f"wa_grouped{a}", align_bytes=64) for a in range(PASSES)]
-        round_rows(nc.vector.tensor_copy, wa_grouped[0][:, H // 2 : H, :], rows["wa", 0][:, :, H // 2 : H])
-        round_rows(nc.scalar.copy, wa_grouped[0][:, 0 : H // 2, :], rows["wa", 0][:, :, 0 : H // 2])
+        left, right = COLUMN_HALVES
+        round_rows(nc.vector.tensor_copy, wa_grouped[0][:, right, :], rows["wa", 0][:, :, right])
+        round_rows(nc.scalar.copy, wa_grouped[0][:, left, :], rows["wa", 0][:, :, left])
         quantised["wa", 0] = quantise_and_keep("wa0", wa_grouped[0])
-        for half in HALVES:
+        for half in COLUMN_HALVES:
             round_rows(nc.vector.tensor_copy, wa_grouped[1][:, half, :], rows["wa", 1][:, :, half])
-        quantised["wa", 1] = quantise_in_halves("wa1", wa_grouped[1])
+        quantised["wa", 1] = quantise_and_keep("wa1", wa_grouped[1], COLUMN_HALVES)
         for j in range(TILES):
             copy_into_planes(b_planes[j], product("wb", j), 1.0)
         wc_grouped = keep.tile([P, PASSES * H, PACK], BF16, name="tab_w0", align_bytes=64)
         round_rows(nc.vector.tensor_copy, wc_grouped[:, 0:H, :], rows["wc", 0][:])
-        a_planes = keep.tile([P, GPSIMD_AB_TILES, H], F32, name="a_planes", align_bytes=64)
-        late_a = {}
-        for j in range(TILES):
+        a_planes = keep.tile([P, len(GPSIMD_FIRST), H], F32, name="a_planes", align_bytes=64)
+        for j in range(GPSIMD_LAST):
             acc = product("wa", j, (0, 1) if j < EARLY_A_TILES else (1, 0))
-            if j < GPSIMD_AB_TILES:
+            if j in GPSIMD_FIRST:
                 copy_into_planes(a_planes[:, j, :], acc, 1.0)
                 nc.gpsimd.tensor_tensor(ab_planes[j][:], a_planes[:, j, :], b_planes[j][:], MULT)
-            elif j < TILES - LATE_AB_TILES:
-                multiply_into_planes(ab_planes[j], acc, b_planes[j])
             else:
-                late_a[j] = acc
+                multiply_into_planes(ab_planes[j], acc, b_planes[j])
+        last_a = product("wa", GPSIMD_LAST, (1, 0))
         round_rows(nc.scalar.copy, wc_grouped[:, H : 2 * H, :], rows["wc", 1][:])
-        for a in range(PASSES):
-            quantised["wc", a] = quantise_and_keep(f"wc{a}", wc_grouped[:, a * H : (a + 1) * H, :])
+        quantised["wc", 0] = quantise_and_keep("wc0", wc_grouped[:, 0:H, :], codes_in="tab_w1")
+        quantised["wc", 1] = quantise_and_keep("wc1", wc_grouped[:, H : 2 * H, :])
 
-        late_a_planes = keep.tile([P, LATE_AB_TILES, H], F32, name="wc_rows1")
-        late_ab_planes = keep.tile([P, LATE_AB_TILES, H], F32, name="tab_w0", align_bytes=64)
-        for n, j in enumerate(late_a):
-            copy_into_planes(late_a_planes[:, n, :], late_a[j], 1.0)
-            ab_planes.append(late_ab_planes[:, n, :])
-            nc.gpsimd.tensor_tensor(ab_planes[j], late_a_planes[:, n, :], b_planes[j][:], MULT)
+        last_a_planes = keep.tile([P, H], F32, name="wc_rows1")
+        ab_planes.append(keep.tile([P, H], F32, name="tab_w0", align_bytes=64))
+        copy_into_planes(last_a_planes, last_a, 1.0)
+        nc.gpsimd.tensor_tensor(ab_planes[GPSIMD_LAST][:], last_a_planes[:], b_planes[GPSIMD_LAST][:], MULT)
 
         def make_minus_d(j):
             copy_into_planes(minus_d_planes[j], product("wd", j), -1.0)
@@ -220,12 +215,6 @@ def tile_list_complex_triple_messages_kernel(
         def make_minus_cd(j):
             copy_into_planes(c_planes[j], product("wc", j), 1.0)
             nc.gpsimd.tensor_tensor(minus_cd_planes[j][:], c_planes[j][:], minus_d_planes[j][:], MULT)
-
-        def make_c(j):
-            copy_into_planes(c_planes[j], product("wc", j), 1.0)
-
-        def make_pair(n):
-            nc.gpsimd.tensor_tensor(cd_pairs[n][:], c_pairs[n][:], d_pairs[n][:], MULT)
 
         held = {}
 
@@ -250,56 +239,37 @@ def tile_list_complex_triple_messages_kernel(
             for j in tiles:
                 turn(j, minus_cd_planes, False)
 
-        c_banks = {}
-        turn_ab((2,))
-        turn_ab((3,))
-        make_minus_d(2)
-        make_minus_d(3)
-        turn_ab((4,))
-        turn_ab((5,))
-        make_minus_cd(2)
-        make_minus_d(4)
-        make_minus_cd(3)
-        make_minus_d(5)
-        make_minus_cd(4)
-        make_minus_d(0)
-        make_minus_cd(5)
-        make_minus_d(1)
-        make_minus_cd(0)
-        make_minus_d(6)
-        make_minus_cd(1)
-        make_minus_d(7)
-        make_minus_cd(6)
-        turn_cd((2,))
-        turn_cd((3,))
-        turn_cd((4,))
-        make_minus_cd(7)
-        turn_cd((5,))
-        turn_ab((0,))
-        turn_cd((0,))
-        turn_ab((1,))
-        turn_cd((1,))
-        turn_ab((6,))
-        turn_ab((7,))
-        turn_cd((6,))
-        turn_cd((7,))
+        turn_ab(TURNED_EARLY[:2])
+        for j in ORDER[:D_AHEAD]:
+            make_minus_d(j)
+        turn_ab(TURNED_EARLY[2:])
+        for n, j in enumerate(ORDER[:-1]):
+            make_minus_cd(j)
+            if n + D_AHEAD < TILES:
+                make_minus_d(ORDER[n + D_AHEAD])
+        turn_cd(TURNED_EARLY)
+        make_minus_cd(ORDER[-1])
+        for j in GPSIMD_FIRST:
+            turn_ab((j,))
+            turn_cd((j,))
+        turn_ab(ORDER[-2:])
+        turn_cd(ORDER[-2:])
 
         picked = keep.tile([P, PACK, S], F32, name="picked")
-        for t, lo, hi in ((0, 0, S), (1, 0, S), (2, 0, S), (3, 0, HALF), (3, HALF, S)):
-            nc.vector.tensor_copy(picked[:, t, lo:hi], gates[t][:].indirect(listed(lo, hi)))
-
+        for t in range(PACK):
+            for lo, hi in LIST_HALVES if t == PACK - 1 else ((0, S),):
+                nc.vector.tensor_copy(picked[:, t, lo:hi], gates[t][:].indirect(listed(lo, hi)))
 
         def staged(shape, dtype):
-            return tail.tile(shape, dtype, name="staged", align_bytes=64, bufs=9)
+            return tail.tile(shape, dtype, name="staged", align_bytes=64, bufs=STAGED)
 
-        chunks = [(0, 2), (2, 4), (4, 6), (6, 7), (7, 8)]
         h_grouped = {}
 
         def weigh(j):
-            chunk = [c for c in chunks if c[0] <= j < c[1]][0]
+            chunk = [tiles for tiles in CHUNKS if j in tiles][0]
             if chunk not in h_grouped:
-                h_grouped[chunk] = staged([P, (chunk[1] - chunk[0]) * P, PACK], BF16)
-            lo = (j - chunk[0]) * P
+                h_grouped[chunk] = staged([P, len(chunk) * P, PACK], BF16)
+            lo = chunk.index(j) * P
             nc.vector.tensor_tensor(
                 h_grouped[chunk][:, lo : lo + P, :].rearrange("p (c e) t -> p c t e", e=2),
                 held[j][:].rearrange("p t (c e) -> p c t e", e=2),
@@ -307,13 +277,12 @@ def tile_list_complex_triple_messages_kernel(
                 MULT,
             )
 
-        def finish(index, engines):
-            chunk = chunks[index]
-            width = (chunk[1] - chunk[0]) * P
+        def finish(chunk):
+            width = len(chunk) * P
             codes = staged([P, width], U32)
-            scales = tail.tile([P, width], U8, name="h_scales", align_bytes=64, bufs=5)
+            scales = tail.tile([P, width], U8, name="h_scales", align_bytes=64)
             quantise(codes, scales, h_grouped[chunk])
-            result = tail.tile([P, N // P, width], F32, name="result", bufs=5)
+            result = tail.tile([P, N // P, width], F32, name="result")
             for n in range(N // P):
                 cols = slice(n * P, (n + 1) * P)
                 y = psum.tile([P, width], F32, name="bank")
@@ -326,29 +295,25 @@ def tile_list_complex_triple_messages_kernel(
                     start=True,
                     stop=True,
                 )
-                if engines[n] == "V":
+                if len(chunk) == 1 and n == 1:
                     nc.vector.tensor_scalar(result[:, n, :], y[:], bias[:, n : n + 1], None, op0=ADD)
                 else:
                     nc.scalar.activation(result[:, n, :], y[:], IDENTITY, bias=bias[:, n : n + 1])
-            nc.sync.dma_start(
-                out[:, chunk[0] * P : chunk[1] * P].rearrange("(n p) j -> p n j", p=P), result[:]
-            )
+            first = chunk[0] * P
+            nc.sync.dma_start(out[:, first : first + width].rearrange("(n p) j -> p n j", p=P), result[:])
 
-        weigh(2)
-        weigh(3)
-        weigh(4)
-        weigh(5)
-        weigh(0)
-        w2_grouped = keep.tile([P, N, PACK], BF16, name="wa_grouped0", align_bytes=64)
+        for j in ORDER[:WEIGHED_FIRST]:
+            weigh(j)
+        w2_grouped = keep.tile([P, N, PACK], BF16, name="wc1_codes", align_bytes=64)
         round_rows(nc.scalar.copy, w2_grouped[:], rows["w2", 0][:])
         w2_codes = staged([P, N], U32)
         w2_scales = keep.tile([P, N], U8, name="w2_scales", align_bytes=64)
         quantise(w2_codes, w2_scales, w2_grouped)
-        finish(1, "SS")
-        finish(2, "SS")
-        weigh(1)
-        weigh(6)
-        finish(0, "SS")
-        weigh(7)
-        finish(3, "SS")
-        finish(4, "SV")
+        waiting = list(CHUNKS)
+        for n in range(WEIGHED_FIRST, TILES + 1):
+            for chunk in [tiles for tiles in waiting if set(tiles) <= set(ORDER[: n - 1])]:
+                finish(chunk)
+                waiting.remove(chunk)
+            if n < TILES:
+                weigh(ORDER[n])
+        finish(CHUNKS[-1])

@@ -30,22 +30,27 @@ PER_COLUMN = 16
 
 PASS_SHIFT = QUADRANT // PASSES
 
+TABLE_PIECES = (((0, P), (P, 4 * P), (4 * P, S)), ((0, 2 * P), (2 * P, 4 * P), (4 * P, S)))
 LIST_HALVES = ((0, S // 2), (S // 2, S))
-FIRST_GATHER = 3 * P
 COLUMN_HALVES = (slice(0, H // 2), slice(H // 2, H))
 
+BANKS = 8
+B_FROM_PASS_0 = 6
 GPSIMD_FIRST = (0, 1)
-GPSIMD_LAST = TILES - 1
-TURNED_EARLY = (2, 3, 4, 5)
-ORDER = TURNED_EARLY + GPSIMD_FIRST + (TILES - 2, GPSIMD_LAST)
-EARLY_A_TILES = 6
-D_AHEAD = 2
+VECTOR_AB = (2, 3, 4, 5, 6, 7)
+A_ORDER = VECTOR_AB[:1] + GPSIMD_FIRST + VECTOR_AB[1:]
+A_FROM_PASS_0 = 6
+ORDER = (2, 3, 4, 5, 0, 1, 6, 7)
+D_BEHIND_A = 3
+TURNED_EARLY = 3
+PLANE_PITCH = S
+C_BUFFERS = 3
 
 CHUNKS = (ORDER[0:2], ORDER[2:4], ORDER[4:6], ORDER[6:7], ORDER[7:8])
 WEIGHED_FIRST = 5
 
-BANKS = 8
-STAGED = 2 * len(CHUNKS) + 1
+VECTOR_BUFFERS = 18
+SCALAR_BUFFERS = 19
 
 
 def tile_list_complex_triple_messages_kernel(
@@ -54,7 +59,6 @@ def tile_list_complex_triple_messages_kernel(
     nc = tc.nc
     with ExitStack() as ctx:
         keep = ctx.enter_context(tc.tile_pool(name="keep", bufs=1))
-        tail = ctx.enter_context(tc.tile_pool(name="tail", bufs=len(CHUNKS)))
         psum = ctx.enter_context(tc.psum_pool(name="psum", bufs=BANKS))
 
         offsets = keep.tile([P, S // PER_COLUMN], U16, name="offsets")
@@ -69,18 +73,14 @@ def tile_list_complex_triple_messages_kernel(
         ident = keep.tile([P, P], F32, name="ident")
         v_w = [keep.tile([P, S], U32, name=f"v_w{a}", align_bytes=64) for a in range(PASSES)]
         v_sc = [keep.tile([P, S], U8, name=f"v_sc{a}", align_bytes=64) for a in range(PASSES)]
-        b_pairs = [
-            keep.tile([P, 2, H], F32, name=("tab_w1" if n == 1 else f"b_planes{n}"), align_bytes=64)
-            for n in range(TILES // 2)
-        ]
-        b_planes = [b_pairs[j // 2][:, j % 2, :] for j in range(TILES)]
-        minus_d_planes = [keep.tile([P, H], F32, name=f"minus_d_planes{j}") for j in range(TILES)]
-        c_planes = [keep.tile([P, H], F32, name=f"c_planes{j}") for j in range(TILES)]
-        ab_planes = [keep.tile([P, H], F32, name=f"ab_planes{j}") for j in range(GPSIMD_LAST)]
-        minus_cd_planes = [
-            keep.tile([P, H], F32, name=f"minus_cd_planes{j}") if j // 2 == 1 else b_planes[j] for j in range(TILES)
-        ]
-        quantised = {}
+        picked_bytes = keep.tile([P, PACK * PLANE_PITCH], F32, name="picked", align_bytes=64)
+        picked = picked_bytes[:].rearrange("p (t c) -> p t c", t=PACK)[:, :, 0:S]
+
+        def vector_out(shape, dtype):
+            return keep.tile(shape, dtype, name="vector_out", align_bytes=64, bufs=VECTOR_BUFFERS)
+
+        def scalar_out(shape, dtype):
+            return keep.tile(shape, dtype, name="scalar_out", align_bytes=64, bufs=SCALAR_BUFFERS)
 
         def listed(lo, hi):
             return offsets[:, lo // PER_COLUMN : hi // PER_COLUMN]
@@ -93,7 +93,8 @@ def tile_list_complex_triple_messages_kernel(
         def load_table_scales():
             by_row = tab_scales.rearrange("a (q s) c -> s q a c", s=SCALE_ROWS)
             for s in range(SCALE_ROWS):
-                nc.sync.dma_start(tab_sc[s:P:PASS_SHIFT], by_row[s].bitcast(I32))
+                queue = nc.sync if s < SCALE_ROWS // 2 else nc.scalar
+                queue.dma_start(tab_sc[s:P:PASS_SHIFT], by_row[s].bitcast(I32))
 
         def load_table_words(a):
             nc.sync.dma_start(tab_w[a][:], tab_words[a].rearrange("p t i -> p (t i)").bitcast(I32))
@@ -101,8 +102,9 @@ def tile_list_complex_triple_messages_kernel(
         def load_fp4_words(name, src):
             nc.sync.dma_start(fp4_w[name][:], src.rearrange("a p n -> p a n").bitcast(I32))
 
-        def load_rows(name, src, a):
-            nc.sync.dma_start(rows[name, a][:], src[a * K_PASS : (a + 1) * K_PASS, :].rearrange("(p i) c -> p i c", i=PACK))
+        def load_rows(name, src, a, which=slice(0, PACK)):
+            by_partition = src[a * K_PASS : (a + 1) * K_PASS, :].rearrange("(p i) c -> p i c", i=PACK)
+            nc.sync.dma_start(rows[name, a][:, which, :], by_partition[:, which, :])
 
         def load_gate(t):
             nc.sync.dma_start(gates[t][:], gT.rearrange("(p t) c -> t p c", t=PACK)[t])
@@ -110,14 +112,15 @@ def tile_list_complex_triple_messages_kernel(
         nc.vector.memset(tab_sc[:], 0)
         nc.sync.dma_start(offsets[:], offs)
         load_fp4_words("wb", wb_words)
-        load_fp4_scales("wb", wb_scales, (0,))
         load_table_scales()
         load_table_words(0)
         nc.vector.tensor_copy(v_sc[0][:], tab_sc[:].bitcast(U8).indirect(listed(0, S)))
-        load_fp4_scales("wb", wb_scales, (1, 2, 3))
+        load_fp4_scales("wb", wb_scales, (0, 1, 2, 3))
         load_table_words(1)
-        load_rows("wa", wa, 0)
-        nc.sync.dma_start(v_sc[1][0 : P - PASS_SHIFT].bitcast(I32), v_sc[0][PASS_SHIFT:P].bitcast(I32))
+        load_rows("wa", wa, 0, slice(0, 1))
+        for s in range(SCALE_ROWS):
+            nc.sync.dma_start(v_sc[1][s:P:QUADRANT].bitcast(I32), v_sc[0][PASS_SHIFT + s : P : QUADRANT].bitcast(I32))
+        load_rows("wa", wa, 0, slice(1, PACK))
         load_rows("wa", wa, 1)
         load_rows("wc", wc, 0)
         load_rows("wc", wc, 1)
@@ -130,145 +133,194 @@ def tile_list_complex_triple_messages_kernel(
             nc.sync.dma_start(bias[:], b2.rearrange("(n p) -> p n", p=P))
         make_identity(nc, ident[:])
 
-        for a, pieces in enumerate((((0, FIRST_GATHER), (FIRST_GATHER, S)), LIST_HALVES)):
-            for lo, hi in pieces:
+        for a in range(PASSES):
+            for lo, hi in TABLE_PIECES[a]:
                 nc.vector.tensor_copy(v_w[a][:, lo:hi], tab_w[a][:].bitcast(U32).indirect(listed(lo, hi)))
 
         def round_rows(copy, dst, src):
             copy(dst.rearrange("p (c e) i -> p c i e", e=2), src.rearrange("p i (c e) -> p c i e", e=2))
 
         def quantise(codes, scales, grouped):
-            nc.vector.quantize_mx(codes[:].bitcast(FP8X4), scales[:], grouped[:].rearrange("p c i -> p (c i)"))
+            nc.vector.quantize_mx(codes.bitcast(FP8X4), scales, grouped.rearrange("p c i -> p (c i)"))
 
-        def quantise_and_keep(name, grouped, pieces=(slice(None),), codes_in=None):
-            width = grouped.shape[1]
-            codes = keep.tile([P, width], U32, name=codes_in or f"{name}_codes", align_bytes=64)
-            scales = keep.tile([P, width], U8, name=f"{name}_scales", align_bytes=64)
-            for piece in pieces:
-                quantise(codes[:, piece], scales[:, piece], grouped[:, piece, :])
-            return codes, scales
+        quantised = {}
+
+        def round_on_vector(name, a):
+            halves = [vector_out([P, H // 2, PACK], BF16) for half in COLUMN_HALVES]
+            for grouped, half in zip(halves, COLUMN_HALVES):
+                round_rows(nc.vector.tensor_copy, grouped[:], rows[name, a][:, :, half])
+            return [grouped[:] for grouped in halves]
+
+        def quantise_pass(name, a, halves):
+            codes = vector_out([P, H], U32)
+            scales = keep.tile([P, H], U8, name=f"{name}_scales{a}", align_bytes=64)
+            for grouped, half in zip(halves, COLUMN_HALVES):
+                quantise(codes[:, half], scales[:, half], grouped)
+            quantised[name, a] = (codes, scales)
+
+        acc = {}
+
+        def multiply(name, j, a):
+            first = (name, j) not in acc
+            if first:
+                acc[name, j] = psum.tile([P, H], F32, name="bank")
+            cols = slice(j * P, (j + 1) * P)
+            if name in fp4_w:
+                codes, scales = fp4_w[name][:, a, :].bitcast(FP4X4), fp4_sc[name][:, a, :].bitcast(U8)
+            else:
+                codes, scales = quantised[name, a][0][:].bitcast(FP8X4), quantised[name, a][1][:]
+            nc.tensor.matmul_mx(
+                acc[name, j][:],
+                lhsT=v_w[a][:, cols].bitcast(FP8X4),
+                lhsT_scale=v_sc[a][:, cols],
+                rhs=codes,
+                rhs_scale=scales,
+                start=first,
+                stop=not first,
+            )
 
         def product(name, j, passes=(0, 1)):
-            acc = psum.tile([P, H], F32, name="bank")
-            cols = slice(j * P, (j + 1) * P)
             for a in passes:
-                if name in fp4_w:
-                    codes, scales = fp4_w[name][:, a, :].bitcast(FP4X4), fp4_sc[name][:, a, :].bitcast(U8)
-                else:
-                    codes, scales = quantised[name, a][0][:].bitcast(FP8X4), quantised[name, a][1][:]
-                nc.tensor.matmul_mx(
-                    acc[:],
-                    lhsT=v_w[a][:, cols].bitcast(FP8X4),
-                    lhsT_scale=v_sc[a][:, cols],
-                    rhs=codes,
-                    rhs_scale=scales,
-                    start=(a == passes[0]),
-                    stop=(a == passes[-1]),
-                )
-            return acc
+                multiply(name, j, a)
 
-        def by_channel(tile):
-            return tile[:].rearrange("p (b m t) -> p b t m", m=4, t=PACK)
+        def by_channel(ap):
+            return ap.rearrange("p (b m t) -> p b t m", m=4, t=PACK)
 
-        def by_plane(tile):
-            return tile[:].rearrange("p (t b m) -> p b t m", m=4, t=PACK)
+        def by_plane(ap):
+            return ap.rearrange("p (t b m) -> p b t m", m=4, t=PACK)
 
-        def multiply_into_planes(planes, acc, other_planes):
-            nc.vector.tensor_tensor(by_plane(planes), by_channel(acc), by_plane(other_planes), MULT)
+        planes = {}
 
-        def copy_into_planes(planes, acc, scale):
-            nc.scalar.activation(by_plane(planes), by_channel(acc), COPY, scale=scale)
+        def copy_out(name, j, dst=None):
+            planes[name, j] = scalar_out([P, H], F32)[:] if dst is None else dst
+            nc.scalar.activation(by_plane(planes[name, j]), by_channel(acc[name, j][:]), COPY, scale=(-1.0 if name == "wd" else 1.0))
 
-        wa_grouped = [keep.tile([P, H, PACK], BF16, name=f"wa_grouped{a}", align_bytes=64) for a in range(PASSES)]
-        left, right = COLUMN_HALVES
-        round_rows(nc.vector.tensor_copy, wa_grouped[0][:, right, :], rows["wa", 0][:, :, right])
-        round_rows(nc.scalar.copy, wa_grouped[0][:, left, :], rows["wa", 0][:, :, left])
-        quantised["wa", 0] = quantise_and_keep("wa0", wa_grouped[0])
-        for half in COLUMN_HALVES:
-            round_rows(nc.vector.tensor_copy, wa_grouped[1][:, half, :], rows["wa", 1][:, :, half])
-        quantised["wa", 1] = quantise_and_keep("wa1", wa_grouped[1], COLUMN_HALVES)
-        for j in range(TILES):
-            copy_into_planes(b_planes[j], product("wb", j), 1.0)
-        wc_grouped = keep.tile([P, PASSES * H, PACK], BF16, name="tab_w0", align_bytes=64)
-        round_rows(nc.vector.tensor_copy, wc_grouped[:, 0:H, :], rows["wc", 0][:])
-        a_planes = keep.tile([P, len(GPSIMD_FIRST), H], F32, name="a_planes", align_bytes=64)
-        for j in range(GPSIMD_LAST):
-            acc = product("wa", j, (0, 1) if j < EARLY_A_TILES else (1, 0))
-            if j in GPSIMD_FIRST:
-                copy_into_planes(a_planes[:, j, :], acc, 1.0)
-                nc.gpsimd.tensor_tensor(ab_planes[j][:], a_planes[:, j, :], b_planes[j][:], MULT)
-            else:
-                multiply_into_planes(ab_planes[j], acc, b_planes[j])
-        last_a = product("wa", GPSIMD_LAST, (1, 0))
-        round_rows(nc.scalar.copy, wc_grouped[:, H : 2 * H, :], rows["wc", 1][:])
-        quantised["wc", 0] = quantise_and_keep("wc0", wc_grouped[:, 0:H, :], codes_in="tab_w1")
-        quantised["wc", 1] = quantise_and_keep("wc1", wc_grouped[:, H : 2 * H, :])
-
-        last_a_planes = keep.tile([P, H], F32, name="wc_rows1")
-        ab_planes.append(keep.tile([P, H], F32, name="tab_w0", align_bytes=64))
-        copy_into_planes(last_a_planes, last_a, 1.0)
-        nc.gpsimd.tensor_tensor(ab_planes[GPSIMD_LAST][:], last_a_planes[:], b_planes[GPSIMD_LAST][:], MULT)
-
-        def make_minus_d(j):
-            copy_into_planes(minus_d_planes[j], product("wd", j), -1.0)
-
-        def make_minus_cd(j):
-            copy_into_planes(c_planes[j], product("wc", j), 1.0)
-            nc.gpsimd.tensor_tensor(minus_cd_planes[j][:], c_planes[j][:], minus_d_planes[j][:], MULT)
+        def ab_on_vector(j):
+            planes["ab", j] = vector_out([P, H], F32)[:]
+            nc.vector.tensor_tensor(by_plane(planes["ab", j]), by_channel(acc["wa", j][:]), by_plane(planes["wb", j]), MULT)
 
         held = {}
 
-        def turn(j, planes, first):
+        def turn(name, j):
+            first = j not in held
             if first:
                 held[j] = psum.tile([P, PACK, P], F32, name="bank")
             for t in range(PACK):
                 nc.tensor.matmul(
                     held[j][:, t, :],
-                    planes[j][:, t * P : (t + 1) * P],
+                    planes[name, j][:, t * P : (t + 1) * P],
                     ident[:],
                     start=(first and t == 0),
                     stop=(not first and t == PACK - 1),
                     is_transpose=True,
                 )
 
-        def turn_ab(tiles):
-            for j in tiles:
-                turn(j, ab_planes, True)
+        for j in range(B_FROM_PASS_0):
+            multiply("wb", j, 0)
+        for j in range(TILES):
+            product("wb", j, (1,) if j < B_FROM_PASS_0 else (1, 0))
+            copy_out("wb", j)
 
-        def turn_cd(tiles):
-            for j in tiles:
-                turn(j, minus_cd_planes, False)
+        quantise_pass("wa", 0, round_on_vector("wa", 0))
+        for j in A_ORDER[:A_FROM_PASS_0]:
+            multiply("wa", j, 0)
+        quantise_pass("wa", 1, round_on_vector("wa", 1))
+        left, right = COLUMN_HALVES
+        wc_left = scalar_out([P, H // 2, PACK], BF16)[:]
+        round_rows(nc.scalar.copy, wc_left, rows["wc", 0][:, :, left])
+        wc_right = vector_out([P, H // 2, PACK], BF16)[:]
+        round_rows(nc.vector.tensor_copy, wc_right, rows["wc", 0][:, :, right])
+        wc_first = [wc_left, wc_right]
+        for n, j in enumerate(A_ORDER):
+            product("wa", j, (1,) if n < A_FROM_PASS_0 else (1, 0))
 
-        turn_ab(TURNED_EARLY[:2])
-        for j in ORDER[:D_AHEAD]:
-            make_minus_d(j)
-        turn_ab(TURNED_EARLY[2:])
-        for n, j in enumerate(ORDER[:-1]):
-            make_minus_cd(j)
-            if n + D_AHEAD < TILES:
-                make_minus_d(ORDER[n + D_AHEAD])
-        turn_cd(TURNED_EARLY)
-        make_minus_cd(ORDER[-1])
+        def as_planes(grouped):
+            return grouped.rearrange("p c i -> p (c i)").bitcast(F32)
+
+        def ab_on_gpsimd(j, dst):
+            planes["ab", j] = dst
+            nc.gpsimd.tensor_tensor(dst, planes["wa", j], planes["wb", j], MULT)
+
         for j in GPSIMD_FIRST:
-            turn_ab((j,))
-            turn_cd((j,))
-        turn_ab(ORDER[-2:])
-        turn_cd(ORDER[-2:])
+            copy_out("wa", j)
+        ab_on_vector(VECTOR_AB[0])
+        quantise_pass("wc", 0, wc_first)
+        for j, grouped in zip(GPSIMD_FIRST, reversed(wc_first)):
+            ab_on_gpsimd(j, as_planes(grouped))
+        for j in VECTOR_AB[1:]:
+            ab_on_vector(j)
+        wc_last = picked_bytes[:, 0:S].bitcast(BF16).rearrange("p (c i) -> p c i", i=PACK)
+        for half in COLUMN_HALVES:
+            round_rows(nc.scalar.copy, wc_last[:, half, :], rows["wc", 1][:, :, half])
+        quantise_pass("wc", 1, [wc_last[:, half, :] for half in COLUMN_HALVES])
 
-        picked = keep.tile([P, PACK, S], F32, name="picked")
+        def make_cd(n):
+            j = ORDER[n]
+            product("wc", j, (1,) if ("wc", j) in acc else (1, 0))
+            copy_out("wc", j, keep.tile([P, H], F32, name="c_planes", align_bytes=64, bufs=C_BUFFERS)[:])
+            planes["cd", j] = planes["wd", j]
+            nc.gpsimd.tensor_tensor(planes["cd", j], planes["wc", j], planes["wd", j], MULT)
+
+        def make_d(n):
+            product("wd", ORDER[n])
+            copy_out("wd", ORDER[n])
+
+        def turn_ab(n):
+            turn("ab", ORDER[n])
+
+        def begin_c(n):
+            multiply("wc", ORDER[n], 0)
+
+        def finish_difference(n):
+            if ORDER[n] not in held:
+                turn("ab", ORDER[n])
+            turn("cd", ORDER[n])
+
+        make_d(0)
+        make_d(1)
+        begin_c(0)
+        begin_c(1)
+        turn_ab(0)
+        turn_ab(1)
+        make_cd(0)
+        make_cd(1)
+        make_d(2)
+        make_cd(2)
+        make_d(3)
+        make_cd(3)
+        turn_ab(2)
+        turn_ab(3)
+        finish_difference(0)
+        make_d(4)
+        make_cd(4)
+        make_d(5)
+        make_cd(5)
+        finish_difference(1)
+        finish_difference(2)
+        make_d(6)
+        make_cd(6)
+        make_d(7)
+        make_cd(7)
+        finish_difference(3)
+        turn_ab(4)
+        finish_difference(4)
+        turn_ab(5)
+        turn_ab(6)
+        turn_ab(7)
+        finish_difference(5)
+        finish_difference(6)
+        finish_difference(7)
+
         for t in range(PACK):
-            for lo, hi in LIST_HALVES if t == PACK - 1 else ((0, S),):
+            for lo, hi in LIST_HALVES if t in (0, PACK - 1) else ((0, S),):
                 nc.vector.tensor_copy(picked[:, t, lo:hi], gates[t][:].indirect(listed(lo, hi)))
-
-        def staged(shape, dtype):
-            return tail.tile(shape, dtype, name="staged", align_bytes=64, bufs=STAGED)
 
         h_grouped = {}
 
         def weigh(j):
             chunk = [tiles for tiles in CHUNKS if j in tiles][0]
             if chunk not in h_grouped:
-                h_grouped[chunk] = staged([P, len(chunk) * P, PACK], BF16)
+                h_grouped[chunk] = vector_out([P, len(chunk) * P, PACK], BF16)
             lo = chunk.index(j) * P
             nc.vector.tensor_tensor(
                 h_grouped[chunk][:, lo : lo + P, :].rearrange("p (c e) t -> p c t e", e=2),
@@ -277,12 +329,19 @@ def tile_list_complex_triple_messages_kernel(
                 MULT,
             )
 
+        h_quantised = {}
+
+        def quantise_chunk(chunk):
+            width = len(chunk) * P
+            codes = vector_out([P, width], U32)
+            scales = keep.tile([P, width], U8, name="h_scales", align_bytes=64, bufs=len(CHUNKS))
+            quantise(codes[:], scales[:], h_grouped[chunk][:])
+            h_quantised[chunk] = (codes, scales)
+
         def finish(chunk):
             width = len(chunk) * P
-            codes = staged([P, width], U32)
-            scales = tail.tile([P, width], U8, name="h_scales", align_bytes=64)
-            quantise(codes, scales, h_grouped[chunk])
-            result = tail.tile([P, N // P, width], F32, name="result")
+            codes, scales = h_quantised[chunk]
+            result = keep.tile([P, N // P, width], F32, name="result", bufs=len(CHUNKS))
             for n in range(N // P):
                 cols = slice(n * P, (n + 1) * P)
                 y = psum.tile([P, width], F32, name="bank")
@@ -302,18 +361,20 @@ def tile_list_complex_triple_messages_kernel(
             first = chunk[0] * P
             nc.sync.dma_start(out[:, first : first + width].rearrange("(n p) j -> p n j", p=P), result[:])
 
+        w2_grouped = keep.tile([P, N, PACK], BF16, name="c_planes", align_bytes=64, bufs=C_BUFFERS)
+        round_rows(nc.scalar.copy, w2_grouped[:], rows["w2", 0][:])
         for j in ORDER[:WEIGHED_FIRST]:
             weigh(j)
-        w2_grouped = keep.tile([P, N, PACK], BF16, name="wc1_codes", align_bytes=64)
-        round_rows(nc.scalar.copy, w2_grouped[:], rows["w2", 0][:])
-        w2_codes = staged([P, N], U32)
+        w2_codes = vector_out([P, N], U32)
         w2_scales = keep.tile([P, N], U8, name="w2_scales", align_bytes=64)
-        quantise(w2_codes, w2_scales, w2_grouped)
+        quantise(w2_codes[:], w2_scales[:], w2_grouped[:])
         waiting = list(CHUNKS)
         for n in range(WEIGHED_FIRST, TILES + 1):
             for chunk in [tiles for tiles in waiting if set(tiles) <= set(ORDER[: n - 1])]:
-                finish(chunk)
+                quantise_chunk(chunk)
                 waiting.remove(chunk)
             if n < TILES:
                 weigh(ORDER[n])
-        finish(CHUNKS[-1])
+        quantise_chunk(CHUNKS[-1])
+        for chunk in CHUNKS:
+            finish(chunk)

@@ -93,8 +93,7 @@ def tile_list_complex_triple_messages_kernel(
         def load_table_scales():
             by_row = tab_scales.rearrange("a (q s) c -> s q a c", s=SCALE_ROWS)
             for s in range(SCALE_ROWS):
-                queue = nc.sync if s < SCALE_ROWS // 2 else nc.scalar
-                queue.dma_start(tab_sc[s:P:PASS_SHIFT], by_row[s].bitcast(I32))
+                nc.sync.dma_start(tab_sc[s:P:PASS_SHIFT], by_row[s].bitcast(I32))
 
         def load_table_words(a):
             nc.sync.dma_start(tab_w[a][:], tab_words[a].rearrange("p t i -> p (t i)").bitcast(I32))

@@ -35,6 +35,7 @@ LIST_HALVES = ((0, S // 2), (S // 2, S))
 COLUMN_HALVES = (slice(0, H // 2), slice(H // 2, H))
 
 BANKS = 8
+WARM_UPS = 6
 B_FROM_PASS_0 = 6
 GPSIMD_FIRST = (0, 1)
 VECTOR_AB = (2, 3, 4, 5, 6, 7)
@@ -113,6 +114,23 @@ def tile_list_complex_triple_messages_kernel(
         load_fp4_words("wb", wb_words)
         load_table_scales()
         load_table_words(0)
+        zeros = keep.tile([P, K_PASS * PACK // 2], I32, name="zeros", align_bytes=64)
+        zero_codes = keep.tile([P, H], U32, name="zero_codes", align_bytes=64)
+        zero_scales = keep.tile([P, H], U8, name="zero_scales", align_bytes=64)
+        nc.vector.memset(zeros[:], 0)
+        nc.vector.quantize_mx(zero_codes[:].bitcast(FP8X4), zero_scales[:], zeros[:].bitcast(BF16))
+        unread = psum.tile([P, H], F32, name="bank")
+        for n in range(WARM_UPS):
+            nc.tensor.matmul_mx(
+                unread[:],
+                lhsT=zero_codes[:, 0:P].bitcast(FP8X4),
+                lhsT_scale=zero_scales[:, 0:P],
+                rhs=zero_codes[:].bitcast(FP8X4),
+                rhs_scale=zero_scales[:],
+                start=(n == 0),
+                stop=(n == WARM_UPS - 1),
+            )
+
         nc.vector.tensor_copy(v_sc[0][:], tab_sc[:].bitcast(U8).indirect(listed(0, S)))
         load_fp4_scales("wb", wb_scales, (0, 1, 2, 3))
         load_table_words(1)

@@ -40,7 +40,7 @@ B_FROM_PASS_0 = 6
 GPSIMD_FIRST = (0, 1)
 VECTOR_AB = (2, 3, 4, 5, 6, 7)
 A_ORDER = VECTOR_AB[:1] + GPSIMD_FIRST + VECTOR_AB[1:]
-A_FROM_PASS_0 = 6
+A_FROM_PASS_0 = 7
 ORDER = (2, 3, 4, 5, 0, 1, 6, 7)
 D_BEHIND_A = 3
 TURNED_EARLY = 3
@@ -71,7 +71,6 @@ def tile_list_complex_triple_messages_kernel(
         rows["w2", 0] = keep.tile([P, PACK, N], F32, name="w2_rows")
         bias = keep.tile([P, N // P], F32, name="bias")
         gates = [keep.tile([P, T], F32, name=f"gate{t}") for t in range(PACK)]
-        ident = keep.tile([P, P], F32, name="ident")
         v_w = [keep.tile([P, S], U32, name=f"v_w{a}", align_bytes=64) for a in range(PASSES)]
         v_sc = [keep.tile([P, S], U8, name=f"v_sc{a}", align_bytes=64) for a in range(PASSES)]
         picked_bytes = keep.tile([P, PACK * PLANE_PITCH], F32, name="picked", align_bytes=64)
@@ -119,13 +118,15 @@ def tile_list_complex_triple_messages_kernel(
         zero_scales = keep.tile([P, H], U8, name="zero_scales", align_bytes=64)
         nc.vector.memset(zeros[:], 0)
         nc.vector.quantize_mx(zero_codes[:].bitcast(FP8X4), zero_scales[:], zeros[:].bitcast(BF16))
+        ident = keep.tile([P, P], F32, name="zeros", align_bytes=64)
+        make_identity(nc, ident[:])
         unread = psum.tile([P, H], F32, name="bank")
         for n in range(WARM_UPS):
             nc.tensor.matmul_mx(
                 unread[:],
                 lhsT=zero_codes[:, 0:P].bitcast(FP8X4),
                 lhsT_scale=zero_scales[:, 0:P],
-                rhs=zero_codes[:].bitcast(FP8X4),
+                rhs=fp4_w["wb"][:, 0, :].bitcast(FP4X4),
                 rhs_scale=zero_scales[:],
                 start=(n == 0),
                 stop=(n == WARM_UPS - 1),
@@ -148,7 +149,6 @@ def tile_list_complex_triple_messages_kernel(
         load_rows("w2", w2, 0)
         with nc.allow_non_contiguous_dma(reason="one bias value for each partition and half of the outputs"):
             nc.sync.dma_start(bias[:], b2.rearrange("(n p) -> p n", p=P))
-        make_identity(nc, ident[:])
 
         for a in range(PASSES):
             for lo, hi in TABLE_PIECES[a]:
@@ -293,12 +293,12 @@ def tile_list_complex_triple_messages_kernel(
                 turn("ab", ORDER[n])
             turn("cd", ORDER[n])
 
+        turn_ab(0)
+        turn_ab(1)
         make_d(0)
         make_d(1)
         begin_c(0)
         begin_c(1)
-        turn_ab(0)
-        turn_ab(1)
         make_cd(0)
         make_cd(1)
         make_d(2)

@@ -40,11 +40,9 @@ B_FROM_PASS_0 = 6
 GPSIMD_FIRST = (0, 1)
 VECTOR_AB = (2, 3, 4, 5, 6, 7)
 A_ORDER = VECTOR_AB[:1] + GPSIMD_FIRST + VECTOR_AB[1:]
-A_FROM_PASS_0 = 7
+A_FROM_PASS_0 = BANKS - 1
 ORDER = (2, 3, 4, 5, 0, 1, 6, 7)
-D_BEHIND_A = 3
-TURNED_EARLY = 3
-PLANE_PITCH = S
+PAIR = 2
 C_BUFFERS = 3
 
 CHUNKS = (ORDER[0:2], ORDER[2:4], ORDER[4:6], ORDER[6:7], ORDER[7:8])
@@ -73,8 +71,7 @@ def tile_list_complex_triple_messages_kernel(
         gates = [keep.tile([P, T], F32, name=f"gate{t}") for t in range(PACK)]
         v_w = [keep.tile([P, S], U32, name=f"v_w{a}", align_bytes=64) for a in range(PASSES)]
         v_sc = [keep.tile([P, S], U8, name=f"v_sc{a}", align_bytes=64) for a in range(PASSES)]
-        picked_bytes = keep.tile([P, PACK * PLANE_PITCH], F32, name="picked", align_bytes=64)
-        picked = picked_bytes[:].rearrange("p (t c) -> p t c", t=PACK)[:, :, 0:S]
+        picked = keep.tile([P, PACK, S], F32, name="picked", align_bytes=64)
 
         def vector_out(shape, dtype):
             return keep.tile(shape, dtype, name="vector_out", align_bytes=64, bufs=VECTOR_BUFFERS)
@@ -118,21 +115,21 @@ def tile_list_complex_triple_messages_kernel(
         zero_scales = keep.tile([P, H], U8, name="zero_scales", align_bytes=64)
         nc.vector.memset(zeros[:], 0)
         nc.vector.quantize_mx(zero_codes[:].bitcast(FP8X4), zero_scales[:], zeros[:].bitcast(BF16))
-        ident = keep.tile([P, P], F32, name="zeros", align_bytes=64)
-        make_identity(nc, ident[:])
         unread = psum.tile([P, H], F32, name="bank")
         for n in range(WARM_UPS):
             nc.tensor.matmul_mx(
                 unread[:],
                 lhsT=zero_codes[:, 0:P].bitcast(FP8X4),
                 lhsT_scale=zero_scales[:, 0:P],
-                rhs=fp4_w["wb"][:, 0, :].bitcast(FP4X4),
+                rhs=zero_codes[:].bitcast(FP8X4),
                 rhs_scale=zero_scales[:],
                 start=(n == 0),
                 stop=(n == WARM_UPS - 1),
             )
 
         nc.vector.tensor_copy(v_sc[0][:], tab_sc[:].bitcast(U8).indirect(listed(0, S)))
+        ident = keep.tile([P, P], F32, name="tab_sc", align_bytes=64)
+        make_identity(nc, ident[:])
         load_fp4_scales("wb", wb_scales, (0, 1, 2, 3))
         load_table_words(1)
         load_rows("wa", wa, 0, slice(0, 1))
@@ -266,7 +263,7 @@ def tile_list_complex_triple_messages_kernel(
             ab_on_gpsimd(j, as_planes(grouped))
         for j in VECTOR_AB[1:]:
             ab_on_vector(j)
-        wc_last = picked_bytes[:, 0:S].bitcast(BF16).rearrange("p (c i) -> p c i", i=PACK)
+        wc_last = picked[:, 0, :].bitcast(BF16).rearrange("p (c i) -> p c i", i=PACK)
         for half in COLUMN_HALVES:
             round_rows(nc.scalar.copy, wc_last[:, half, :], rows["wc", 1][:, :, half])
         quantise_pass("wc", 1, [wc_last[:, half, :] for half in COLUMN_HALVES])
@@ -293,40 +290,25 @@ def tile_list_complex_triple_messages_kernel(
                 turn("ab", ORDER[n])
             turn("cd", ORDER[n])
 
-        turn_ab(0)
-        turn_ab(1)
-        make_d(0)
-        make_d(1)
-        begin_c(0)
-        begin_c(1)
-        make_cd(0)
-        make_cd(1)
-        make_d(2)
-        make_cd(2)
-        make_d(3)
-        make_cd(3)
-        turn_ab(2)
-        turn_ab(3)
-        finish_difference(0)
-        make_d(4)
-        make_cd(4)
-        make_d(5)
-        make_cd(5)
-        finish_difference(1)
-        finish_difference(2)
-        make_d(6)
-        make_cd(6)
-        make_d(7)
-        make_cd(7)
-        finish_difference(3)
-        turn_ab(4)
-        finish_difference(4)
-        turn_ab(5)
-        turn_ab(6)
-        turn_ab(7)
-        finish_difference(5)
-        finish_difference(6)
-        finish_difference(7)
+        for n in range(PAIR):
+            turn_ab(n)
+        for n in range(PAIR):
+            make_d(n)
+        for n in range(PAIR):
+            begin_c(n)
+        finished = 0
+        for n in range(TILES):
+            if n >= PAIR:
+                make_d(n)
+            make_cd(n)
+            if n % PAIR == PAIR - 1 and n >= C_BUFFERS:
+                for early in range(len(held), BANKS // 2):
+                    turn_ab(early)
+                for done in range(finished, n - C_BUFFERS + 1):
+                    finish_difference(done)
+                finished = n - C_BUFFERS + 1
+        for n in range(finished, TILES):
+            finish_difference(n)
 
         for t in range(PACK):
             for lo, hi in LIST_HALVES if t in (0, PACK - 1) else ((0, S),):

@@ -152,7 +152,7 @@ def tile_list_complex_triple_messages_kernel(
                 nc.vector.tensor_copy(v_w[a][:, lo:hi], tab_w[a][:].bitcast(U32).indirect(listed(lo, hi)))
 
         def round_rows(copy, dst, src):
-            copy(dst.rearrange("p (c e) i -> p c i e", e=2), src.rearrange("p i (c e) -> p c i e", e=2))
+            copy(dst.rearrange("p (c e) i -> p c i e", e=4), src.rearrange("p i (c e) -> p c i e", e=4))
 
         def quantise(codes, scales, grouped):
             nc.vector.quantize_mx(codes.bitcast(FP8X4), scales, grouped.rearrange("p c i -> p (c i)"))
@@ -322,9 +322,9 @@ def tile_list_complex_triple_messages_kernel(
                 h_grouped[chunk] = vector_out([P, len(chunk) * P, PACK], BF16)
             lo = chunk.index(j) * P
             nc.vector.tensor_tensor(
-                h_grouped[chunk][:, lo : lo + P, :].rearrange("p (c e) t -> p c t e", e=2),
-                held[j][:].rearrange("p t (c e) -> p c t e", e=2),
-                picked[:, :, j * P : (j + 1) * P].rearrange("p t (c e) -> p c t e", e=2),
+                h_grouped[chunk][:, lo : lo + P, :].rearrange("p (c e) t -> p c t e", e=4),
+                held[j][:].rearrange("p t (c e) -> p c t e", e=4),
+                picked[:, :, j * P : (j + 1) * P].rearrange("p t (c e) -> p c t e", e=4),
                 MULT,
             )
 

from contextlib import ExitStack

import concourse.mybir as mybir
from concourse.masks import make_identity

K, H, N, T, S = 1024, 512, 256, 2048, 1024
FLOPS = 2 * (4 * K * H * S + H * N * S)

F32 = mybir.dt.float32
BF16 = mybir.dt.bfloat16
I32 = mybir.dt.int32
U32 = mybir.dt.uint32
U16 = mybir.dt.uint16
U8 = mybir.dt.uint8
FP8X4 = mybir.dt.float8_e4m3fn_x4
FP4X4 = mybir.dt.float4_e2m1fn_x4
MULT = mybir.AluOpType.mult
ADD = mybir.AluOpType.add
COPY = mybir.ActivationFunctionType.Copy
IDENTITY = mybir.ActivationFunctionType.Identity

P = 128
PACK = 4
K_PASS = P * PACK
PASSES = K // K_PASS
QUADRANT = 32
SCALE_ROWS = 4
TILES = S // P
PER_COLUMN = 16

PASS_SHIFT = QUADRANT // PASSES

TABLE_PIECES = (((0, P), (P, 4 * P), (4 * P, S)), ((0, 2 * P), (2 * P, 4 * P), (4 * P, S)))
LIST_HALVES = ((0, S // 2), (S // 2, S))
COLUMN_HALVES = (slice(0, H // 2), slice(H // 2, H))

BANKS = 8
WARM_UPS = 6
B_FROM_PASS_0 = 6
GPSIMD_FIRST = (0, 1)
VECTOR_AB = (2, 3, 4, 5, 6, 7)
A_ORDER = VECTOR_AB[:1] + GPSIMD_FIRST + VECTOR_AB[1:]
A_FROM_PASS_0 = BANKS - 1
ORDER = (2, 3, 4, 5, 0, 1, 6, 7)
PAIR = 2
C_BUFFERS = 3

CHUNKS = (ORDER[0:2], ORDER[2:4], ORDER[4:6], ORDER[6:7], ORDER[7:8])
WEIGHED_FIRST = 5

VECTOR_BUFFERS = 18
SCALAR_BUFFERS = 19


def tile_list_complex_triple_messages_kernel(
    tc, tab_words, tab_scales, offs, wa, wb_words, wb_scales, wc, wd_words, wd_scales, gT, w2, b2, out
):
    nc = tc.nc
    with ExitStack() as ctx:
        keep = ctx.enter_context(tc.tile_pool(name="keep", bufs=1))
        psum = ctx.enter_context(tc.psum_pool(name="psum", bufs=BANKS))

        offsets = keep.tile([P, S // PER_COLUMN], U16, name="offsets")
        tab_w = [keep.tile([P, T], I32, name=f"tab_w{a}", align_bytes=64) for a in range(PASSES)]
        tab_sc = keep.tile([P, T // 4], I32, name="tab_sc", align_bytes=64)
        fp4_sc = {w: keep.tile([P, PASSES, H // 4], I32, name=f"{w}_sc", align_bytes=64) for w in ("wb", "wd")}
        fp4_w = {w: keep.tile([P, PASSES, H // 2], I32, name=f"{w}_w", align_bytes=64) for w in ("wb", "wd")}
        rows = {(w, a): keep.tile([P, PACK, H], F32, name=f"{w}_rows{a}") for w in ("wa", "wc") for a in range(PASSES)}
        rows["w2", 0] = keep.tile([P, PACK, N], F32, name="w2_rows")
        bias = keep.tile([P, N // P], F32, name="bias")
        gates = [keep.tile([P, T], F32, name=f"gate{t}") for t in range(PACK)]
        v_w = [keep.tile([P, S], U32, name=f"v_w{a}", align_bytes=64) for a in range(PASSES)]
        v_sc = [keep.tile([P, S], U8, name=f"v_sc{a}", align_bytes=64) for a in range(PASSES)]
        picked = keep.tile([P, PACK, S], F32, name="picked", align_bytes=64)

        def vector_out(shape, dtype):
            return keep.tile(shape, dtype, name="vector_out", align_bytes=64, bufs=VECTOR_BUFFERS)

        def scalar_out(shape, dtype):
            return keep.tile(shape, dtype, name="scalar_out", align_bytes=64, bufs=SCALAR_BUFFERS)

        def listed(lo, hi):
            return offsets[:, lo // PER_COLUMN : hi // PER_COLUMN]

        def load_fp4_scales(name, src, which):
            by_row = src.rearrange("a (q s) c -> s q a c", s=SCALE_ROWS)
            for s in which:
                nc.sync.dma_start(fp4_sc[name][s:P:QUADRANT], by_row[s].bitcast(I32))

        def load_table_scales():
            by_row = tab_scales.rearrange("a (q s) c -> s q a c", s=SCALE_ROWS)
            for s in range(SCALE_ROWS):
                nc.sync.dma_start(tab_sc[s:P:PASS_SHIFT], by_row[s].bitcast(I32))

        def load_table_words(a):
            nc.sync.dma_start(tab_w[a][:], tab_words[a].rearrange("p t i -> p (t i)").bitcast(I32))

        def load_fp4_words(name, src):
            nc.sync.dma_start(fp4_w[name][:], src.rearrange("a p n -> p a n").bitcast(I32))

        def load_rows(name, src, a, which=slice(0, PACK)):
            by_partition = src[a * K_PASS : (a + 1) * K_PASS, :].rearrange("(p i) c -> p i c", i=PACK)
            nc.sync.dma_start(rows[name, a][:, which, :], by_partition[:, which, :])

        def load_gate(t):
            nc.sync.dma_start(gates[t][:], gT.rearrange("(p t) c -> t p c", t=PACK)[t])

        nc.vector.memset(tab_sc[:], 0)
        nc.sync.dma_start(offsets[:], offs)
        load_fp4_words("wb", wb_words)
        load_table_scales()
        load_table_words(0)
        zeros = keep.tile([P, K_PASS * PACK // 2], I32, name="zeros", align_bytes=64)
        zero_codes = keep.tile([P, H], U32, name="zero_codes", align_bytes=64)
        zero_scales = keep.tile([P, H], U8, name="zero_scales", align_bytes=64)
        nc.vector.memset(zeros[:], 0)
        nc.vector.quantize_mx(zero_codes[:].bitcast(FP8X4), zero_scales[:], zeros[:].bitcast(BF16))
        unread = psum.tile([P, H], F32, name="bank")
        for n in range(WARM_UPS):
            nc.tensor.matmul_mx(
                unread[:],
                lhsT=zero_codes[:, 0:P].bitcast(FP8X4),
                lhsT_scale=zero_scales[:, 0:P],
                rhs=zero_codes[:].bitcast(FP8X4),
                rhs_scale=zero_scales[:],
                start=(n == 0),
                stop=(n == WARM_UPS - 1),
            )

        nc.vector.tensor_copy(v_sc[0][:], tab_sc[:].bitcast(U8).indirect(listed(0, S)))
        ident = keep.tile([P, P], F32, name="tab_sc", align_bytes=64)
        make_identity(nc, ident[:])
        load_fp4_scales("wb", wb_scales, (0, 1, 2, 3))
        load_table_words(1)
        load_rows("wa", wa, 0, slice(0, 1))
        for s in range(SCALE_ROWS):
            nc.sync.dma_start(v_sc[1][s:P:QUADRANT].bitcast(I32), v_sc[0][PASS_SHIFT + s : P : QUADRANT].bitcast(I32))
        load_rows("wa", wa, 0, slice(1, PACK))
        load_rows("wa", wa, 1)
        load_rows("wc", wc, 0)
        load_rows("wc", wc, 1)
        load_fp4_words("wd", wd_words)
        load_fp4_scales("wd", wd_scales, (0, 1, 2, 3))
        for t in range(PACK):
            load_gate(t)
        load_rows("w2", w2, 0)
        with nc.allow_non_contiguous_dma(reason="one bias value for each partition and half of the outputs"):
            nc.sync.dma_start(bias[:], b2.rearrange("(n p) -> p n", p=P))

        for a in range(PASSES):
            for lo, hi in TABLE_PIECES[a]:
                nc.vector.tensor_copy(v_w[a][:, lo:hi], tab_w[a][:].bitcast(U32).indirect(listed(lo, hi)))

        def round_rows(copy, dst, src):
            copy(dst.rearrange("p (c e) i -> p c i e", e=4), src.rearrange("p i (c e) -> p c i e", e=4))

        def quantise(codes, scales, grouped):
            nc.vector.quantize_mx(codes.bitcast(FP8X4), scales, grouped.rearrange("p c i -> p (c i)"))

        quantised = {}

        def round_on_vector(name, a):
            halves = [vector_out([P, H // 2, PACK], BF16) for half in COLUMN_HALVES]
            for grouped, half in zip(halves, COLUMN_HALVES):
                round_rows(nc.vector.tensor_copy, grouped[:], rows[name, a][:, :, half])
            return [grouped[:] for grouped in halves]

        def quantise_pass(name, a, halves):
            codes = vector_out([P, H], U32)
            scales = keep.tile([P, H], U8, name=f"{name}_scales{a}", align_bytes=64)
            for grouped, half in zip(halves, COLUMN_HALVES):
                quantise(codes[:, half], scales[:, half], grouped)
            quantised[name, a] = (codes, scales)

        acc = {}

        def multiply(name, j, a):
            first = (name, j) not in acc
            if first:
                acc[name, j] = psum.tile([P, H], F32, name="bank")
            cols = slice(j * P, (j + 1) * P)
            if name in fp4_w:
                codes, scales = fp4_w[name][:, a, :].bitcast(FP4X4), fp4_sc[name][:, a, :].bitcast(U8)
            else:
                codes, scales = quantised[name, a][0][:].bitcast(FP8X4), quantised[name, a][1][:]
            nc.tensor.matmul_mx(
                acc[name, j][:],
                lhsT=v_w[a][:, cols].bitcast(FP8X4),
                lhsT_scale=v_sc[a][:, cols],
                rhs=codes,
                rhs_scale=scales,
                start=first,
                stop=not first,
            )

        def product(name, j, passes=(0, 1)):
            for a in passes:
                multiply(name, j, a)

        def by_channel(ap):
            return ap.rearrange("p (b m t) -> p b t m", m=4, t=PACK)

        def by_plane(ap):
            return ap.rearrange("p (t b m) -> p b t m", m=4, t=PACK)

        planes = {}

        def copy_out(name, j, dst=None):
            planes[name, j] = scalar_out([P, H], F32)[:] if dst is None else dst
            nc.scalar.activation(by_plane(planes[name, j]), by_channel(acc[name, j][:]), COPY, scale=(-1.0 if name == "wd" else 1.0))

        def ab_on_vector(j):
            planes["ab", j] = vector_out([P, H], F32)[:]
            nc.vector.tensor_tensor(by_plane(planes["ab", j]), by_channel(acc["wa", j][:]), by_plane(planes["wb", j]), MULT)

        held = {}

        def turn(name, j):
            first = j not in held
            if first:
                held[j] = psum.tile([P, PACK, P], F32, name="bank")
            for t in range(PACK):
                nc.tensor.matmul(
                    held[j][:, t, :],
                    planes[name, j][:, t * P : (t + 1) * P],
                    ident[:],
                    start=(first and t == 0),
                    stop=(not first and t == PACK - 1),
                    is_transpose=True,
                )

        for j in range(B_FROM_PASS_0):
            multiply("wb", j, 0)
        for j in range(TILES):
            product("wb", j, (1,) if j < B_FROM_PASS_0 else (1, 0))
            copy_out("wb", j)

        quantise_pass("wa", 0, round_on_vector("wa", 0))
        for j in A_ORDER[:A_FROM_PASS_0]:
            multiply("wa", j, 0)
        quantise_pass("wa", 1, round_on_vector("wa", 1))
        left, right = COLUMN_HALVES
        wc_left = scalar_out([P, H // 2, PACK], BF16)[:]
        round_rows(nc.scalar.copy, wc_left, rows["wc", 0][:, :, left])
        wc_right = vector_out([P, H // 2, PACK], BF16)[:]
        round_rows(nc.vector.tensor_copy, wc_right, rows["wc", 0][:, :, right])
        wc_first = [wc_left, wc_right]
        for n, j in enumerate(A_ORDER):
            product("wa", j, (1,) if n < A_FROM_PASS_0 else (1, 0))

        def as_planes(grouped):
            return grouped.rearrange("p c i -> p (c i)").bitcast(F32)

        def ab_on_gpsimd(j, dst):
            planes["ab", j] = dst
            nc.gpsimd.tensor_tensor(dst, planes["wa", j], planes["wb", j], MULT)

        for j in GPSIMD_FIRST:
            copy_out("wa", j)
        ab_on_vector(VECTOR_AB[0])
        quantise_pass("wc", 0, wc_first)
        for j, grouped in zip(GPSIMD_FIRST, reversed(wc_first)):
            ab_on_gpsimd(j, as_planes(grouped))
        for j in VECTOR_AB[1:]:
            ab_on_vector(j)
        wc_last = picked[:, 0, :].bitcast(BF16).rearrange("p (c i) -> p c i", i=PACK)
        for half in COLUMN_HALVES:
            round_rows(nc.scalar.copy, wc_last[:, half, :], rows["wc", 1][:, :, half])
        quantise_pass("wc", 1, [wc_last[:, half, :] for half in COLUMN_HALVES])

        def make_cd(n):
            j = ORDER[n]
            product("wc", j, (1,) if ("wc", j) in acc else (1, 0))
            copy_out("wc", j, keep.tile([P, H], F32, name="c_planes", align_bytes=64, bufs=C_BUFFERS)[:])
            planes["cd", j] = planes["wd", j]
            nc.gpsimd.tensor_tensor(planes["cd", j], planes["wc", j], planes["wd", j], MULT)

        def make_d(n):
            product("wd", ORDER[n])
            copy_out("wd", ORDER[n])

        def turn_ab(n):
            turn("ab", ORDER[n])

        def begin_c(n):
            multiply("wc", ORDER[n], 0)

        def finish_difference(n):
            if ORDER[n] not in held:
                turn("ab", ORDER[n])
            turn("cd", ORDER[n])

        for n in range(PAIR):
            turn_ab(n)
        for n in range(PAIR):
            make_d(n)
        for n in range(PAIR):
            begin_c(n)
        finished = 0
        for n in range(TILES):
            if n >= PAIR:
                make_d(n)
            make_cd(n)
            if n % PAIR == PAIR - 1 and n >= C_BUFFERS:
                for early in range(len(held), BANKS // 2):
                    turn_ab(early)
                for done in range(finished, n - C_BUFFERS + 1):
                    finish_difference(done)
                finished = n - C_BUFFERS + 1
        for n in range(finished, TILES):
            finish_difference(n)

        for t in range(PACK):
            for lo, hi in LIST_HALVES if t in (0, PACK - 1) else ((0, S),):
                nc.vector.tensor_copy(picked[:, t, lo:hi], gates[t][:].indirect(listed(lo, hi)))

        h_grouped = {}

        def weigh(j):
            chunk = [tiles for tiles in CHUNKS if j in tiles][0]
            if chunk not in h_grouped:
                h_grouped[chunk] = vector_out([P, len(chunk) * P, PACK], BF16)
            lo = chunk.index(j) * P
            nc.vector.tensor_tensor(
                h_grouped[chunk][:, lo : lo + P, :].rearrange("p (c e) t -> p c t e", e=4),
                held[j][:].rearrange("p t (c e) -> p c t e", e=4),
                picked[:, :, j * P : (j + 1) * P].rearrange("p t (c e) -> p c t e", e=4),
                MULT,
            )

        h_quantised = {}

        def quantise_chunk(chunk):
            width = len(chunk) * P
            codes = vector_out([P, width], U32)
            scales = keep.tile([P, width], U8, name="h_scales", align_bytes=64, bufs=len(CHUNKS))
            quantise(codes[:], scales[:], h_grouped[chunk][:])
            h_quantised[chunk] = (codes, scales)

        def finish(chunk):
            width = len(chunk) * P
            codes, scales = h_quantised[chunk]
            result = keep.tile([P, N // P, width], F32, name="result", bufs=len(CHUNKS))
            for n in range(N // P):
                cols = slice(n * P, (n + 1) * P)
                y = psum.tile([P, width], F32, name="bank")
                nc.tensor.matmul_mx(
                    y[:],
                    lhsT=w2_codes[:, cols].bitcast(FP8X4),
                    lhsT_scale=w2_scales[:, cols],
                    rhs=codes[:].bitcast(FP8X4),
                    rhs_scale=scales[:],
                    start=True,
                    stop=True,
                )
                if len(chunk) == 1 and n == 1:
                    nc.vector.tensor_scalar(result[:, n, :], y[:], bias[:, n : n + 1], None, op0=ADD)
                else:
                    nc.scalar.activation(result[:, n, :], y[:], IDENTITY, bias=bias[:, n : n + 1])
            first = chunk[0] * P
            nc.sync.dma_start(out[:, first : first + width].rearrange("(n p) j -> p n j", p=P), result[:])

        w2_grouped = keep.tile([P, N, PACK], BF16, name="c_planes", align_bytes=64, bufs=C_BUFFERS)
        round_rows(nc.scalar.copy, w2_grouped[:], rows["w2", 0][:])
        for j in ORDER[:WEIGHED_FIRST]:
            weigh(j)
        w2_codes = vector_out([P, N], U32)
        w2_scales = keep.tile([P, N], U8, name="w2_scales", align_bytes=64)
        quantise(w2_codes[:], w2_scales[:], w2_grouped[:])
        waiting = list(CHUNKS)
        for n in range(WEIGHED_FIRST, TILES + 1):
            for chunk in [tiles for tiles in waiting if set(tiles) <= set(ORDER[: n - 1])]:
                quantise_chunk(chunk)
                waiting.remove(chunk)
            if n < TILES:
                weigh(ORDER[n])
        quantise_chunk(CHUNKS[-1])
        for chunk in CHUNKS:
            finish(chunk)
